import numpy as np, ml_dtypes
CORES = [66,74,82,90,194,202,210,218]
N = 8
import mx_ref
BF = ml_dtypes.bfloat16
def gentries(a):
    return np.ascontiguousarray(a.reshape(8, 16, -1).transpose(0, 2, 1)).reshape(8, -1)
def gtable(e):
    e = np.asarray(e); return np.ascontiguousarray(e.reshape(8, -1, 16).transpose(0, 2, 1)).reshape(128, -1).astype(np.int32)
def gcols(t, e):
    v = np.concatenate([t.reshape(8, 16, -1, 4), np.zeros((8, 16, 1, 4), BF)], axis=2)
    return np.ascontiguousarray(np.stack([v[g][:, e[g]] for g in range(8)])).reshape(128, -1)
def tile(rs):
    return np.stack(rs, axis=2).reshape(128, -1).astype(BF)
def pick(q, e):
    c = np.concatenate([q[0].reshape(128, -1, 4), np.zeros((128, 1, 4), np.uint8)], axis=1); s = np.concatenate([q[1], np.ones((16, 1), np.uint8)], axis=1)
    return (np.ascontiguousarray(c[:, e].reshape(128, -1)), np.ascontiguousarray(s[:, e]))
def join(*qs):
    return (np.concatenate([q[0] for q in qs], axis=1), np.concatenate([q[1] for q in qs], axis=1))
def put(q, e, v):
    c, s = q[0].reshape(128, -1, 4).copy(), q[1].copy(); c[:, e] = v[0].reshape(128, -1, 4); s[:, e] = v[1]
    return (c.reshape(128, -1), s)
def pk(c, s):
    return (np.ascontiguousarray(c), mx_ref.live(s))
def emit(q):
    return q[0], q[1]
def packed(v, rng):
    q = [mx_ref.quantize(np.ascontiguousarray(v[r])) for r in range(N)]
    return np.stack([a for a, b in q]), np.stack([mx_ref.plane(b, rng) for a, b in q])
def values_of_codes():
    e, c = np.zeros((128, 128, 4), np.float32), np.zeros((128, 2, 4), np.uint8)
    e[np.arange(128), np.arange(128), 0] = 1
    c[:127, :, 0] = np.arange(256).reshape(2, 128).T[:127]
    return mx_ref.matmul(mx_ref.quantize(e.reshape(128, 512).astype(BF)), (c.reshape(128, 8), np.full((16, 2), 127, np.uint8))).T.reshape(-1).astype(np.float64)
CODE_VALUE, SCALE_VALUE = values_of_codes(), 2.0 ** (np.arange(256) - 127.0)
def decode(q):
    return (CODE_VALUE[q[0]].reshape(16, 8, -1, 4) * SCALE_VALUE[q[1]][:, None, :, None] + 0.0).reshape(128, -1).astype(np.float32)
def f(rng, *shape):
    return mx_ref.flush((rng.standard_normal(shape, dtype=np.float32) * np.exp2(rng.integers(-2, 3, shape[:-1] + (1,)))).astype(BF))
def wide(rng, *shape, cols=0):
    v = rng.standard_normal(shape, dtype=np.float32) * np.exp2(rng.integers(-12, 13, shape)).astype(np.float32)
    if cols: v *= np.repeat(np.exp2(rng.integers(-cols, cols + 1, shape[:-2] + (1, shape[-1] // 4))) * (rng.random(shape[:-2] + (1, shape[-1] // 4)) > 0.0625), 4, axis=-1).astype(np.float32)
    return mx_ref.flush(v.astype(BF))
C, R = 352, 3
STEP = [4, 2, 1]
def big(v):
    v = v.astype(np.float32)
    v[np.abs(v) < np.float32(2.0 ** -16)] = 0
    return v.astype(BF)
def numbers_of(rng):
    return {"x": big(f(rng, N, 128, 4 * C)), "u": np.array(f(rng, N, 128, 512)), "v": np.array(f(rng, N, 128, 512))}
def layers(rng):
    return big(f(rng, N, 128, 2048)).reshape(N, 8, 16, 4, 8, 16, 4)
def weights(rng, w):
    c, p = packed(np.ascontiguousarray(w).reshape(N, 128, 2048), rng)
    return {"wc": c, "ws": p}
def stored(e):
    return {"vg": np.stack([gtable(e[r]) for r in range(N)])}
def pointers(rng):
    return stored(rng.integers(0, 2 * C, (N, 8, C)))
def setup_inputs(rng):
    return {**numbers_of(rng), **weights(rng, layers(rng)), **pointers(rng)}
def setup_inputs_ties(rng):
    d = numbers_of(rng)
    e = rng.permutation(N)
    lo, hi = sorted((int(e[0]), int(e[0]) ^ STEP[0]))
    u = d["u"].reshape(N, 128, 128, 4)
    for r in range(N):
        k = np.zeros(8, int) if r in (lo, hi) else rng.permutation(8) % 3
        a = u[r][:, 1:4].copy()
        a[:, 2] = 0
        u[r][:, ::16] = a[:, k]
    d["x"][e[1]] = 0
    p = rng.integers(0, 2 * C, (N, 8, C))
    p[lo, 7] = np.arange(C)
    p[hi, 7] = rng.permutation(C)
    return {"x": d["x"], "u": u.reshape(N, 128, 512), "v": d["v"], **weights(rng, layers(rng)), **stored(p)}
def setup_inputs_near(rng):
    d = numbers_of(rng)
    x = d["x"].astype(np.float32).reshape(N, 8, 16, C, 4)
    s = rng.integers(0, 4, (2, N, 8, C))
    x[:, :, 0] = 0
    x[:, :, 0, :, 0] = 1
    x[:, :, 8:10] = 0
    for i, k in ((0, 2.0 ** -22), (1, 2.0 ** -29)):
        x[:, :, 8 + i, :, 0] = (s[i] & 1) * k
        x[:, :, 8 + i, :, 1] = (s[i] >> 1) * (2 * k)
    x[:, :, 10:] = rng.integers(4, 8, (N, 8, 6, C, 4)) * 2.0 ** -25
    n = rng.integers(0, 4, (N, 8, C))
    x[:, :, 10, :, 0] = (8 + 2 * n) * 2.0 ** -33
    x[:, :, 11, :, 0] = (14 - 2 * n) * 2.0 ** -33
    u = d["u"].reshape(N, 128, 128, 4)
    u[:, :, ::16] = 0
    o = rng.permutation(N) % 4
    for r in range(N):
        k = (1.0, -1.0, 2.0 ** -30, 2.0 ** -30)[o[r]]
        for h in range(0, 128, 16):
            if o[r] < 3:
                u[r, h, h, 0] = k
                u[r, h + 8, h, :2] = abs(k)
            else:
                u[r, h + 9, h, :2] = k
                u[r, h + 10, h, 0] = 9 * 2.0 ** -33
                u[r, h + 11, h, 0] = 8 * 2.0 ** -33
        if o[r] == 3:
            h = 16 * int(rng.integers(8))
            u[r, h, h, 0] = 1.0
    w = layers(rng)
    for i in (0, 8, 9, 10, 11, 12, 13, 14, 15):
        w[:, :, i] = 0
        w[:, :, :, :, :, i] = 0
    return {"x": x.reshape(N, 128, 4 * C).astype(BF), "u": u.reshape(N, 128, 512), "v": d["v"], **weights(rng, w), **pointers(rng)}
def setup_inputs_huge(rng):
    d = numbers_of(rng)
    x = -2.0 ** 30 * (0.55 + 0.2 * rng.random((N, 8, 1, C, 1)) + 0.05 * rng.random((N, 8, 16, C, 4)))
    u = d["u"].reshape(N, 128, 128, 4)
    o = rng.permutation(N) % 4
    s = np.stack([np.full(8, 1.0 - 2.0 * o[r]) if o[r] < 2 else rng.permutation(8) % 2 * 2.0 - 1.0 for r in range(N)])
    own = np.where(np.arange(128)[:, None] // 16 == np.arange(8), 1.0, 0.75)
    a = 2.0 ** 30 * (1 - 0.1 * rng.random((N, 128, 8, 4))) * own[None, :, :, None] * s[:, None, :, None]
    u[:, :, ::16] = a.astype(np.float32).astype(BF)
    w = np.zeros((N, 128, 4, 128, 4), np.float32)
    i = np.arange(128)
    for b in range(4): w[:, i, b, i, b] = -1
    return {"x": x.astype(np.float32).reshape(N, 128, 4 * C).astype(BF), "u": u.reshape(N, 128, 512), "v": d["v"], **weights(rng, w.astype(BF)), **pointers(rng)}
def setup_inputs_asks(rng):
    d = numbers_of(rng)
    e = np.zeros((N, 8, C), int)
    first = [r for r in range(N) if r < (r ^ STEP[0])]
    for i, r in enumerate(rng.permutation(first)):
        m, o = np.arange(2 * C), rng.permutation(2 * C)
        if i == 0:
            k = C + rng.permutation(C)
            m[:C] = k
            m[k] = np.arange(C)
        if i == 1:
            m[o[C // 2:C]] = o[0]
            k = np.sort(o[C:])
            m[k[:-1]] = k[1:]
        if i == 2: m[:] = o[0]
        e[r] = m[:C]
        e[r ^ STEP[0]] = m[C:]
    return {**d, **weights(rng, layers(rng)), **stored(e)}
def setup_inputs_spread(rng):
    d = setup_inputs(rng)
    d["x"] = big(wide(rng, N, 128, 4 * C, cols=6))
    return d
def check_inputs(d):
    b = []
    for k in ("x", "u", "v"):
        a = np.abs(d[k].astype(np.float32))
        if not (np.isfinite(a).all() and ((a == 0) | (a >= 2.0 ** -30) & (a <= 2.0 ** 30)).all()): b.append("a value of " + k)
    if ((d["wc"] & 0x7F) == 0x7F).any(): b.append("a code of wc that is no number")
    none, least, most = [emit(mx_ref.quantize(np.full((128, 16), k, np.float32).astype(BF)))[1][0, 0] for k in (0.0, 2.0 ** -30, 2.0 ** 30)]
    for r in range(N):
        s = mx_ref.live(d["ws"][r])
        if ((s != none) & ((s < least) | (s > most))).any(): b.append("a scale of ws")
    if ((d["vg"] < 0) | (d["vg"] >= 2 * C)).any(): b.append("a pointer of vg")
    return b
def swapped(p, s):
    n = np.arange(2 * C)
    o = np.argsort(-(s + np.float32(0.0)), axis=0, kind="stable")
    a = p[o[7], n]
    asks = a != n
    low = np.where(asks, n, 2 * C)
    np.minimum.at(low, a[asks], n[asks])
    c = n[asks & (low == n) & (low[a] == n)]
    k, new = a[c], p.copy()
    for m in range(4):
        g = o[m, c]
        new[g, c], new[g, k] = p[g, k], p[g, c]
    g = o[7, c]
    new[g, c], new[g, k] = p[g, k], c
    return new
def reference(x, u, v, wc, ws, vg):
    qu = [mx_ref.quantize(u[r]) for r in range(N)]
    lay = [pk(wc[r], ws[r]) for r in range(N)]
    now = [x[r] for r in range(N)]
    at = [gentries(vg[r]) for r in range(N)]
    for t in range(R):
        had = [decode(mx_ref.quantize(now[r])).astype(BF) for r in range(N)]
        score = []
        for r in range(N):
            one, two = min(r, r ^ STEP[t]), max(r, r ^ STEP[t])
            z = np.concatenate([had[one], had[two]], axis=1)
            p = np.concatenate([at[one], at[two]], axis=1)
            a, b = gcols(z, at[r]), gcols(z, np.take_along_axis(p, at[r], axis=1))
            q = mx_ref.quantize(((a.astype(np.float32) + b.astype(np.float32)) * np.float32(0.5)).astype(BF))
            score.append(mx_ref.matmul(qu[r], q)[::16])
            now[r] = tile([np.maximum(mx_ref.matmul(pick(lay[r], np.arange(128 * i, 128 * i + 128)), q), np.float32(0.0)) * np.float32(0.03125) + had[r][:, i::4].astype(np.float32) for i in range(4)])
        for r in range(N):
            e = r ^ STEP[t]
            if r < e:
                p = swapped(np.concatenate([at[r], at[e]], axis=1), np.concatenate([score[r], score[e]], axis=1))
                at[r], at[e] = p[:, :C], p[:, C:]
    y, ov = np.zeros((N, 128, C), np.float32), np.zeros((N, 8, C), np.float32)
    oc, osc = np.zeros((N, 128, 4 * C), np.uint8), np.zeros((N, 16, C), np.uint8)
    for r in range(N):
        q = mx_ref.quantize(now[r])
        y[r] = mx_ref.matmul(mx_ref.quantize(v[r]), q)
        ov[r] = at[r]
        oc[r], osc[r] = emit(q)
    return {"y": y, "ov": ov, "oc": oc, "osc": osc}

@@ -1,0 +1,525 @@
+from concourse.bass import DstId, RemoteDMATransfer
+from concourse.mybir import dt, AluOpType as O, ActivationFunctionType as AF
+
+C, J = 352, 704
+STEP = [4, 2, 1]
+F32, BF, I32, U16, MX, U8 = "float32", "bfloat16", "int32", "uint16", "float8_e4m3fn_x4", "uint8"
+
+
+def sb(n, t=F32):
+    return ("sbuf", [128, n], t)
+
+
+SCRATCH = {
+    "xt": sb(4 * C, BF), "xn": sb(4 * C, BF), "yt": sb(1536, BF), "fj": sb(4 * J, BF), "ab": sb(4 * C, BF), "rl": sb(4 * C),
+    "ut": sb(512, BF), "vt": sb(512, BF), "et": sb(2048, BF), "yo": sb(C),
+    "qy": sb(384, MX), "sy": sb(384, U8), "qu": sb(128, MX), "su": sb(128, U8), "qp": sb(128, MX), "sp": sb(128, U8),
+    "qv": sb(128, MX), "sv": sb(128, U8), "qw": sb(512, MX), "sw": sb(512, U8), "qe": sb(512, MX), "se": sb(512, U8),
+    "psa": ("psum", [128, 2048], F32), "psb": ("psum", [128, 2048], F32),
+    "pi": sb(16, I32), "cc": sb(48), "iof": sb(J), "zz": sb(192), "upk": sb(8, U16), "uw": sb(32), "cu": sb(128, U16), "c16": sb(48), "ctrl": sb(C),
+    "coef": sb(192), "c96": sb(96), "wt": sb(96), "rs": sb(192), "mk": sb(32), "on": sb(32), "zo": sb(4), "th": sb(36), "zc": sb(24),
+    "rc": sb(3 * 192), "cb": sb(32), "vgi": sb(22, I32), "vb": sb(J, I32), "dv": ("dram", [128, 22], I32),
+    "win0": sb(4 * J), "win1": sb(4 * J), "win2": sb(2 * J), "win3": sb(C),
+    "la": sb(66, U16), "lb": sb(66, U16), "ppf": sb(C), "sc": sb(C), "tt": sb(384), "pl": sb(112), "pw": sb(128),
+    "sr": sb(192), "fl": sb(192), "s1": sb(192), "f96": sb(96), "fw": sb(96), "so": sb(96), "r96": sb(96), "t96": sb(96),
+    "rm": sb(96), "eq": sb(96), "dup": sb(96), "m1": sb(8), "nu": sb(4), "lsc": sb(6, U16), "rb": sb(96), "tbv": sb(96),
+    "tb": sb(744), "tt7": sb(J), "ar": sb(56), "a1": sb(56), "mg": sb(48), "wout": sb(3 * 56), "wl": sb(7 * 24),
+    "vi": sb(24, I32), "ti": sb(J), "wv": sb(J), "oi": sb(32, I32), "lq": sb(22, U16), "gq": sb(C), "tg": sb(C),
+    "rw": sb(88, I32), "p7": sb(44 * 11, I32), "ix": sb(44, U16),
+    "dsrc0": ("dram", [128, 44], F32), "dsrc1": ("dram", [128, 44], F32), "dland0": ("dram", [128, 44], F32), "dland1": ("dram", [128, 44], F32),
+}
+for _t in range(4):
+    SCRATCH["qx%d" % _t] = sb(C, MX)
+    SCRATCH["sx%d" % _t] = sb(C, U8)
+for _t in range(3):
+    SCRATCH["lq%d" % _t] = sb(C, MX)
+    SCRATCH["ls%d" % _t] = sb(C, U8)
+SEMAPHORES = ["sv", "sa", "sp", "sg", "sent", "av", "ad0", "ad1", "ad2", "aw0", "aw1", "aw2", "af0", "af1"] + ["d%d" % _t for _t in range(24)]
+BIG = 2.0 ** 25
+
+
+def rank_program(g, core, T, topo):
+    rank = T.rank_of(core)
+    if rank is None:
+        return
+    eng = {"v": g.vector, "a": g.scalar, "p": g.tensor, "g": g, "s": g.sync}
+    qsem = {"v": "sv", "a": "sa", "p": "sp", "g": "sg"}
+    cnt = {}
+    know = {k: {} for k in eng}
+    log = {}
+    nd = [0]
+
+    def A(n, c0=None, c1=None, st=1, p0=0, p1=128, ps=1):
+        w = SCRATCH[n][1][1]
+        c0, c1 = (0, w) if c0 is None else (c0, c0 + 1 if c1 is None else c1)
+        ap = T[n][slice(p0, p1, ps) if ps > 1 else slice(p0, p1), slice(c0, c1, st) if st > 1 else slice(c0, c1)]
+        if SCRATCH[n][0] == "psum":
+            return {"ap": ap, "r": [(n, 0, 128, c0 // 512 * 512, c0 // 512 * 512 + 512, 1)], "x": True}
+        return {"ap": ap, "r": [(n, p0, p1, c0, c1, st)]}
+
+    def ind(w, o):
+        return {"ap": w["ap"].indirect(o["ap"]), "r": w["r"] + o["r"], "w": w["r"], "o": o["r"]}
+
+    def cast(a, d):
+        return {"ap": a["ap"].bitcast(d), "r": a["r"]}
+
+    def ext(ap):
+        return {"ap": ap, "r": []}
+
+    def meet(a, b):
+        if a[1] >= b[2] or b[1] >= a[2] or a[3] >= b[4] or b[3] >= a[4]:
+            return False
+        return not (a[5] == b[5] and a[5] > 1 and (a[3] - b[3]) % a[5])
+
+    def wait(q, ev):
+        if know[q].get(ev[0], 0) < ev[1]:
+            eng[q].wait_ge(T.sem[ev[0]], ev[1])
+            for k, v in list(ev[2].items()) + [(ev[0], ev[1])]:
+                know[q][k] = max(know[q].get(k, 0), v)
+
+    def deps(q, outs, ins):
+        rd, wr = [], []
+        for a in outs:
+            wr += a.get("w", a["r"])
+            rd += a.get("o", [])
+        for a in ins:
+            if isinstance(a, dict):
+                (wr if a.get("x") else rd).extend(a["r"])
+        need = {}
+        for regs, anyk in ((rd, False), (wr, True)):
+            for r in regs:
+                for (r2, isw, ev) in log.get(r[0], []):
+                    if (isw or anyk) and meet(r, r2) and need.get(ev[0], (0, 0))[1] < ev[1]:
+                        need[ev[0]] = ev
+        for ev in sorted(need.values(), key=lambda e: -len(e[2])):
+            wait(q, ev)
+        return rd, wr
+
+    def note(rd, wr, ev):
+        for r in rd:
+            log.setdefault(r[0], []).append((r, False, ev))
+        for r in wr:
+            log.setdefault(r[0], []).append((r, True, ev))
+
+    def ap(a):
+        return a["ap"] if isinstance(a, dict) else a
+
+    def op(q, outs, ins, f):
+        rd, wr = deps(q, outs, ins)
+        s = qsem[q]
+        if q == "g":
+            wait(q, (s, cnt.get(s, 0), {}))
+        cnt[s] = cnt.get(s, 0) + 1
+        f().then_inc(T.sem[s], 1)
+        note(rd, wr, (s, cnt[s], dict(know[q])))
+
+    def dma(q, pairs):
+        s = "d%d" % nd[0]
+        nd[0] += 1
+        rw = [deps(q, [o], [i]) for o, i in pairs]
+        for o, i in pairs:
+            eng[q].dma_start(ap(o), ap(i)).then_inc(T.sem[s], 16)
+        cnt[s] = 16 * len(pairs)
+        for rd, wr in rw:
+            note(rd, wr, (s, cnt[s], dict(know[q])))
+
+    def arrive(sem, n, lands):
+        cnt[sem] = n
+        note([], [r for a in lands for r in a["r"]], (sem, n, {}))
+
+    def peer(x):
+        return T.cores[rank ^ x]
+
+    def send(x, o, i, sem):
+        deps("g", [], [i])
+        m = topo.mask(core, peer(x))
+        rid, pid = topo.addr(peer(x), core)
+        g.remote_dma(ap(o), ap(i), T.sem[sem], T.sem["sent"], pid, rid, m)
+        cnt["sent"] = cnt.get("sent", 0) + bin(m).count("1")
+        return bin(m).count("1")
+
+    V = g.vector
+
+    def tc(o, i):
+        op("v", [o], [i], lambda: V.tensor_copy(ap(o), ap(i)))
+
+    def tt(o, a, b, f):
+        op("v", [o], [a, b], lambda: V.tensor_tensor(ap(o), ap(a), ap(b), f))
+
+    def ts(o, a, s1, f1, s2=None, f2=None):
+        if f2 is None:
+            op("v", [o], [a, s1], lambda: V.tensor_scalar(ap(o), ap(a), ap(s1), None, f1))
+        else:
+            op("v", [o], [a, s1, s2], lambda: V.tensor_scalar(ap(o), ap(a), ap(s1), ap(s2), f1, f2))
+
+    def ms(o, v):
+        op("v", [o], [], lambda: V.memset(ap(o), v))
+
+    def scan(o, a, b, f1, f2):
+        op("v", [o], [a, b], lambda: V.tensor_tensor_scan(ap(o), ap(a), ap(b), 0.0, f1, f2))
+
+    def tr(o, i):
+        op("v", [o], [i], lambda: V.transpose(ap(o), ap(i)))
+
+    def act(o, i, f=AF.Copy, scale=None, bias=None):
+        kw = {}
+        if scale is not None:
+            kw["scale"] = ap(scale)
+        if bias is not None:
+            kw["bias"] = ap(bias)
+        op("a", [o], [i, scale, bias], lambda: g.scalar.activation(ap(o), ap(i), f, **kw))
+
+    def aff(o, i, scale, bias):
+        act(o, i, AF.Identity, scale, bias)
+
+    def fill(n, c0, c1, st, v, p0=0, p1=128):
+        aff(A(n, c0, c1, st, p0, p1), A("zz", 0, len(range(c0, c1, st)), 1, p0, p1), 1.0, float(v))
+
+    def quant(q, s, i):
+        op("v", [q, s], [i], lambda: V.quantize_mx(ap(q), ap(s), ap(i)))
+
+    def mm(o, l, ls, r, rs):
+        op("p", [o], [l, ls, r, rs], lambda: g.tensor.matmul_mx(ap(o), ap(l), ap(ls), ap(r), ap(rs), True, True))
+
+    def iota(o, pat, base, cm, fl=True):
+        if fl:
+            op("g", [o], [], lambda: g.iota(ap(o), pat, base, cm, allow_small_or_imprecise_dtypes=True))
+        else:
+            op("g", [o], [], lambda: g.iota(ap(o), pat, base, cm))
+
+    hi = [1 if rank & s else 0 for s in STEP]
+    names = ["P", "q", "j32", "e", "g", "hb", "i8", "a", "qh", "b0", "b1", "b2", "b5", "b6", "g1", "q1", "corr", "D0", "D1", "S0", "S1", "pw", "c7", "c1", "fb",
+             "dd", "pq", "pe", "mb", "q22", "x0", "x1", "x2", "x3"]
+    col = {n: A("cc", k) for k, n in enumerate(names)}
+    cu = {"unb": A("cu", 44, 66), "F": A("cu", 66, 72), "rept": A("cu", 72, 78),
+          "kg": A("cu", 80, 82), "q0": A("cu", 82, 84), "q1": A("cu", 84, 86), "q2": A("cu", 86, 88), "m16": A("cu", 96, 118)}
+
+    def io(a, b, st=1):
+        return A("iof", a, b, st)
+
+    dma("a", [(A("vgi"), ext(T.vg[:]))])
+    dma("s", [(A("xt"), ext(T.x[:]))])
+    dma("s", [(A("vb", 0, C, p0=r, ps=16), ext(T.vg[:])) for r in range(16)])
+    dma("s", [(A("ut"), ext(T.u[:]))])
+    dma("s", [(cast(A("qw"), dt.uint8), ext(T.wc[:])), (A("sw"), ext(T.ws[:])), (A("vt"), ext(T.v[:]))])
+    iota(A("pi", 0), [[0, 1]], 0, 1, False)
+    iota(A("iof"), [[1, J]], 0, 0)
+    arrive("av", send(STEP[0], A("dv"), A("vgi"), "av"), [A("dv")])
+    dma("s", [(A("vb", C, J, p0=r, ps=16), A("dv")) for r in range(16)])
+
+    ms(A("zz"), 0.0)
+    ms(A("et"), 0.0)
+    sh, an = O.arith_shift_right, O.bitwise_and
+    for k, (s_, m_) in enumerate([(0, 15), (0, 31), (4, 1), (4, 7), (3, 1), (0, 7), (5, 3), (1, 7), (0, 1), (1, 1), (2, 1), (5, 1), (6, 1)]):
+        ts(A("pi", k + 1), A("pi", 0), s_, sh, m_, an)
+    tc(A("cc", 0, 14), A("pi", 0, 14))
+    for k in range(8):
+        fill("wt", k, 72, 24, 2 ** k)
+        fill("wt", 8 + k, 72, 24, -2 ** k)
+    fill("coef", 0, 192, 1, 1)
+    fill("rs", 0, 192, 1, 1)
+    fill("on", 0, 32, 1, 1)
+    fill("tt", C, 384, 1, -1)
+    fill("pl", 0, 112, 1, 0)
+    fill("ar", 0, 56, 1, BIG)
+    fill("tb", 0, 8, 1, 0)
+    fill("tb", 8 + J, 744, 1, 0)
+    fill("rs", 0, 72, 24, 0)
+    fill("rs", 72, 96, 8, 0)
+    fill("rs", 96, 192, 32, 0)
+    for a in range(4):
+        fill("cc", names.index("pq"), names.index("pq") + 1, 1, 2 ** (7 - 2 * a), 32 * a, 32 * a + 32)
+    for n_, i_, s_, b_ in (("q22", "q", 22, 0), ("q1", "q", 1, 1), ("c7", "i8", -1, 7), ("c1", "i8", 1, 1), ("fb", "i8", 8, 7), ("dd", "j32", 1, J),
+                           ("pe", "e", -0.5, 1), ("D0", "q", 1, 712), ("D1", "q", 1, 728), ("S0", "e", 2 ** 24 - 4096, 4096),
+                           ("S1", "e", 4096 - 2 ** 24, 2 ** 24), ("g1", "g", 1, 1), ("mb", "j32", -8, 8)):
+        aff(col[n_], col[i_], float(s_), float(b_))
+    for b in range(4):
+        ts(A("et", 512 * b + b, 512 * b + 512, 4), io(0, 128), col["P"], O.is_equal)
+
+    def send_x(t):
+        n = send(STEP[t], cast(A("lq%d" % t), dt.uint8), cast(A("qx%d" % t), dt.uint8), "ad%d" % t)
+        n += send(STEP[t], A("ls%d" % t), A("sx%d" % t), "ad%d" % t)
+        arrive("ad%d" % t, n, [A("lq%d" % t), A("ls%d" % t)])
+
+    def unpack(ps, q, s):
+        for b in range(4):
+            mm(A(ps, 512 * b, 512 * b + C), A("qe", 128 * b, 128 * b + 128), A("se", 128 * b, 128 * b + 128), A(q), A(s))
+
+    def halve(ps, at, b):
+        act(A("fj", J * b + at, J * b + at + C), A(ps, 512 * b, 512 * b + C), scale=0.5)
+
+    def first(t, b):
+        act(A("ab", C * b, C * b + C), ind(A("fj", J * b, J * b + J), A("la", 22 * t, 22 * t + 22)))
+
+    def listed(src, dst):
+        scan(A("sc"), A("ctrl"), src, O.add, O.max)
+        ts(dst, A("sc", 15, C, 16), col["corr"], O.subtract)
+
+    def share(t):
+        dma("s", [(A("dsrc%d" % t), A("win%d" % t, 0, J, ps=16))])
+        arrive("af%d" % t, send(STEP[t + 1], A("dland%d" % t), A("dsrc%d" % t), "af%d" % t), [A("dland%d" % t)])
+        dma("s", [(A("win%d" % t, 2 * J, 3 * J, p0=r, ps=16), A("dland%d" % t)) for r in range(16)])
+
+    def round_constants(t):
+        o = 192 * t
+        pr = 2.0 ** 22 * hi[t]
+        aff(A("rc", o + 32, o + 64), A("rc", 0, 32), 1.0, float(C * hi[t]))
+        fill("rc", o + 48, o + 56, 1, -1, 96, 128)
+        for at, k in ((104, 0), (126, 0), (148, 0), (170, 2 * J)):
+            aff(A("rc", o + at, o + at + 22), A("cb", 0, 22), 1.0, float(C * hi[t] + k))
+        aff(A("rc", o + 64, o + 96), A("rc", o + 32, o + 64), -1.0, col["dd"])
+        aff(A("rc", o + 96, o + 99), A("rc", o + 32, o + 56, 8), 4096.0, 255.0 + pr)
+        aff(A("rc", o + 100, o + 103), A("rc", o + 32, o + 56, 8), 4096.0, pr)
+        for k in range(3):
+            aff(A("th", 12 * t + 4 * k, 12 * t + 4 * k + 4), A("zo"), 1.0, A("rc", o + 100 + k))
+
+    def table():
+        aff(A("tb", 8, 8 + J), io(0, J), 4096.0, 2.0 ** 23)
+
+    def by_column_1(t):
+        tr(A("tt", 0, C), A("win%d" % t, C * hi[t], C * hi[t] + C))
+        for e in range(2):
+            tc(A("pl", 12 * e, 12 * e + 12), A("tt", 16 * e, 384, 32))
+
+    def by_column_2():
+        for a in range(4):
+            act(A("pl", 24, 48, p0=32 * a, p1=32 * a + 32), A("pl", 0, 24, p0=32 * (a ^ 1), p1=32 * (a ^ 1) + 32))
+        for h in range(2):
+            act(A("pl", 48, 96, p0=64 * h, p1=64 * h + 64), A("pl", 0, 48, p0=64 - 64 * h, p1=128 - 64 * h))
+
+    quant(A("qx0"), A("sx0"), A("xt"))
+    send_x(0)
+    quant(A("qe"), A("se"), A("et"))
+    op("g", [A("coef")], [A("coef")], lambda: g.affine_select(ap(A("coef")), ap(A("coef")), [[0, 3], [1, 8], [1, 8]], O.not_equal, -1.0, -7, 0))
+    iota(A("rc", 0, 32), [[128, 4], [0, 8]], 0, 1)
+    iota(A("c96"), [[0, 12], [1, 8]], 1, 0)
+    for k in range(3):
+        iota(A("c96", 24 * k + 8, 24 * k + 16), [[1, 8]], -2, 0)
+    for k in (1, 3):
+        iota(A("win0", J * k, J * k + J), [[1, J]], 0, 0)
+    unpack("psa", "qx0", "sx0")
+    for b in range(4):
+        halve("psa", C * hi[0], b)
+    tc(A("la", 0, 22), A("vgi"))
+    ts(cu["unb"], io(0, 22), col["q22"], O.add)
+    ts(col["corr"], col["q"], 15.0, O.is_lt, 4096.0, O.mult)
+    ts(A("c16", 0, 16), io(0, 16), col["q"], O.is_equal, -2.0 ** 20, O.mult)
+    ts(A("c16", 16, 32), io(0, 16), col["q1"], O.is_equal, 4096.0, O.mult)
+    ts(cu["m16"], A("zz", 0, 22), col["q"], O.add)
+    ts(A("zo"), io(0, 4), col["a"], O.not_equal, BIG, O.mult)
+    tt(A("c16", 32, 48), A("c16", 0, 16), A("c16", 16, 32), O.add)
+    tc(A("win0", C * hi[0], C * hi[0] + C), ind(A("vb", 0, C), cu["unb"]))
+    act(A("ctrl"), ind(A("c16", 32, 48), cu["m16"]))
+    by_column_1(0)
+    ts(A("uw", 0, 4), io(0, 8, 2), col["hb"], O.add)
+    ts(col["x0"], col["b1"], col["b5"], O.not_equal, 24.0, O.mult)
+    ts(A("uw", 4, 8), A("uw", 0, 4), col["i8"], O.add, -7.0, O.add)
+    ts(col["x1"], col["b2"], col["b6"], O.not_equal, 48.0, O.mult)
+    ts(A("uw", 8, 12), A("uw", 4, 8), 0.0, O.is_lt)
+    ts(col["x2"], col["b0"], 12.0, O.mult, col["a"], O.add)
+    ts(A("uw", 12, 16), A("uw", 8, 12), col["c7"], O.mult)
+    ts(A("uw", 16, 20), A("uw", 8, 12), col["c1"], O.mult)
+    ts(col["x3"], col["hb"], 4.0, O.mult, col["x0"], O.add)
+    ts(A("uw", 28), col["hb"], -128.0, O.mult, 128.0, O.add)
+    tt(A("uw", 20, 24), A("uw", 12, 16), A("uw", 4, 8), O.add)
+    tt(A("uw", 24, 28), A("uw", 16, 20), A("uw", 0, 4), O.add)
+    ts(A("cu", 80), col["x3"], col["x1"], O.add, col["x2"], O.add)
+    tc(A("cu", 66), col["fb"])
+    ts(A("cu", 67), col["hb"], 64.0, O.mult, col["fb"], O.add)
+    ts(A("cu", 68, 70), io(64, 192, 64), col["fb"], O.add)
+    ts(A("upk"), A("uw", 20, 28), 16.0, O.mult)
+    ts(A("cu", 70), A("uw", 28), col["fb"], O.add)
+    ts(A("cu", 71), A("cu", 67), 64.0, O.add)
+    ts(A("cu", 81), A("cu", 80), 8.0, O.add)
+    quant(A("qu"), A("su"), A("ut"))
+    for k in range(3):
+        ts(A("zc", 8 * k, 8 * k + 8), io(0, 8), 0.0625, O.mult)
+    op("v", [A("qp")], [A("qu"), A("upk")], lambda: V.tensor_copy(T.qp[:, 0:128].bitcast(dt.uint32), T.qu[:, 0:128].bitcast(dt.uint32).indirect(T.upk[:, 0:8])))
+    op("v", [A("sp")], [A("su"), A("upk")], lambda: V.tensor_copy(T.sp[:, 0:128], T.su[:, 0:128].indirect(T.upk[:, 0:8])))
+    ms(A("yt", 4 * C, 1536), 0.0)
+    for e in range(2):
+        ts(A("cu", 72 + e, 78, 2), io(0, 24, 8), 7.0, O.add)
+    ms(A("coef", 0, 192, 8), 0.0)
+    tt(col["pw"], col["pq"], col["pe"], O.mult)
+    ts(A("uw", 30, 32), io(0, 16, 8), col["qh"], O.add, 10.0, O.min)
+    for k in range(3):
+        ts(cu["q%d" % k], A("uw", 30, 32), 11.0 * hi[k], O.add)
+    aff(A("cb", 0, 22), io(0, C, 16), 1.0, col["q"])
+    round_constants(0)
+    by_column_2()
+    act(A("mk"), io(0, 32), AF.Relu, 8.0, col["mb"])
+    table()
+    tc(A("win0", C - C * hi[0], J - C * hi[0]), ind(A("vb", C, J), cu["unb"]))
+    tc(A("ppf"), ind(A("win0", 0, J), A("la", 0, 22)))
+    share(0)
+    listed(A("ppf"), A("lb", 0, 22))
+    unpack("psb", "lq0", "ls0")
+    for b in range(4):
+        halve("psb", C * (1 - hi[0]), b)
+        first(0, b)
+    iota(A("ti"), [[0, J]], 0, 0)
+    for a in range(4):
+        iota(A("ti", 8, J, 16, 32 * a, 32 * a + 32), [[32, 22], [0, 2]], 0, 1)
+    for k in (1, 3):
+        iota(A("win1", J * k, J * k + J), [[1, J]], 0, 0)
+
+    for t in range(3):
+        o = 192 * t
+        for b in range(4):
+            tt(A("yt", b, 4 * C, 4), ind(A("fj", J * b, J * b + J), A("lb", 22 * t, 22 * t + 22)), A("ab", C * b, C * b + C), O.add)
+        quant(A("qy"), A("sy"), A("yt"))
+        for k in range(3):
+            mm(A("psb", 512 * k, 512 * k + 128), A("qy", 128 * k, 128 * k + 128), A("sy", 128 * k, 128 * k + 128), A("qp"), A("sp"))
+        bank = [3, 0, 1, 2]
+
+        def layer(b):
+            mm(A("psb", 512 * bank[b], 512 * bank[b] + C), A("qw", 128 * b, 128 * b + 128), A("sw", 128 * b, 128 * b + 128), A("qy", 0, C), A("sy", 0, C))
+
+        def relu(b):
+            act(A("rl", C * b, C * b + C), A("psb", 512 * bank[b], 512 * bank[b] + C), AF.Relu, scale=0.03125)
+
+        layer(0)
+        pk = ind(A("pl"), cu["kg"])
+        tt(A("pw", 0, 32), pk, A("rc", o + 32, o + 64), O.is_equal)
+        tt(A("pw", 32, 64), A("pw", 0, 32), A("rc", o + 64, o + 96), O.mult)
+        tt(A("pw", 64, 96), pk, A("pw", 32, 64), O.add)
+        tt(A("pw", 96, 120), A("pw", 64, 88), A("zc"), O.add)
+        for k in range(3):
+            act(A("sr", 64 * k, 64 * k + 64), A("psb", 512 * k + 64, 512 * k + 128))
+            tt(A("fl", 64 * k, 64 * k + 64), A("psb", 512 * k, 512 * k + 64), A("sr", 64 * k, 64 * k + 64), O.is_ge)
+        for b in range(1, 4):
+            layer(b)
+        aff(A("wt", 72, 96), A("pw", 64, 88), 2.0 ** -12, 2.0 ** -9)
+        for k in range(3):
+            aff(A("wt", 24 * k + 16, 24 * k + 24), A("pw", 96 + 8 * k, 104 + 8 * k), 4096.0, 511.0 + 2.0 ** 22 * hi[t])
+        relu(0)
+        scan(A("s1"), A("coef"), A("fl"), O.mult, O.add)
+        tt(A("f96"), ind(A("s1"), cu["F"]), A("c96"), O.is_ge)
+        tt(A("fw"), A("f96"), A("wt"), O.mult)
+        scan(A("so"), A("rs", 0, 96), A("fw"), O.mult, O.add)
+        tsc = A("so", 79, 96, 8)
+        tc(A("r96"), ind(A("so", 72, 96), cu["rept"]))
+        for k in range(3):
+            aff(A("rm", 32 * k, 32 * k + 32), A("mk"), 1.0, A("so", 79 + 8 * k))
+        for k in range(3):
+            aff(A("rb", 32 * k, 32 * k + 32), A("on"), A("so", 15 + 24 * k), A("rc", o + 96 + k))
+        act(A("nu", 0, 3), tsc, AF.Relu, 2.0 ** 38, -711.5 * 2.0 ** 26)
+        for k in range(3):
+            aff(A("ar", 24 + 4 * k, 28 + 4 * k), A("zo"), 1.0, A("so", 23 + 24 * k))
+        for k in range(3):
+            aff(A("ar", 40 + 4 * k, 44 + 4 * k), A("th", 12 * t + 4 * k, 12 * t + 4 * k + 4), 1.0, A("nu", k))
+        for b in range(1, 4):
+            relu(b)
+        tr(A("t96"), A("r96"))
+        tt(A("eq"), A("t96"), A("rm"), O.is_equal)
+        scan(A("dup"), A("rs", 96, 192), A("eq"), O.mult, O.max)
+        tr(A("tbv"), A("rb"))
+        tt(A("m1", 0, 3), A("dup", 31, 96, 32), tsc, O.max)
+        for e in range(2):
+            ts(A("lsc", e, 6, 2), A("m1", 0, 3), col["S%d" % e], O.mult, col["D%d" % e], O.min)
+        for k in (2, 1, 0):
+            tc(ind(A("tb"), A("lsc", 2 * k, 2 * k + 2)), A("tbv", 32 * k, 32 * k + 32))
+        tr(A("tt7"), A("tb", 8, 8 + J))
+        tt(A("ar", 0, 22), A("tt7", 0, J, 32), A("tt7", 16, J, 32), O.min)
+        tt(A("a1", p1=64), A("ar", p1=64), A("ar", p0=64), O.min)
+        w = 56 * t
+        for a in range(2):
+            tt(A("wout", w, w + 56, p0=32 * a, p1=32 * a + 32), A("a1", p1=32), A("a1", p0=32, p1=64), O.min)
+        own = A("wout", w + 11 * hi[t], w + 11 * hi[t] + 11, p1=64)
+        tt(A("mg", 0, 11, p1=64), A("wout", w + 40, w + 51, p1=64), own, O.is_lt)
+        tt(A("mg", 16, 27, p1=64), A("wout", w + 24, w + 35, p1=64), own, O.subtract)
+        tt(A("mg", 32, 43, p1=64), A("mg", 0, 11, p1=64), A("mg", 16, 27, p1=64), O.mult)
+        tt(own, own, A("mg", 32, 43, p1=64), O.add)
+        tc(A("wout", w, w + 22, p0=64), A("wout", w, w + 22, p1=64))
+        W = A("wout", w, w + 22)
+        to = [STEP[t]] + ([STEP[t + 1], STEP[t] ^ STEP[t + 1]] if t < 2 else [])
+        lands = [A("wl", 24 * (3 * t + k), 24 * (3 * t + k) + 22) for k in range(len(to))]
+        deps("g", [], [W])
+        m = topo.mask(core, peer(to[0]))
+        for x in to:
+            m &= topo.mask(core, peer(x))
+        ids = [topo.addr(peer(x), core) for x in to]
+        g.remote_dma_fused([RemoteDMATransfer(dst_ids=[DstId(rid=r_, pnc=p_) for r_, p_ in ids], dma_engine_mask=m, remote_sem=T.sem["aw%d" % t],
+                                              srcs=[ap(W)], dsts=[ap(a) for a in lands])], local_sem=T.sem["sent"])
+        cnt["sent"] += bin(m).count("1")
+        arrive("aw%d" % t, bin(m).count("1") * len(to), lands)
+        for b in range(4):
+            tt(A("xn", b, 4 * C, 4), A("psa", 512 * b, 512 * b + C), A("rl", C * b, C * b + C), O.add)
+        qn, sn = "qx%d" % (t + 1), "sx%d" % (t + 1)
+        quant(A(qn), A(sn), A("xn"))
+        if t < 2:
+            send_x(t + 1)
+            unpack("psa", qn, sn)
+            for b in range(4):
+                halve("psa", C * hi[t + 1], b)
+            table()
+            round_constants(t + 1)
+            if t == 0:
+                iota(A("win2", J, 2 * J), [[1, J]], 0, 0)
+        else:
+            quant(A("qv"), A("sv"), A("vt"))
+            mm(A("psa", 0, C), A("qv"), A("sv"), A(qn), A(sn))
+            dma("s", [(ext(T.oc[:]), cast(A(qn), dt.uint8))] + [(ext(T.osc[4 * k:4 * k + 4, :]), A(sn, p0=32 * k, p1=32 * k + 4)) for k in range(4)])
+            act(A("yo"), A("psa", 0, C))
+            dma("a", [(ext(T.y[:]), A("yo"))])
+        if t < 2:
+            tt(A("ti", 0, J, 32, p1=64), A("wout", w, w + 22, p1=64), A("wl", 72 * t, 72 * t + 22, p1=64), O.min)
+            tt(A("ti", 0, J, 32, p0=64), A("wl", 72 * t + 24, 72 * t + 46, p0=64), A("wl", 72 * t + 48, 72 * t + 70, p0=64), O.min)
+        else:
+            tt(A("ti", 0, J, 32), W, lands[0], O.min)
+        tc(A("ti", 16, J, 32), A("ti", 0, J, 32))
+        tc(A("vi", 0, 22), A("ti", 0, J, 32))
+        tr(A("wv"), A("ti"))
+        ts(A("oi"), ind(A("vi", 0, 22), cu["q%d" % t]), 12, sh, 1023, an)
+        tc(A("lq"), A("oi", 0, 22))
+        act(A("gq", 192, C), ind(A("wv"), A("lq", 12, 22)))
+        tc(A("gq", 0, 192), ind(A("wv"), A("lq", 0, 12)))
+        tr(A("tg"), A("gq"))
+        if t < 2:
+            n = 44
+            for s in range(2):
+                for d in range(2):
+                    tc(A("rw", 44 * s, 44 * s + 44, p0=64 * d, p1=64 * d + 64), A("tg", 0, C, 8, p0=64 * s, p1=64 * s + 64))
+        else:
+            n = 22
+            tc(A("rw", 0, 44), A("tg", 0, C, 8))
+        Vw, Mw = A("rw", 0, 2 * n, 2), A("rw", 1, 2 * n, 2)
+        p = [A("p7", 44 * k, 44 * k + n) for k in range(11)]
+        nj, nb = A("rc", o + 104, o + 104 + n), A("rc", o + 148, o + 148 + n)
+        ts(p[0], Vw, col["pw"], O.mult)
+        ts(p[1], Vw, 12, sh, 1023, an)
+        ts(p[2], Vw, 8, sh, 15, an)
+        ts(p[3], p[0], 7, sh, 1, an)
+        tt(p[4], p[1], nj, O.is_equal)
+        ts(p[5], p[2], col["g1"], O.is_equal, float(J), O.mult)
+        tt(p[6], Mw, nj, O.subtract)
+        tt(p[7], p[3], p[4], O.mult)
+        tt(p[8], p[6], p[5], O.add)
+        tt(p[9], p[8], p[7], O.mult)
+        tt(p[10], p[9], nb, O.add)
+        tc(A("ix", 0, n), p[10])
+        w0, w1 = A("win%d" % t), "win%d" % (t + 1)
+        at = C * hi[t + 1] if t < 2 else 0
+        if t < 2:
+            act(A(w1, C - at, J - at), ind(w0, A("ix", 22, 44)))
+            tc(A(w1, at, at + C), ind(w0, A("ix", 0, 22)))
+            listed(A(w1, at, at + C), A("la", 22 * t + 22, 22 * t + 44))
+            unpack("psb", "lq%d" % (t + 1), "ls%d" % (t + 1))
+            for b in range(2):
+                halve("psb", C - at, b)
+            act(A("ppf"), ind(A(w1, 0, J), A("la", 22 * t + 22, 22 * t + 44)))
+            by_column_1(t + 1)
+            listed(A("ppf"), A("lb", 22 * t + 22, 22 * t + 44))
+            for b in range(4):
+                if b >= 2:
+                    halve("psb", C - at, b)
+                first(t + 1, b)
+            by_column_2()
+            if t == 0:
+                share(1)
+        else:
+            act(A(w1, 192, C), ind(w0, A("ix", 12, 22)))
+            tc(A(w1, 0, 192), ind(w0, A("ix", 0, 12)))
+            dma("s", [(ext(T.ov[:]), A(w1, ps=16))])
+    for s, n in cnt.items():
+        g.wait_ge(T.sem[s], n)

@@ -1,5 +1,5 @@
 from concourse.bass import DstId, RemoteDMATransfer
-from concourse.mybir import dt, AluOpType as O, ActivationFunctionType as AF
+from concourse.mybir import dt, AluOpType as O, ActivationFunctionType as AF, AxisListType as AX
 
 C, J = 352, 704
 STEP = [4, 2, 1]
@@ -13,19 +13,19 @@ def sb(n, t=F32):
 SCRATCH = {
     "xt": sb(4 * C, BF), "xn": sb(4 * C, BF), "yt": sb(1536, BF), "fj": sb(4 * J, BF), "ab": sb(4 * C, BF), "rl": sb(4 * C),
     "ut": sb(512, BF), "vt": sb(512, BF), "et": sb(2048, BF), "yo": sb(C),
-    "qy": sb(384, MX), "sy": sb(384, U8), "qu": sb(128, MX), "su": sb(128, U8), "qp": sb(128, MX), "sp": sb(128, U8),
+    "qy": sb(384, MX), "sy": sb(384, U8), "qu": sb(128, MX), "su": sb(128, U8), "qp": sb(144, MX), "sp": sb(144, U8),
     "qv": sb(128, MX), "sv": sb(128, U8), "qw": sb(512, MX), "sw": sb(512, U8), "qe": sb(512, MX), "se": sb(512, U8),
     "psa": ("psum", [128, 2048], F32), "psb": ("psum", [128, 2048], F32),
-    "pi": sb(16, I32), "cc": sb(48), "iof": sb(J), "zz": sb(192), "upk": sb(8, U16), "uw": sb(32), "cu": sb(128, U16), "c16": sb(48), "ctrl": sb(C),
-    "coef": sb(192), "c96": sb(96), "wt": sb(96), "rs": sb(192), "mk": sb(32), "on": sb(32), "zo": sb(4), "th": sb(36), "zc": sb(24),
-    "rc": sb(3 * 192), "cb": sb(32), "vgi": sb(22, I32), "vb": sb(J, I32), "dv": ("dram", [128, 22], I32),
-    "win0": sb(4 * J), "win1": sb(4 * J), "win2": sb(2 * J), "win3": sb(C),
-    "la": sb(66, U16), "lb": sb(66, U16), "ppf": sb(C), "sc": sb(C), "tt": sb(384), "pl": sb(112), "pw": sb(128),
-    "sr": sb(192), "fl": sb(192), "s1": sb(192), "f96": sb(96), "fw": sb(96), "so": sb(96), "r96": sb(96), "t96": sb(96),
-    "rm": sb(96), "eq": sb(96), "dup": sb(96), "m1": sb(8), "nu": sb(4), "lsc": sb(6, U16), "rb": sb(96), "tbv": sb(96),
-    "tb": sb(744), "tt7": sb(J), "ar": sb(56), "a1": sb(56), "mg": sb(48), "wout": sb(3 * 56), "wl": sb(7 * 24),
-    "vi": sb(24, I32), "ti": sb(J), "wv": sb(J), "oi": sb(32, I32), "lq": sb(22, U16), "gq": sb(C), "tg": sb(C),
-    "rw": sb(88, I32), "p7": sb(44 * 11, I32), "ix": sb(44, U16),
+    "pi": sb(16, I32), "cc": sb(48), "zz": sb(192), "upk": sb(10, U16), "uw": sb(432), "cu": sb(64, U16), "c16": sb(48), "ctrl": sb(C),
+    "coef": sb(72), "c96": sb(96), "wt": sb(96), "rs": sb(96), "on": sb(32), "zo": sb(4), "me": sb(2), "zc": sb(48), "w8": sb(16),
+    "rc": sb(3 * 152), "cb": sb(72), "vgi": sb(22, I32), "vb": sb(J, I32), "dv0": ("dram", [128, 22], I32), "dv": ("dram", [128, 22], I32),
+    "win": sb(6 * J), "wov": sb(C),
+    "la": sb(66, U16), "lb": sb(66, U16), "ppf": sb(C), "sc": sb(C), "tt": sb(384), "pl": sb(104), "pw": sb(4 * 48),
+    "sr": sb(216), "fl": sb(216), "s1": sb(1134), "dz": sb(126), "z": sb(126), "f96": sb(96), "fw": sb(96), "so": sb(96), "t96": sb(96),
+    "m3": sb(4), "lsc": sb(6, U16), "rb": sb(96), "tbv": sb(96),
+    "tb": sb(32 + J), "tt7": sb(J), "ar": sb(24), "a1": sb(24), "ar2": sb(24), "b1": sb(24), "b2": sb(24), "mg": sb(48), "wout": sb(3 * 24), "wl": sb(7 * 24),
+    "vi": sb(16, I32), "ti": sb(J), "wv": sb(J), "oi": sb(32, I32), "lq": sb(22, U16), "gq": sb(C), "tg": sb(C),
+    "dd": sb(3 * 176), "e0": sb(3 * 176), "so2": sb(176), "p7": sb(44 * 5, I32), "ix": sb(44, U16),
     "dsrc0": ("dram", [128, 44], F32), "dsrc1": ("dram", [128, 44], F32), "dland0": ("dram", [128, 44], F32), "dland1": ("dram", [128, 44], F32),
 }
 for _t in range(4):
@@ -36,6 +36,10 @@ for _t in range(3):
     SCRATCH["ls%d" % _t] = sb(C, U8)
 SEMAPHORES = ["sv", "sa", "sp", "sg", "sent", "av", "ad0", "ad1", "ad2", "aw0", "aw1", "aw2", "af0", "af1"] + ["d%d" % _t for _t in range(24)]
 BIG = 2.0 ** 25
+K = 2048.0
+TOP = 7 * 4096 + 1.0
+OWN, NEXT, NUM = [J, 3 * J, 5 * J], [0, 4 * J], 2 * J
+WINDOW = [(0, 3 * J), (2 * J, 5 * J), (2 * J, 6 * J)]
 
 
 def rank_program(g, core, T, topo):
@@ -78,54 +82,51 @@ def rank_program(g, core, T, topo):
                 know[q][k] = max(know[q].get(k, 0), v)
 
     def deps(q, outs, ins):
-        rd, wr = [], []
+        touch = []
         for a in outs:
-            wr += a.get("w", a["r"])
-            rd += a.get("o", [])
+            touch += [(r, "w") for r in a.get("w", a["r"])] + [(r, "r") for r in a.get("o", [])]
         for a in ins:
             if isinstance(a, dict):
-                (wr if a.get("x") else rd).extend(a["r"])
+                touch += [(r, "x" if a.get("x") else "r") for r in a["r"]]
         need = {}
-        for regs, anyk in ((rd, False), (wr, True)):
-            for r in regs:
-                for (r2, isw, ev) in log.get(r[0], []):
-                    if (isw or anyk) and meet(r, r2) and need.get(ev[0], (0, 0))[1] < ev[1]:
-                        need[ev[0]] = ev
+        for r, k in touch:
+            for (r2, k2, ev) in log.get(r[0], []):
+                clash = k == "w" or k2 == "w" or (k == "x" and ev[0] != qsem.get(q))
+                if clash and meet(r, r2) and need.get(ev[0], (0, 0))[1] < ev[1]:
+                    need[ev[0]] = ev
         for ev in sorted(need.values(), key=lambda e: -len(e[2])):
             wait(q, ev)
-        return rd, wr
+        return touch
 
-    def note(rd, wr, ev):
-        for r in rd:
-            log.setdefault(r[0], []).append((r, False, ev))
-        for r in wr:
-            log.setdefault(r[0], []).append((r, True, ev))
+    def note(touch, ev):
+        for r, k in touch:
+            log.setdefault(r[0], []).append((r, k, ev))
 
     def ap(a):
         return a["ap"] if isinstance(a, dict) else a
 
     def op(q, outs, ins, f):
-        rd, wr = deps(q, outs, ins)
+        touch = deps(q, outs, ins)
         s = qsem[q]
         if q == "g":
             wait(q, (s, cnt.get(s, 0), {}))
         cnt[s] = cnt.get(s, 0) + 1
         f().then_inc(T.sem[s], 1)
-        note(rd, wr, (s, cnt[s], dict(know[q])))
+        note(touch, (s, cnt[s], dict(know[q])))
 
     def dma(q, pairs):
         s = "d%d" % nd[0]
         nd[0] += 1
-        rw = [deps(q, [o], [i]) for o, i in pairs]
+        touch = [deps(q, [o], [i]) for o, i in pairs]
         for o, i in pairs:
             eng[q].dma_start(ap(o), ap(i)).then_inc(T.sem[s], 16)
         cnt[s] = 16 * len(pairs)
-        for rd, wr in rw:
-            note(rd, wr, (s, cnt[s], dict(know[q])))
+        for x in touch:
+            note(x, (s, cnt[s], dict(know[q])))
 
     def arrive(sem, n, lands):
         cnt[sem] = n
-        note([], [r for a in lands for r in a["r"]], (sem, n, {}))
+        note([(r, "w") for a in lands for r in a["r"]], (sem, n, {}))
 
     def peer(x):
         return T.cores[rank ^ x]
@@ -155,8 +156,11 @@ def rank_program(g, core, T, topo):
     def ms(o, v):
         op("v", [o], [], lambda: V.memset(ap(o), v))
 
-    def scan(o, a, b, f1, f2):
-        op("v", [o], [a, b], lambda: V.tensor_tensor_scan(ap(o), ap(a), ap(b), 0.0, f1, f2))
+    def scan(o, a, b, f1, f2, init=0.0):
+        op("v", [o], [a, b], lambda: V.tensor_tensor_scan(ap(o), ap(a), ap(b), init, f1, f2))
+
+    def least(o, i):
+        op("v", [o], [i], lambda: V.tensor_reduce(ap(o), ap(i), AX.X, O.min))
 
     def tr(o, i):
         op("v", [o], [i], lambda: V.transpose(ap(o), ap(i)))
@@ -188,23 +192,28 @@ def rank_program(g, core, T, topo):
             op("g", [o], [], lambda: g.iota(ap(o), pat, base, cm))
 
     hi = [1 if rank & s else 0 for s in STEP]
-    names = ["P", "q", "j32", "e", "g", "hb", "i8", "a", "qh", "b0", "b1", "b2", "b5", "b6", "g1", "q1", "corr", "D0", "D1", "S0", "S1", "pw", "c7", "c1", "fb",
-             "dd", "pq", "pe", "mb", "q22", "x0", "x1", "x2", "x3"]
+    names = ["P", "q", "j32", "e", "g", "hb", "i8", "a", "qh", "b0", "b1", "b2", "b5", "b6", "g1", "q1", "corr", "pw", "fb", "pq", "pe", "q22",
+             "r16", "self", "last", "hb96", "x0", "x1", "x2", "x3"]
     col = {n: A("cc", k) for k, n in enumerate(names)}
-    cu = {"unb": A("cu", 44, 66), "F": A("cu", 66, 72), "rept": A("cu", 72, 78),
-          "kg": A("cu", 80, 82), "q0": A("cu", 82, 84), "q1": A("cu", 84, 86), "q2": A("cu", 86, 88), "m16": A("cu", 96, 118)}
+    cu = {"unb": A("cu", 0, 22), "m16": A("cu", 22, 44), "F": A("cu", 44, 50), "kg": A("cu", 50, 53), "q": A("cu", 54, 56)}
 
     def io(a, b, st=1):
-        return A("iof", a, b, st)
+        return A("win", NUM + a, NUM + b, st)
 
-    dma("a", [(A("vgi"), ext(T.vg[:]))])
+    def own_win(t, c0=0, c1=J, **k):
+        return A("win", OWN[t] + c0, OWN[t] + c1, **k)
+
+    dma("a", [(A("dv0"), ext(T.vg[:]))])
     dma("s", [(A("xt"), ext(T.x[:]))])
+    dma("a", [(A("vgi"), ext(T.vg[:]))])
     dma("s", [(A("vb", 0, C, p0=r, ps=16), ext(T.vg[:])) for r in range(16)])
     dma("s", [(A("ut"), ext(T.u[:]))])
     dma("s", [(cast(A("qw"), dt.uint8), ext(T.wc[:])), (A("sw"), ext(T.ws[:])), (A("vt"), ext(T.v[:]))])
     iota(A("pi", 0), [[0, 1]], 0, 1, False)
-    iota(A("iof"), [[1, J]], 0, 0)
-    arrive("av", send(STEP[0], A("dv"), A("vgi"), "av"), [A("dv")])
+    iota(io(0, J), [[1, J]], 0, 0)
+    iota(A("uw", 144, 216), [[16, 8], [0, 9]], 0, 0)
+    iota(A("uw", 216, 288), [[16, 8], [16, 9]], 0, 0)
+    arrive("av", send(STEP[0], A("dv"), A("dv0"), "av"), [A("dv")])
     dma("s", [(A("vb", C, J, p0=r, ps=16), A("dv")) for r in range(16)])
 
     ms(A("zz"), 0.0)
@@ -213,26 +222,30 @@ def rank_program(g, core, T, topo):
     for k, (s_, m_) in enumerate([(0, 15), (0, 31), (4, 1), (4, 7), (3, 1), (0, 7), (5, 3), (1, 7), (0, 1), (1, 1), (2, 1), (5, 1), (6, 1)]):
         ts(A("pi", k + 1), A("pi", 0), s_, sh, m_, an)
     tc(A("cc", 0, 14), A("pi", 0, 14))
-    for k in range(8):
-        fill("wt", k, 72, 24, 2 ** k)
-        fill("wt", 8 + k, 72, 24, -2 ** k)
-    fill("coef", 0, 192, 1, 1)
-    fill("rs", 0, 192, 1, 1)
+    fill("coef", 0, 72, 1, 1)
+    fill("rs", 0, 96, 1, 1)
     fill("on", 0, 32, 1, 1)
+    fill("w8", 8, 16, 1, 2)
+    fill("c96", 0, 96, 1, 7 * 4096)
     fill("tt", C, 384, 1, -1)
-    fill("pl", 0, 112, 1, 0)
-    fill("ar", 0, 56, 1, BIG)
-    fill("tb", 0, 8, 1, 0)
-    fill("tb", 8 + J, 744, 1, 0)
-    fill("rs", 0, 72, 24, 0)
-    fill("rs", 72, 96, 8, 0)
-    fill("rs", 96, 192, 32, 0)
+    fill("pl", 96, 104, 1, -K)
+    fill("tb", 0, 32, 1, 0)
+    fill("dz", 0, 126, 1, 0)
+    fill("wout", 0, 72, 1, 0)
+    for c0, c1, st, v in ((0, 72, 9, 0), (8, 72, 9, 4096), (16, 57, 8, -1)):
+        fill("coef", c0, c1, st, v)
+    fill("rs", 0, 96, 32, 0)
+    fill("rs", 24, 96, 32, 0)
+    for k in range(3):
+        fill("c96", 32 * k, 32 * k + 8, 1, 4 * 4096)
+    fill("dz", 0, 126, 42, -BIG)
+    fill("coef", 8, 9, 1, -4096)
     for a in range(4):
         fill("cc", names.index("pq"), names.index("pq") + 1, 1, 2 ** (7 - 2 * a), 32 * a, 32 * a + 32)
-    for n_, i_, s_, b_ in (("q22", "q", 22, 0), ("q1", "q", 1, 1), ("c7", "i8", -1, 7), ("c1", "i8", 1, 1), ("fb", "i8", 8, 7), ("dd", "j32", 1, J),
-                           ("pe", "e", -0.5, 1), ("D0", "q", 1, 712), ("D1", "q", 1, 728), ("S0", "e", 2 ** 24 - 4096, 4096),
-                           ("S1", "e", 4096 - 2 ** 24, 2 ** 24), ("g1", "g", 1, 1), ("mb", "j32", -8, 8)):
+    for n_, i_, s_, b_ in (("q22", "q", 22, 0), ("q1", "q", 1, 1), ("fb", "i8", 9, 8), ("pe", "e", -0.5, 1), ("g1", "g", 1, 1), ("r16", "q", 1, 16),
+                           ("self", "q", 1, -16), ("last", "q", -1, 16 - TOP), ("hb96", "hb", 96, 0)):
         aff(col[n_], col[i_], float(s_), float(b_))
+    aff(A("coef", 1, 72, 9), io(0, 8), 1.0, -7.0)
     for b in range(4):
         ts(A("et", 512 * b + b, 512 * b + 512, 4), io(0, 128), col["P"], O.is_equal)
 
@@ -245,41 +258,50 @@ def rank_program(g, core, T, topo):
         for b in range(4):
             mm(A(ps, 512 * b, 512 * b + C), A("qe", 128 * b, 128 * b + 128), A("se", 128 * b, 128 * b + 128), A(q), A(s))
 
-    def halve(ps, at, b):
-        act(A("fj", J * b + at, J * b + at + C), A(ps, 512 * b, 512 * b + C), scale=0.5)
+    def halve(ps, at, b, on="a"):
+        o, i = A("fj", J * b + at, J * b + at + C), A(ps, 512 * b, 512 * b + C)
+        if on == "a":
+            act(o, i, scale=0.5)
+        else:
+            ts(o, i, 0.5, O.mult)
 
     def first(t, b):
         act(A("ab", C * b, C * b + C), ind(A("fj", J * b, J * b + J), A("la", 22 * t, 22 * t + 22)))
 
-    def listed(src, dst):
-        scan(A("sc"), A("ctrl"), src, O.add, O.max)
-        ts(dst, A("sc", 15, C, 16), col["corr"], O.subtract)
+    def listed(src, dst, n=C):
+        scan(A("sc", 0, n), A("ctrl", 0, n), src, O.add, O.max)
+        ts(dst, A("sc", 15, n, 16), col["corr"], O.subtract)
+
+    def split(n, at, w, l, l0):
+        act(A(n, at + 192, at + C), ind(w, A(l, l0 + 12, l0 + 22)))
+        tc(A(n, at, at + 192), ind(w, A(l, l0, l0 + 12)))
 
     def share(t):
-        dma("s", [(A("dsrc%d" % t), A("win%d" % t, 0, J, ps=16))])
+        dma("s", [(A("dsrc%d" % t), own_win(t, ps=16))])
         arrive("af%d" % t, send(STEP[t + 1], A("dland%d" % t), A("dsrc%d" % t), "af%d" % t), [A("dland%d" % t)])
-        dma("s", [(A("win%d" % t, 2 * J, 3 * J, p0=r, ps=16), A("dland%d" % t)) for r in range(16)])
+        dma("s", [(A("win", NEXT[t], NEXT[t] + J, p0=r, ps=16), A("dland%d" % t)) for r in range(16)])
 
     def round_constants(t):
-        o = 192 * t
-        pr = 2.0 ** 22 * hi[t]
-        aff(A("rc", o + 32, o + 64), A("rc", 0, 32), 1.0, float(C * hi[t]))
-        fill("rc", o + 48, o + 56, 1, -1, 96, 128)
-        for at, k in ((104, 0), (126, 0), (148, 0), (170, 2 * J)):
-            aff(A("rc", o + at, o + at + 22), A("cb", 0, 22), 1.0, float(C * hi[t] + k))
-        aff(A("rc", o + 64, o + 96), A("rc", o + 32, o + 64), -1.0, col["dd"])
-        aff(A("rc", o + 96, o + 99), A("rc", o + 32, o + 56, 8), 4096.0, 255.0 + pr)
-        aff(A("rc", o + 100, o + 103), A("rc", o + 32, o + 56, 8), 4096.0, pr)
-        for k in range(3):
-            aff(A("th", 12 * t + 4 * k, 12 * t + 4 * k + 4), A("zo"), 1.0, A("rc", o + 100 + k))
+        o, pr, j0 = 152 * t, 2.0 ** 22 * hi[t], float(C * hi[t])
+        aff(A("rc", o, o + 48), A("cb", 24, 72), 1.0, j0)
+        fill("e0", 176 * t, 176 * t + 176, 1, 0)
+        fill("rc", o + 32, o + 48, 1, -1, 96, 128)
+        aff(A("rc", o + 104, o + 148, 2), A("cb", 0, 22), 4096.0, 4096 * j0)
+        aff(A("rc", o + 105, o + 148, 2), A("cb", 0, 22), 1.0, j0)
+        for s, base in enumerate([OWN[t]] + NEXT[t:t + 1]):
+            at = 176 * t + 88 * s
+            aff(A("dd", at + 3, at + 88, 4), A("cb", 0, 22), 1.0, j0 + base - WINDOW[t][0])
+            fill("e0", at + 2, at + 88, 4, NUM - base)
+        aff(A("rc", o + 48, o + 96), A("rc", o, o + 48), -1.0, col["self"])
+        aff(A("rc", o + 96, o + 99), A("rc", o, o + 48, 16), 4096.0, 255.0 + pr)
+        aff(A("rc", o + 100, o + 103), A("rc", o, o + 48, 16), 4096.0, pr)
 
     def table():
-        aff(A("tb", 8, 8 + J), io(0, J), 4096.0, 2.0 ** 23)
+        aff(A("tb", 32, 32 + J), io(0, J), 4096.0, 2.0 ** 23)
 
     def by_column_1(t):
-        tr(A("tt", 0, C), A("win%d" % t, C * hi[t], C * hi[t] + C))
-        for e in range(2):
-            tc(A("pl", 12 * e, 12 * e + 12), A("tt", 16 * e, 384, 32))
+        tr(A("tt", 0, C), own_win(t, C * hi[t], C * hi[t] + C))
+        tc(A("pl", 0, 24), A("tt", 0, 384, 16))
 
     def by_column_2():
         for a in range(4):
@@ -290,16 +312,7 @@ def rank_program(g, core, T, topo):
     quant(A("qx0"), A("sx0"), A("xt"))
     send_x(0)
     quant(A("qe"), A("se"), A("et"))
-    op("g", [A("coef")], [A("coef")], lambda: g.affine_select(ap(A("coef")), ap(A("coef")), [[0, 3], [1, 8], [1, 8]], O.not_equal, -1.0, -7, 0))
-    iota(A("rc", 0, 32), [[128, 4], [0, 8]], 0, 1)
-    iota(A("c96"), [[0, 12], [1, 8]], 1, 0)
-    for k in range(3):
-        iota(A("c96", 24 * k + 8, 24 * k + 16), [[1, 8]], -2, 0)
-    for k in (1, 3):
-        iota(A("win0", J * k, J * k + J), [[1, J]], 0, 0)
     unpack("psa", "qx0", "sx0")
-    for b in range(4):
-        halve("psa", C * hi[0], b)
     tc(A("la", 0, 22), A("vgi"))
     ts(cu["unb"], io(0, 22), col["q22"], O.add)
     ts(col["corr"], col["q"], 15.0, O.is_lt, 4096.0, O.mult)
@@ -308,69 +321,69 @@ def rank_program(g, core, T, topo):
     ts(cu["m16"], A("zz", 0, 22), col["q"], O.add)
     ts(A("zo"), io(0, 4), col["a"], O.not_equal, BIG, O.mult)
     tt(A("c16", 32, 48), A("c16", 0, 16), A("c16", 16, 32), O.add)
-    tc(A("win0", C * hi[0], C * hi[0] + C), ind(A("vb", 0, C), cu["unb"]))
+    tc(own_win(0, C * hi[0], C * hi[0] + C), ind(A("vb", 0, C), cu["unb"]))
     act(A("ctrl"), ind(A("c16", 32, 48), cu["m16"]))
-    by_column_1(0)
-    ts(A("uw", 0, 4), io(0, 8, 2), col["hb"], O.add)
+    for b in range(4):
+        halve("psa", C * hi[0], b)
+    ts(A("uw", 288, 360), A("uw", 216, 288), 128.0, O.is_ge, 128.0, O.mult)
     ts(col["x0"], col["b1"], col["b5"], O.not_equal, 24.0, O.mult)
-    ts(A("uw", 4, 8), A("uw", 0, 4), col["i8"], O.add, -7.0, O.add)
     ts(col["x1"], col["b2"], col["b6"], O.not_equal, 48.0, O.mult)
-    ts(A("uw", 8, 12), A("uw", 4, 8), 0.0, O.is_lt)
-    ts(col["x2"], col["b0"], 12.0, O.mult, col["a"], O.add)
-    ts(A("uw", 12, 16), A("uw", 8, 12), col["c7"], O.mult)
-    ts(A("uw", 16, 20), A("uw", 8, 12), col["c1"], O.mult)
-    ts(col["x3"], col["hb"], 4.0, O.mult, col["x0"], O.add)
-    ts(A("uw", 28), col["hb"], -128.0, O.mult, 128.0, O.add)
-    tt(A("uw", 20, 24), A("uw", 12, 16), A("uw", 4, 8), O.add)
-    tt(A("uw", 24, 28), A("uw", 16, 20), A("uw", 0, 4), O.add)
-    ts(A("cu", 80), col["x3"], col["x1"], O.add, col["x2"], O.add)
-    tc(A("cu", 66), col["fb"])
-    ts(A("cu", 67), col["hb"], 64.0, O.mult, col["fb"], O.add)
-    ts(A("cu", 68, 70), io(64, 192, 64), col["fb"], O.add)
-    ts(A("upk"), A("uw", 20, 28), 16.0, O.mult)
-    ts(A("cu", 70), A("uw", 28), col["fb"], O.add)
-    ts(A("cu", 71), A("cu", 67), 64.0, O.add)
-    ts(A("cu", 81), A("cu", 80), 8.0, O.add)
+    ts(col["x2"], col["a"], 2.0, O.mult, col["b0"], O.add)
+    tt(A("uw", 360, 432), A("uw", 216, 288), A("uw", 288, 360), O.subtract)
+    by_column_1(0)
+    ts(col["x3"], col["x0"], col["x1"], O.add, col["x2"], O.add)
+    tt(A("uw", 0, 72), A("uw", 144, 216), A("uw", 360, 432), O.min)
+    tt(A("uw", 72, 144), A("uw", 144, 216), A("uw", 360, 432), O.max)
+    ts(cu["kg"], io(0, 24, 8), col["x3"], O.add, col["hb96"], O.max)
     quant(A("qu"), A("su"), A("ut"))
-    for k in range(3):
-        ts(A("zc", 8 * k, 8 * k + 8), io(0, 8), 0.0625, O.mult)
-    op("v", [A("qp")], [A("qu"), A("upk")], lambda: V.tensor_copy(T.qp[:, 0:128].bitcast(dt.uint32), T.qu[:, 0:128].bitcast(dt.uint32).indirect(T.upk[:, 0:8])))
-    op("v", [A("sp")], [A("su"), A("upk")], lambda: V.tensor_copy(T.sp[:, 0:128], T.su[:, 0:128].indirect(T.upk[:, 0:8])))
-    ms(A("yt", 4 * C, 1536), 0.0)
+    scan(A("w8", 0, 8), A("w8", 8, 16), A("zz", 0, 8), O.mult, O.add, 0.5)
+    listed(A("uw", 0, 144), A("upk", 0, 9), 144)
     for e in range(2):
-        ts(A("cu", 72 + e, 78, 2), io(0, 24, 8), 7.0, O.add)
-    ms(A("coef", 0, 192, 8), 0.0)
-    tt(col["pw"], col["pq"], col["pe"], O.mult)
-    ts(A("uw", 30, 32), io(0, 16, 8), col["qh"], O.add, 10.0, O.min)
+        ts(A("cu", 44 + e, 50, 2), io(0, 3), 378.0, O.mult, col["fb"], O.add)
     for k in range(3):
-        ts(cu["q%d" % k], A("uw", 30, 32), 11.0 * hi[k], O.add)
+        ts(A("cb", 24 + 16 * k, 40 + 16 * k), A("zz", 0, 16), col["P"], O.add, 128.0 * k, O.add)
+        ts(A("zc", 16 * k, 16 * k + 16), io(1, 17), 0.0625, O.mult)
+        ts(A("dz", 42 * k + 9, 42 * k + 41), io(0, 32), col["j32"], O.is_equal, -K, O.mult)
+    op("v", [A("qp")], [A("qu"), A("upk")], lambda: V.tensor_copy(T.qp[:, 0:144].bitcast(dt.uint32), T.qu[:, 0:128].bitcast(dt.uint32).indirect(T.upk[:, 0:9])))
+    op("v", [A("sp")], [A("su"), A("upk")], lambda: V.tensor_copy(T.sp[:, 0:144], T.su[:, 0:128].indirect(T.upk[:, 0:9])))
+    ms(A("yt", 4 * C, 1536), 0.0)
+    ts(A("uw", 288, 290), io(0, 2), col["e"], O.is_equal, BIG, O.mult)
+    tt(col["pw"], col["pq"], col["pe"], O.mult)
+    ts(cu["q"], io(0, 16, 8), col["qh"], O.add, 10.0, O.min)
+    ts(A("me"), A("uw", 288, 290), -16.0, O.add)
+    ms(A("s1"), 0.0)
+    ms(A("ti"), 0.0)
     aff(A("cb", 0, 22), io(0, C, 16), 1.0, col["q"])
-    round_constants(0)
+    aff(A("dz", 41, 126, 42), A("zz", 0, 3), 1.0, col["last"])
+    for k in range(3):
+        aff(A("wt", 32 * k, 32 * k + 8), A("w8", 0, 8), -1.0, 0.0)
+        aff(A("wt", 32 * k + 8, 32 * k + 16), A("w8", 0, 8), 1.0, 0.0)
     by_column_2()
-    act(A("mk"), io(0, 32), AF.Relu, 8.0, col["mb"])
+    round_constants(0)
     table()
-    tc(A("win0", C - C * hi[0], J - C * hi[0]), ind(A("vb", C, J), cu["unb"]))
-    tc(A("ppf"), ind(A("win0", 0, J), A("la", 0, 22)))
+    for j in (8, 24):
+        aff(A("ti", j, J, 32), io(0, J, 32), 1.0, col["j32"])
+    tc(own_win(0, C - C * hi[0], J - C * hi[0]), ind(A("vb", C, J), cu["unb"]))
+    tc(A("ppf"), ind(own_win(0), A("la", 0, 22)))
     share(0)
     listed(A("ppf"), A("lb", 0, 22))
     unpack("psb", "lq0", "ls0")
     for b in range(4):
-        halve("psb", C * (1 - hi[0]), b)
+        halve("psb", C * (1 - hi[0]), b, "a" if b == 1 else "v")
+    for b in range(4):
         first(0, b)
-    iota(A("ti"), [[0, J]], 0, 0)
-    for a in range(4):
-        iota(A("ti", 8, J, 16, 32 * a, 32 * a + 32), [[32, 22], [0, 2]], 0, 1)
-    for k in (1, 3):
-        iota(A("win1", J * k, J * k + J), [[1, J]], 0, 0)
 
     for t in range(3):
-        o = 192 * t
+        o = 152 * t
+        down = (2, 1, 0)
         for b in range(4):
             tt(A("yt", b, 4 * C, 4), ind(A("fj", J * b, J * b + J), A("lb", 22 * t, 22 * t + 22)), A("ab", C * b, C * b + C), O.add)
+        pk = ind(A("pl"), cu["kg"])
+        tt(A("pw", 0, 48), pk, A("rc", o, o + 48), O.is_equal)
         quant(A("qy"), A("sy"), A("yt"))
-        for k in range(3):
-            mm(A("psb", 512 * k, 512 * k + 128), A("qy", 128 * k, 128 * k + 128), A("sy", 128 * k, 128 * k + 128), A("qp"), A("sp"))
-        bank = [3, 0, 1, 2]
+        for k in down:
+            mm(A("psb", 512 * k, 512 * k + 144), A("qy", 128 * k, 128 * k + 128), A("sy", 128 * k, 128 * k + 128), A("qp"), A("sp"))
+        bank = [3, 2, 1, 0]
 
         def layer(b):
             mm(A("psb", 512 * bank[b], 512 * bank[b] + C), A("qw", 128 * b, 128 * b + 128), A("sw", 128 * b, 128 * b + 128), A("qy", 0, C), A("sy", 0, C))
@@ -378,59 +391,91 @@ def rank_program(g, core, T, topo):
         def relu(b):
             act(A("rl", C * b, C * b + C), A("psb", 512 * bank[b], 512 * bank[b] + C), AF.Relu, scale=0.03125)
 
+        left = [(b, h) for b in range(4) for h in range(2)]
+
+        def state(n=1):
+            for b, h in left[:n]:
+                c0, c1 = C // 2 * h, C // 2 * h + C // 2
+                tt(A("xn", b + 4 * c0, 4 * c1, 4), A("psa", 512 * b + c0, 512 * b + c1), A("rl", C * b + c0, C * b + c1), O.add)
+            del left[:n]
+
         layer(0)
-        pk = ind(A("pl"), cu["kg"])
-        tt(A("pw", 0, 32), pk, A("rc", o + 32, o + 64), O.is_equal)
-        tt(A("pw", 32, 64), A("pw", 0, 32), A("rc", o + 64, o + 96), O.mult)
-        tt(A("pw", 64, 96), pk, A("pw", 32, 64), O.add)
-        tt(A("pw", 96, 120), A("pw", 64, 88), A("zc"), O.add)
+        tt(A("pw", 48, 96), A("pw", 0, 48), A("rc", o + 48, o + 96), O.mult)
         for k in range(3):
-            act(A("sr", 64 * k, 64 * k + 64), A("psb", 512 * k + 64, 512 * k + 128))
-            tt(A("fl", 64 * k, 64 * k + 64), A("psb", 512 * k, 512 * k + 64), A("sr", 64 * k, 64 * k + 64), O.is_ge)
+            aff(A("wt", 32 * k + 24, 32 * k + 32), A("pw", 16 * k, 16 * k + 8), BIG, A("rc", o + 100 + k))
+        tt(A("pw", 96, 144), pk, A("pw", 48, 96), O.add)
+        tt(A("pw", 144, 192), A("pw", 96, 144), A("zc"), O.add)
+        for k in down:
+            tt(A("dz", 42 * k + 1, 42 * k + 9), A("pw", 96 + 16 * k, 104 + 16 * k), A("pw", 97 + 16 * k, 105 + 16 * k), O.subtract)
+        for k in down:
+            act(A("sr", 72 * k, 72 * k + 72), A("psb", 512 * k + 72, 512 * k + 144))
+            tt(A("fl", 72 * k, 72 * k + 72), A("psb", 512 * k, 512 * k + 72), A("sr", 72 * k, 72 * k + 72), O.is_ge)
+            if k < 2:
+                scan(A("s1", 378 * k + 378, 378 * k + 450), A("coef"), A("fl", 72 * k + 72, 72 * k + 144), O.mult, O.add)
         for b in range(1, 4):
             layer(b)
-        aff(A("wt", 72, 96), A("pw", 64, 88), 2.0 ** -12, 2.0 ** -9)
         for k in range(3):
-            aff(A("wt", 24 * k + 16, 24 * k + 24), A("pw", 96 + 8 * k, 104 + 8 * k), 4096.0, 511.0 + 2.0 ** 22 * hi[t])
+            aff(A("wt", 32 * k + 16, 32 * k + 24), A("pw", 144 + 16 * k, 152 + 16 * k), 4096.0, 255.0 + 2.0 ** 22 * hi[t])
         relu(0)
-        scan(A("s1"), A("coef"), A("fl"), O.mult, O.add)
+
+        def asked(k):
+            scan(A("z", 42 * k, 42 * k + 42), A("dz", 42 * k, 42 * k + 42), A("s1", 378 * k + 8, 378 * k + 378, 9), O.add, O.max)
+
+        def turned(k):
+            tr(A("t96", 32 * k, 32 * k + 32), A("z", 42 * k + 8, 42 * k + 40))
+
+        def repeats(k):
+            ts(A("z", 42 * k + 8, 42 * k + 40), A("t96", 32 * k, 32 * k + 32), A("z", 42 * k + 40), O.not_equal, BIG, O.mult)
+
+        asked(2)
+        scan(A("s1", 0, 72), A("coef"), A("fl", 0, 72), O.mult, O.add)
+        asked(1)
+        turned(2)
         tt(A("f96"), ind(A("s1"), cu["F"]), A("c96"), O.is_ge)
+        asked(0)
+        turned(1)
         tt(A("fw"), A("f96"), A("wt"), O.mult)
-        scan(A("so"), A("rs", 0, 96), A("fw"), O.mult, O.add)
-        tsc = A("so", 79, 96, 8)
-        tc(A("r96"), ind(A("so", 72, 96), cu["rept"]))
+        repeats(2)
+        turned(0)
+        scan(A("so"), A("rs"), A("fw"), O.mult, O.add)
+        for k in down:
+            aff(A("rb", 32 * k, 32 * k + 32), A("on"), A("so", 15 + 32 * k), A("rc", o + 96 + k))
         for k in range(3):
-            aff(A("rm", 32 * k, 32 * k + 32), A("mk"), 1.0, A("so", 79 + 8 * k))
-        for k in range(3):
-            aff(A("rb", 32 * k, 32 * k + 32), A("on"), A("so", 15 + 24 * k), A("rc", o + 96 + k))
-        act(A("nu", 0, 3), tsc, AF.Relu, 2.0 ** 38, -711.5 * 2.0 ** 26)
-        for k in range(3):
-            aff(A("ar", 24 + 4 * k, 28 + 4 * k), A("zo"), 1.0, A("so", 23 + 24 * k))
-        for k in range(3):
-            aff(A("ar", 40 + 4 * k, 44 + 4 * k), A("th", 12 * t + 4 * k, 12 * t + 4 * k + 4), 1.0, A("nu", k))
+            aff(A("ar2", 4 * k, 4 * k + 4), A("zo"), 1.0, A("so", 23 + 32 * k))
+            aff(A("ar2", 12 + 4 * k, 16 + 4 * k), A("zo"), 1.0, A("so", 31 + 32 * k))
         for b in range(1, 4):
             relu(b)
-        tr(A("t96"), A("r96"))
-        tt(A("eq"), A("t96"), A("rm"), O.is_equal)
-        scan(A("dup"), A("rs", 96, 192), A("eq"), O.mult, O.max)
-        tr(A("tbv"), A("rb"))
-        tt(A("m1", 0, 3), A("dup", 31, 96, 32), tsc, O.max)
-        for e in range(2):
-            ts(A("lsc", e, 6, 2), A("m1", 0, 3), col["S%d" % e], O.mult, col["D%d" % e], O.min)
-        for k in (2, 1, 0):
+        repeats(1)
+        repeats(0)
+        for k in down:
+            least(A("m3", k), A("z", 42 * k + 8, 42 * k + 42))
+        for k in down:
+            ts(A("lsc", 2 * k, 2 * k + 2), A("me"), A("m3", k), O.min, col["r16"], O.add)
+        for k in down:
+            tr(A("tbv", 32 * k, 32 * k + 32), A("rb", 32 * k, 32 * k + 32))
+        for k in down:
             tc(ind(A("tb"), A("lsc", 2 * k, 2 * k + 2)), A("tbv", 32 * k, 32 * k + 32))
-        tr(A("tt7"), A("tb", 8, 8 + J))
-        tt(A("ar", 0, 22), A("tt7", 0, J, 32), A("tt7", 16, J, 32), O.min)
-        tt(A("a1", p1=64), A("ar", p1=64), A("ar", p0=64), O.min)
-        w = 56 * t
+            if k:
+                state()
+        tt(A("b1", p1=64), A("ar2", p1=64), A("ar2", p0=64), O.min)
+        tr(A("tt7"), A("tb", 32, 32 + J))
         for a in range(2):
-            tt(A("wout", w, w + 56, p0=32 * a, p1=32 * a + 32), A("a1", p1=32), A("a1", p0=32, p1=64), O.min)
+            tt(A("b2", p0=32 * a, p1=32 * a + 32), A("b1", p1=32), A("b1", p0=32, p1=64), O.min)
+        tt(A("ar", 0, 22), A("tt7", 0, J, 32), A("tt7", 16, J, 32), O.min)
+        state()
+        tt(A("a1", 0, 22, p1=64), A("ar", 0, 22, p1=64), A("ar", 0, 22, p0=64), O.min)
+        state()
+        w = 24 * t
+        for a in range(2):
+            tt(A("wout", w, w + 22, p0=32 * a, p1=32 * a + 32), A("a1", 0, 22, p1=32), A("a1", 0, 22, p0=32, p1=64), O.min)
+        state()
         own = A("wout", w + 11 * hi[t], w + 11 * hi[t] + 11, p1=64)
-        tt(A("mg", 0, 11, p1=64), A("wout", w + 40, w + 51, p1=64), own, O.is_lt)
-        tt(A("mg", 16, 27, p1=64), A("wout", w + 24, w + 35, p1=64), own, O.subtract)
+        tt(A("mg", 0, 11, p1=64), A("b2", 12, 23, p1=64), own, O.is_lt)
+        tt(A("mg", 16, 27, p1=64), A("b2", 0, 11, p1=64), own, O.subtract)
+        state()
         tt(A("mg", 32, 43, p1=64), A("mg", 0, 11, p1=64), A("mg", 16, 27, p1=64), O.mult)
+        state()
         tt(own, own, A("mg", 32, 43, p1=64), O.add)
-        tc(A("wout", w, w + 22, p0=64), A("wout", w, w + 22, p1=64))
         W = A("wout", w, w + 22)
         to = [STEP[t]] + ([STEP[t + 1], STEP[t] ^ STEP[t + 1]] if t < 2 else [])
         lands = [A("wl", 24 * (3 * t + k), 24 * (3 * t + k) + 22) for k in range(len(to))]
@@ -443,83 +488,77 @@ def rank_program(g, core, T, topo):
                                               srcs=[ap(W)], dsts=[ap(a) for a in lands])], local_sem=T.sem["sent"])
         cnt["sent"] += bin(m).count("1")
         arrive("aw%d" % t, bin(m).count("1") * len(to), lands)
-        for b in range(4):
-            tt(A("xn", b, 4 * C, 4), A("psa", 512 * b, 512 * b + C), A("rl", C * b, C * b + C), O.add)
+        state(8)
         qn, sn = "qx%d" % (t + 1), "sx%d" % (t + 1)
         quant(A(qn), A(sn), A("xn"))
         if t < 2:
             send_x(t + 1)
             unpack("psa", qn, sn)
+            table()
             for b in range(4):
                 halve("psa", C * hi[t + 1], b)
-            table()
             round_constants(t + 1)
-            if t == 0:
-                iota(A("win2", J, 2 * J), [[1, J]], 0, 0)
         else:
             quant(A("qv"), A("sv"), A("vt"))
             mm(A("psa", 0, C), A("qv"), A("sv"), A(qn), A(sn))
             dma("s", [(ext(T.oc[:]), cast(A(qn), dt.uint8))] + [(ext(T.osc[4 * k:4 * k + 4, :]), A(sn, p0=32 * k, p1=32 * k + 4)) for k in range(4)])
             act(A("yo"), A("psa", 0, C))
             dma("a", [(ext(T.y[:]), A("yo"))])
-        if t < 2:
-            tt(A("ti", 0, J, 32, p1=64), A("wout", w, w + 22, p1=64), A("wl", 72 * t, 72 * t + 22, p1=64), O.min)
-            tt(A("ti", 0, J, 32, p0=64), A("wl", 72 * t + 24, 72 * t + 46, p0=64), A("wl", 72 * t + 48, 72 * t + 70, p0=64), O.min)
-        else:
-            tt(A("ti", 0, J, 32), W, lands[0], O.min)
-        tc(A("ti", 16, J, 32), A("ti", 0, J, 32))
-        tc(A("vi", 0, 22), A("ti", 0, J, 32))
-        tr(A("wv"), A("ti"))
-        ts(A("oi"), ind(A("vi", 0, 22), cu["q%d" % t]), 12, sh, 1023, an)
+        two = [("wout", w, "wl", 72 * t), ("wl", 72 * t + 24, "wl", 72 * t + 48) if t < 2 else ("wout", w, "wl", 72 * t)]
+
+        def lower(n, c0, c1, st, at, wide):
+            for s, (n0, a0, n1, a1) in enumerate(two):
+                tt(A(n, c0, c1, st, 64 * s, 64 * s + 64), A(n0, a0 + at, a0 + at + wide, p1=64), A(n1, a1 + at, a1 + at + wide, p1=64), O.min)
+
+        lower("vi", 0, 11, 1, 11 * hi[t], 11)
+        lower("ti", 0, J, 32, 0, 22)
+        lower("ti", 16, J, 32, 0, 22)
+        ts(A("oi"), ind(A("vi", 0, 11), cu["q"]), 12, sh, 1023, an)
+        tr(A("wv", 0, C), A("ti", 0, C))
         tc(A("lq"), A("oi", 0, 22))
-        act(A("gq", 192, C), ind(A("wv"), A("lq", 12, 22)))
-        tc(A("gq", 0, 192), ind(A("wv"), A("lq", 0, 12)))
-        tr(A("tg"), A("gq"))
-        if t < 2:
-            n = 44
-            for s in range(2):
-                for d in range(2):
-                    tc(A("rw", 44 * s, 44 * s + 44, p0=64 * d, p1=64 * d + 64), A("tg", 0, C, 8, p0=64 * s, p1=64 * s + 64))
-        else:
-            n = 22
-            tc(A("rw", 0, 44), A("tg", 0, C, 8))
-        Vw, Mw = A("rw", 0, 2 * n, 2), A("rw", 1, 2 * n, 2)
-        p = [A("p7", 44 * k, 44 * k + n) for k in range(11)]
-        nj, nb = A("rc", o + 104, o + 104 + n), A("rc", o + 148, o + 148 + n)
-        ts(p[0], Vw, col["pw"], O.mult)
-        ts(p[1], Vw, 12, sh, 1023, an)
-        ts(p[2], Vw, 8, sh, 15, an)
-        ts(p[3], p[0], 7, sh, 1, an)
-        tt(p[4], p[1], nj, O.is_equal)
-        ts(p[5], p[2], col["g1"], O.is_equal, float(J), O.mult)
-        tt(p[6], Mw, nj, O.subtract)
-        tt(p[7], p[3], p[4], O.mult)
-        tt(p[8], p[6], p[5], O.add)
-        tt(p[9], p[8], p[7], O.mult)
-        tt(p[10], p[9], nb, O.add)
-        tc(A("ix", 0, n), p[10])
-        w0, w1 = A("win%d" % t), "win%d" % (t + 1)
+        tr(A("wv", C, J), A("ti", C, J))
+        split("gq", 0, A("wv"), "lq", 0)
         at = C * hi[t + 1] if t < 2 else 0
         if t < 2:
-            act(A(w1, C - at, J - at), ind(w0, A("ix", 22, 44)))
-            tc(A(w1, at, at + C), ind(w0, A("ix", 0, 22)))
-            listed(A(w1, at, at + C), A("la", 22 * t + 22, 22 * t + 44))
             unpack("psb", "lq%d" % (t + 1), "ls%d" % (t + 1))
-            for b in range(2):
+            for b in range(4):
                 halve("psb", C - at, b)
-            act(A("ppf"), ind(A(w1, 0, J), A("la", 22 * t + 22, 22 * t + 44)))
+        tr(A("tg"), A("gq"))
+        d = 176 * t
+        n = 44 if t < 2 else 22
+        cn = [o + 104, o + 148, 1]
+        if t < 2:
+            for s in range(2):
+                for h in range(2):
+                    tt(A("dd", d + 88 * s, d + 88 * s + 88, 2, 64 * h, 64 * h + 64), A("tg", 0, C, 8, 64 * s, 64 * s + 64), A("rc", *cn, 64 * s, 64 * s + 64), O.subtract)
+        else:
+            tt(A("dd", d, d + 88, 2), A("tg", 0, C, 8), A("rc", *cn), O.subtract)
+        D = A("dd", d, d + 4 * n, 4)
+        p = [A("p7", 44 * k, 44 * k + n) for k in range(5)]
+        ts(p[0], D, col["pw"], O.mult)
+        tc(p[1], D)
+        ts(p[2], p[0], 7, sh, 1, an)
+        ts(p[3], p[1], 12, sh, 1023, an)
+        ts(p[4], p[1], 8, sh, 16383, an)
+        tt(A("e0", d + 3, d + 4 * n, 4), p[2], p[3], O.is_gt)
+        ts(A("dd", d + 1, d + 4 * n, 4), p[4], col["g1"], O.is_equal)
+        scan(A("so2", 0, 4 * n), A("e0", d, d + 4 * n), A("dd", d, d + 4 * n), O.mult, O.add)
+        tc(A("ix", 0, n), A("so2", 3, 4 * n, 4))
+        w0 = A("win", *WINDOW[t])
+        if t < 2:
+            split("win", OWN[t + 1] + at, w0, "ix", 0)
+            act(own_win(t + 1, C - at, J - at), ind(w0, A("ix", 22, 44)))
+            listed(own_win(t + 1, at, at + C), A("la", 22 * t + 22, 22 * t + 44))
+            split("ppf", 0, own_win(t + 1), "la", 22 * t + 22)
             by_column_1(t + 1)
             listed(A("ppf"), A("lb", 22 * t + 22, 22 * t + 44))
             for b in range(4):
-                if b >= 2:
-                    halve("psb", C - at, b)
                 first(t + 1, b)
             by_column_2()
             if t == 0:
                 share(1)
         else:
-            act(A(w1, 192, C), ind(w0, A("ix", 12, 22)))
-            tc(A(w1, 0, 192), ind(w0, A("ix", 0, 12)))
-            dma("s", [(ext(T.ov[:]), A(w1, ps=16))])
+            split("wov", 0, w0, "ix", 0)
+            dma("s", [(ext(T.ov[:]), A("wov", ps=16))])
     for s, n in cnt.items():
         g.wait_ge(T.sem[s], n)

@@ -17,16 +17,17 @@ SCRATCH = {
     "qv": sb(128, MX), "sv": sb(128, U8), "qw": sb(512, MX), "sw": sb(512, U8), "qe": sb(512, MX), "se": sb(512, U8),
     "psa": ("psum", [128, 2048], F32), "psb": ("psum", [128, 2048], F32),
     "pi": sb(16, I32), "cc": sb(48), "zz": sb(192), "upk": sb(10, U16), "uw": sb(432), "cu": sb(64, U16), "c16": sb(48), "ctrl": sb(C),
-    "coef": sb(72), "c96": sb(96), "wt": sb(96), "rs": sb(96), "on": sb(32), "zo": sb(4), "me": sb(2), "zc": sb(48), "w8": sb(16),
-    "rc": sb(3 * 152), "cb": sb(72), "vgi": sb(22, I32), "vb": sb(J, I32), "dv0": ("dram", [128, 22], I32), "dv": ("dram", [128, 22], I32),
+    "coef": sb(72), "c32": sb(32), "wt": sb(32), "rs": sb(32), "on": sb(32), "zo": sb(8), "me": sb(4), "zc": sb(8),
+    "rc": sb(3 * 168), "cb": sb(72), "vgi": sb(22, I32), "vb": sb(2 * J, I32),
+    "dv0": ("dram", [128, 22], I32), "dv": ("dram", [128, 22], I32), "dv2": ("dram", [128, 22], I32), "dv3": ("dram", [128, 22], I32),
     "win": sb(6 * J), "wov": sb(C),
-    "la": sb(66, U16), "lb": sb(66, U16), "ppf": sb(C), "sc": sb(C), "tt": sb(384), "pl": sb(104), "pw": sb(4 * 48),
-    "sr": sb(216), "fl": sb(216), "s1": sb(1134), "dz": sb(126), "z": sb(126), "f96": sb(96), "fw": sb(96), "so": sb(96), "t96": sb(96),
-    "m3": sb(4), "lsc": sb(6, U16), "rb": sb(96), "tbv": sb(96),
+    "la": sb(66, U16), "lb": sb(66, U16), "ppf": sb(C), "sc": sb(2 * C), "tt": sb(384), "pl": sb(104), "pw": sb(3 * 48),
+    "sr": sb(216), "fl": sb(216), "s1": sb(3 * 384), "dz": sb(126), "z": sb(126), "f96": sb(96), "fw": sb(96), "so": sb(96), "t96": sb(96),
+    "m3": sb(4), "ow": sb(8), "lsc": sb(6, U16), "rb": sb(96), "tbv": sb(96),
     "tb": sb(32 + J), "tt7": sb(J), "ar": sb(24), "a1": sb(24), "ar2": sb(24), "b1": sb(24), "b2": sb(24), "mg": sb(48), "wout": sb(3 * 24), "wl": sb(7 * 24),
     "vi": sb(16, I32), "ti": sb(J), "wv": sb(J), "oi": sb(32, I32), "lq": sb(22, U16), "gq": sb(C), "tg": sb(C),
     "dd": sb(3 * 176), "e0": sb(3 * 176), "so2": sb(176), "p7": sb(44 * 5, I32), "ix": sb(44, U16),
-    "dsrc0": ("dram", [128, 44], F32), "dsrc1": ("dram", [128, 44], F32), "dland0": ("dram", [128, 44], F32), "dland1": ("dram", [128, 44], F32),
+    "dsrc1": ("dram", [128, 44], F32), "dland1": ("dram", [128, 44], F32),
 }
 for _t in range(4):
     SCRATCH["qx%d" % _t] = sb(C, MX)
@@ -40,6 +41,8 @@ K = 2048.0
 TOP = 7 * 4096 + 1.0
 OWN, NEXT, NUM = [J, 3 * J, 5 * J], [0, 4 * J], 2 * J
 WINDOW = [(0, 3 * J), (2 * J, 5 * J), (2 * J, 6 * J)]
+CHUNK = [(0, 128), (128, 256), (256, C)]
+DOWN = (2, 1, 0)
 
 
 def rank_program(g, core, T, topo):
@@ -58,8 +61,8 @@ def rank_program(g, core, T, topo):
         c0, c1 = (0, w) if c0 is None else (c0, c0 + 1 if c1 is None else c1)
         ap = T[n][slice(p0, p1, ps) if ps > 1 else slice(p0, p1), slice(c0, c1, st) if st > 1 else slice(c0, c1)]
         if SCRATCH[n][0] == "psum":
-            return {"ap": ap, "r": [(n, 0, 128, c0 // 512 * 512, c0 // 512 * 512 + 512, 1)], "x": True}
-        return {"ap": ap, "r": [(n, p0, p1, c0, c1, st)]}
+            return {"ap": ap, "r": [(n, 0, 128, c0 // 512 * 512, c0 // 512 * 512 + 512, 1, 1)], "x": True}
+        return {"ap": ap, "r": [(n, p0, p1, c0, c1, st, ps)]}
 
     def ind(w, o):
         return {"ap": w["ap"].indirect(o["ap"]), "r": w["r"] + o["r"], "w": w["r"], "o": o["r"]}
@@ -73,7 +76,7 @@ def rank_program(g, core, T, topo):
     def meet(a, b):
         if a[1] >= b[2] or b[1] >= a[2] or a[3] >= b[4] or b[3] >= a[4]:
             return False
-        return not (a[5] == b[5] and a[5] > 1 and (a[3] - b[3]) % a[5])
+        return not any(a[s] == b[s] and a[s] > 1 and (a[c] - b[c]) % a[s] for s, c in ((5, 3), (6, 1)))
 
     def wait(q, ev):
         if know[q].get(ev[0], 0) < ev[1]:
@@ -139,6 +142,17 @@ def rank_program(g, core, T, topo):
         cnt["sent"] = cnt.get("sent", 0) + bin(m).count("1")
         return bin(m).count("1")
 
+    def spread(to, i, lands, sem):
+        deps("g", [], [i])
+        m = topo.mask(core, peer(to[0]))
+        for x in to:
+            m &= topo.mask(core, peer(x))
+        ids = [topo.addr(peer(x), core) for x in to]
+        g.remote_dma_fused([RemoteDMATransfer(dst_ids=[DstId(rid=r_, pnc=p_) for r_, p_ in ids], dma_engine_mask=m, remote_sem=T.sem[sem],
+                                              srcs=[ap(i)], dsts=[ap(a) for a in lands])], local_sem=T.sem["sent"])
+        cnt["sent"] = cnt.get("sent", 0) + bin(m).count("1")
+        arrive(sem, bin(m).count("1") * len(to), lands)
+
     V = g.vector
 
     def tc(o, i):
@@ -192,10 +206,11 @@ def rank_program(g, core, T, topo):
             op("g", [o], [], lambda: g.iota(ap(o), pat, base, cm))
 
     hi = [1 if rank & s else 0 for s in STEP]
-    names = ["P", "q", "j32", "e", "g", "hb", "i8", "a", "qh", "b0", "b1", "b2", "b5", "b6", "g1", "q1", "corr", "pw", "fb", "pq", "pe", "q22",
+    names = ["P", "q", "j32", "e", "g", "hb", "i8", "a", "qh", "b0", "a2", "g1", "q1", "corr", "pw", "fb", "pq", "pe", "q22",
              "r16", "self", "last", "hb96", "x0", "x1", "x2", "x3"]
     col = {n: A("cc", k) for k, n in enumerate(names)}
-    cu = {"unb": A("cu", 0, 22), "m16": A("cu", 22, 44), "F": A("cu", 44, 50), "kg": A("cu", 50, 53), "q": A("cu", 54, 56)}
+    cu = {"unb": A("cu", 0, 22), "m16": A("cu", 22, 44), "F": A("cu", 44, 46), "kg": A("cu", 50, 53), "q": A("cu", 54, 56)}
+    sh, an = O.arith_shift_right, O.bitwise_and
 
     def io(a, b, st=1):
         return A("win", NUM + a, NUM + b, st)
@@ -203,51 +218,8 @@ def rank_program(g, core, T, topo):
     def own_win(t, c0=0, c1=J, **k):
         return A("win", OWN[t] + c0, OWN[t] + c1, **k)
 
-    dma("a", [(A("dv0"), ext(T.vg[:]))])
-    dma("s", [(A("xt"), ext(T.x[:]))])
-    dma("a", [(A("vgi"), ext(T.vg[:]))])
-    dma("s", [(A("vb", 0, C, p0=r, ps=16), ext(T.vg[:])) for r in range(16)])
-    dma("s", [(A("ut"), ext(T.u[:]))])
-    dma("s", [(cast(A("qw"), dt.uint8), ext(T.wc[:])), (A("sw"), ext(T.ws[:])), (A("vt"), ext(T.v[:]))])
-    iota(A("pi", 0), [[0, 1]], 0, 1, False)
-    iota(io(0, J), [[1, J]], 0, 0)
-    iota(A("uw", 144, 216), [[16, 8], [0, 9]], 0, 0)
-    iota(A("uw", 216, 288), [[16, 8], [16, 9]], 0, 0)
-    arrive("av", send(STEP[0], A("dv"), A("dv0"), "av"), [A("dv")])
-    dma("s", [(A("vb", C, J, p0=r, ps=16), A("dv")) for r in range(16)])
-
-    ms(A("zz"), 0.0)
-    ms(A("et"), 0.0)
-    sh, an = O.arith_shift_right, O.bitwise_and
-    for k, (s_, m_) in enumerate([(0, 15), (0, 31), (4, 1), (4, 7), (3, 1), (0, 7), (5, 3), (1, 7), (0, 1), (1, 1), (2, 1), (5, 1), (6, 1)]):
-        ts(A("pi", k + 1), A("pi", 0), s_, sh, m_, an)
-    tc(A("cc", 0, 14), A("pi", 0, 14))
-    fill("coef", 0, 72, 1, 1)
-    fill("rs", 0, 96, 1, 1)
-    fill("on", 0, 32, 1, 1)
-    fill("w8", 8, 16, 1, 2)
-    fill("c96", 0, 96, 1, 7 * 4096)
-    fill("tt", C, 384, 1, -1)
-    fill("pl", 96, 104, 1, -K)
-    fill("tb", 0, 32, 1, 0)
-    fill("dz", 0, 126, 1, 0)
-    fill("wout", 0, 72, 1, 0)
-    for c0, c1, st, v in ((0, 72, 9, 0), (8, 72, 9, 4096), (16, 57, 8, -1)):
-        fill("coef", c0, c1, st, v)
-    fill("rs", 0, 96, 32, 0)
-    fill("rs", 24, 96, 32, 0)
-    for k in range(3):
-        fill("c96", 32 * k, 32 * k + 8, 1, 4 * 4096)
-    fill("dz", 0, 126, 42, -BIG)
-    fill("coef", 8, 9, 1, -4096)
-    for a in range(4):
-        fill("cc", names.index("pq"), names.index("pq") + 1, 1, 2 ** (7 - 2 * a), 32 * a, 32 * a + 32)
-    for n_, i_, s_, b_ in (("q22", "q", 22, 0), ("q1", "q", 1, 1), ("fb", "i8", 9, 8), ("pe", "e", -0.5, 1), ("g1", "g", 1, 1), ("r16", "q", 1, 16),
-                           ("self", "q", 1, -16), ("last", "q", -1, 16 - TOP), ("hb96", "hb", 96, 0)):
-        aff(col[n_], col[i_], float(s_), float(b_))
-    aff(A("coef", 1, 72, 9), io(0, 8), 1.0, -7.0)
-    for b in range(4):
-        ts(A("et", 512 * b + b, 512 * b + 512, 4), io(0, 128), col["P"], O.is_equal)
+    def lst(n, at, k):
+        return A(n, at + CHUNK[k][0] // 16, at + CHUNK[k][1] // 16)
 
     def send_x(t):
         n = send(STEP[t], cast(A("lq%d" % t), dt.uint8), cast(A("qx%d" % t), dt.uint8), "ad%d" % t)
@@ -265,124 +237,189 @@ def rank_program(g, core, T, topo):
         else:
             ts(o, i, 0.5, O.mult)
 
-    def first(t, b):
-        act(A("ab", C * b, C * b + C), ind(A("fj", J * b, J * b + J), A("la", 22 * t, 22 * t + 22)))
+    def run_max(at, src, c0, c1):
+        scan(A("sc", at + c0, at + c1), A("ctrl", c0, c1), src, O.add, O.max)
 
-    def listed(src, dst, n=C):
-        scan(A("sc", 0, n), A("ctrl", 0, n), src, O.add, O.max)
-        ts(dst, A("sc", 15, n, 16), col["corr"], O.subtract)
-
-    def split(n, at, w, l, l0):
-        act(A(n, at + 192, at + C), ind(w, A(l, l0 + 12, l0 + 22)))
-        tc(A(n, at, at + 192), ind(w, A(l, l0, l0 + 12)))
+    def listed(dst, at, c0, c1):
+        ts(dst, A("sc", at + c0 + 15, at + c1, 16), col["corr"], O.subtract)
 
     def share(t):
         dma("s", [(A("dsrc%d" % t), own_win(t, ps=16))])
         arrive("af%d" % t, send(STEP[t + 1], A("dland%d" % t), A("dsrc%d" % t), "af%d" % t), [A("dland%d" % t)])
         dma("s", [(A("win", NEXT[t], NEXT[t] + J, p0=r, ps=16), A("dland%d" % t)) for r in range(16)])
 
-    def round_constants(t):
-        o, pr, j0 = 152 * t, 2.0 ** 22 * hi[t], float(C * hi[t])
-        aff(A("rc", o, o + 48), A("cb", 24, 72), 1.0, j0)
-        fill("e0", 176 * t, 176 * t + 176, 1, 0)
+    def early_constants(t):
+        o = 168 * t
+        aff(A("rc", o, o + 48), A("cb", 24, 72), 1.0, float(C * hi[t]))
         fill("rc", o + 32, o + 48, 1, -1, 96, 128)
+        aff(A("rc", o + 48, o + 96), A("rc", o, o + 48), -1.0, col["self"])
+
+    def word_constants(t):
+        o, pr = 168 * t, 2.0 ** 22 * hi[t]
+        aff(A("rc", o + 148, o + 152), A("zo", 4, 8), 1.0, 255.0 + pr)
+        aff(A("rc", o + 96, o + 99), A("rc", o, o + 48, 16), 4096.0, 255.0 + pr)
+        aff(A("rc", o + 100, o + 103), A("rc", o, o + 48, 16), 4096.0, pr)
+        for k in range(3):
+            aff(A("rc", o + 152 + 4 * k, o + 156 + 4 * k), A("zo", 0, 4), 1.0, A("rc", o + 100 + k))
+
+    def late_constants(t):
+        o, j0 = 168 * t, float(C * hi[t])
+        fill("e0", 176 * t, 176 * t + 176, 1, 0)
         aff(A("rc", o + 104, o + 148, 2), A("cb", 0, 22), 4096.0, 4096 * j0)
         aff(A("rc", o + 105, o + 148, 2), A("cb", 0, 22), 1.0, j0)
         for s, base in enumerate([OWN[t]] + NEXT[t:t + 1]):
             at = 176 * t + 88 * s
             aff(A("dd", at + 3, at + 88, 4), A("cb", 0, 22), 1.0, j0 + base - WINDOW[t][0])
             fill("e0", at + 2, at + 88, 4, NUM - base)
-        aff(A("rc", o + 48, o + 96), A("rc", o, o + 48), -1.0, col["self"])
-        aff(A("rc", o + 96, o + 99), A("rc", o, o + 48, 16), 4096.0, 255.0 + pr)
-        aff(A("rc", o + 100, o + 103), A("rc", o, o + 48, 16), 4096.0, pr)
 
     def table():
         aff(A("tb", 32, 32 + J), io(0, J), 4096.0, 2.0 ** 23)
 
-    def by_column_1(t):
-        tr(A("tt", 0, C), own_win(t, C * hi[t], C * hi[t] + C))
+    def by_column():
         tc(A("pl", 0, 24), A("tt", 0, 384, 16))
+        dma("s", [(A("pl", 24 * m, 24 * m + 24, p0=p0, p1=p1), A("pl", 0, 24, p0=(p0 + 32 * m) % 128, p1=(p0 + 32 * m) % 128 + p1 - p0))
+                  for m in range(1, 4) for p0, p1 in ((0, 128 - 32 * m), (128 - 32 * m, 128))])
 
-    def by_column_2():
-        for a in range(4):
-            act(A("pl", 24, 48, p0=32 * a, p1=32 * a + 32), A("pl", 0, 24, p0=32 * (a ^ 1), p1=32 * (a ^ 1) + 32))
-        for h in range(2):
-            act(A("pl", 48, 96, p0=64 * h, p1=64 * h + 64), A("pl", 0, 48, p0=64 - 64 * h, p1=128 - 64 * h))
+    dma("a", [(A("dv0"), ext(T.vg[:]))])
+    dma("s", [(A("vgi"), ext(T.vg[:]))])
+    dma("s", [(A("xt"), ext(T.x[:]))])
+    dma("s", [(A("vb", 0, C, p0=r, ps=16), ext(T.vg[:])) for r in range(16)])
+    dma("s", [(A("ut"), ext(T.u[:]))])
+    iota(A("pi", 0), [[0, 1]], 0, 1, False)
+    iota(io(0, 128), [[1, 128]], 0, 0)
+    iota(A("uw", 144, 216), [[16, 8], [0, 9]], 0, 0)
+    iota(A("uw", 216, 288), [[16, 8], [16, 9]], 0, 0)
+    spread([STEP[0], STEP[1], STEP[0] ^ STEP[1]], A("dv0"), [A("dv"), A("dv2"), A("dv3")], "av")
+    dma("s", [(A("vb", C, J, p0=r, ps=16), A("dv")) for r in range(8)])
 
-    quant(A("qx0"), A("sx0"), A("xt"))
-    send_x(0)
-    quant(A("qe"), A("se"), A("et"))
-    unpack("psa", "qx0", "sx0")
+    ms(A("zz"), 0.0)
+    ms(A("et"), 0.0)
+    for k, (s_, m_) in enumerate([(0, 15), (0, 31), (4, 1), (4, 7), (3, 1), (0, 7), (5, 3), (1, 7), (0, 1), (1, 3)]):
+        ts(A("pi", k + 1), A("pi", 0), s_, sh, m_, an)
+    tc(A("cc", 0, 11), A("pi", 0, 11))
+    for n_, c0, c1, v in (("coef", 0, 72, 1), ("rs", 0, 32, 1), ("on", 0, 32, 1), ("zc", 0, 8, 2), ("c32", 0, 8, 4 * 4096), ("c32", 8, 32, 7 * 4096),
+                          ("tt", C, 384, -1), ("pl", 96, 104, -K), ("tb", 0, 32, 0), ("dz", 0, 126, 0), ("wout", 0, 72, 0), ("wt", 24, 32, 0)):
+        fill(n_, c0, c1, 1, v)
+    for n_, i_, s_, b_ in (("q22", "q", 22, 0), ("q1", "q", 1, 1), ("fb", "i8", 9, 8), ("pe", "e", -0.5, 1), ("g1", "g", 1, 1), ("r16", "q", 1, 16),
+                           ("self", "q", 1, -16), ("last", "q", -1, 16 - TOP), ("hb96", "hb", 96, 0), ("x3", "q", 4096, -16 * 4096)):
+        aff(col[n_], col[i_], float(s_), float(b_))
+    for b in range(4):
+        ts(A("et", 512 * b + b, 512 * b + 512, 4), io(0, 128), col["P"], O.is_equal)
+    for n_, c0, c1, st, v in (("coef", 0, 72, 9, 0), ("coef", 8, 72, 9, 4096), ("coef", 16, 57, 8, -1), ("rs", 0, 1, 1, 0), ("dz", 0, 126, 42, -BIG), ("coef", 8, 9, 1, -4096)):
+        fill(n_, c0, c1, st, v)
+    aff(A("coef", 1, 72, 9), io(0, 8), 1.0, -7.0)
+    aff(A("dz", 41, 126, 42), A("zz", 0, 3), 1.0, col["last"])
+    pv = [A("p7", 44 * k + c, 44 * k + c + 22) for k in range(3) for c in (0, 22)]
     tc(A("la", 0, 22), A("vgi"))
-    ts(cu["unb"], io(0, 22), col["q22"], O.add)
+    ts(pv[0], A("vgi"), 15, an)
+    ts(pv[1], A("vgi"), 4, sh)
+    ts(pv[2], A("vgi"), float(C), O.is_ge, -374.0 if hi[0] else 330.0, O.mult)
+    quant(A("qe"), A("se"), A("et"))
+    ts(pv[3], pv[0], 22.0, O.mult, float(C * hi[0]), O.add)
+    tt(pv[4], pv[1], pv[2], O.add)
+    ts(A("uw", 288, 360), A("uw", 216, 288), 128.0, O.is_ge, 128.0, O.mult)
     ts(col["corr"], col["q"], 15.0, O.is_lt, 4096.0, O.mult)
+    tt(pv[5], pv[3], pv[4], O.add)
     ts(A("c16", 0, 16), io(0, 16), col["q"], O.is_equal, -2.0 ** 20, O.mult)
     ts(A("c16", 16, 32), io(0, 16), col["q1"], O.is_equal, 4096.0, O.mult)
     ts(cu["m16"], A("zz", 0, 22), col["q"], O.add)
-    ts(A("zo"), io(0, 4), col["a"], O.not_equal, BIG, O.mult)
+    tc(A("ix", 0, 22), pv[5])
     tt(A("c16", 32, 48), A("c16", 0, 16), A("c16", 16, 32), O.add)
-    tc(own_win(0, C * hi[0], C * hi[0] + C), ind(A("vb", 0, C), cu["unb"]))
+    quant(A("qx0"), A("sx0"), A("xt"))
+    send_x(0)
+    iota(A("ti"), [[0, J]], 0, 0)
+    unpack("psa", "qx0", "sx0")
     act(A("ctrl"), ind(A("c16", 32, 48), cu["m16"]))
-    for b in range(4):
-        halve("psa", C * hi[0], b)
-    ts(A("uw", 288, 360), A("uw", 216, 288), 128.0, O.is_ge, 128.0, O.mult)
-    ts(col["x0"], col["b1"], col["b5"], O.not_equal, 24.0, O.mult)
-    ts(col["x1"], col["b2"], col["b6"], O.not_equal, 48.0, O.mult)
-    ts(col["x2"], col["a"], 2.0, O.mult, col["b0"], O.add)
     tt(A("uw", 360, 432), A("uw", 216, 288), A("uw", 288, 360), O.subtract)
-    by_column_1(0)
-    ts(col["x3"], col["x0"], col["x1"], O.add, col["x2"], O.add)
+    ts(cu["unb"], io(0, 22), col["q22"], O.add)
+    ts(A("zo", 0, 4), io(0, 4), col["a"], O.not_equal, BIG, O.mult)
+    ts(A("pi", 12), col["a2"], col["a"], O.subtract, 4.0, O.add)
     tt(A("uw", 0, 72), A("uw", 144, 216), A("uw", 360, 432), O.min)
     tt(A("uw", 72, 144), A("uw", 144, 216), A("uw", 360, 432), O.max)
-    ts(cu["kg"], io(0, 24, 8), col["x3"], O.add, col["hb96"], O.max)
-    quant(A("qu"), A("su"), A("ut"))
-    scan(A("w8", 0, 8), A("w8", 8, 16), A("zz", 0, 8), O.mult, O.add, 0.5)
-    listed(A("uw", 0, 144), A("upk", 0, 9), 144)
-    for e in range(2):
-        ts(A("cu", 44 + e, 50, 2), io(0, 3), 378.0, O.mult, col["fb"], O.add)
     for k in range(3):
         ts(A("cb", 24 + 16 * k, 40 + 16 * k), A("zz", 0, 16), col["P"], O.add, 128.0 * k, O.add)
-        ts(A("zc", 16 * k, 16 * k + 16), io(1, 17), 0.0625, O.mult)
+    ts(A("zo", 4, 8), A("zo", 0, 4), col["x3"], O.add)
+    ts(A("pi", 13), A("pi", 12), 3, an)
+    ts(col["x2"], col["a"], 2.0, O.mult, col["b0"], O.add)
+    run_max(0, A("uw", 0, 144), 0, 144)
+    halve("psa", C * hi[0], 0)
+    halve("psa", C * hi[0], 1)
+    dma("a", [(A("vb", C, J, p0=r, ps=16), A("dv")) for r in range(8, 16)])
+    halve("psa", C * hi[0], 2)
+    halve("psa", C * hi[0], 3)
+    early_constants(0)
+    for c in (128, 256, 512):
+        aff(io(c, min(2 * c, J)), io(0, min(c, J - c)), 1.0, float(c))
+    ts(col["x0"], A("pi", 13), 24.0, O.mult, col["x2"], O.add)
+    scan(A("wt", 8, 16), A("zc"), A("zz", 0, 8), O.mult, O.add, 0.5)
+    ts(cu["F"], A("zz", 0, 2), col["fb"], O.add)
+    listed(A("upk", 0, 9), 0, 0, 144)
+    tc(own_win(0, C * hi[0], C * hi[0] + C), ind(A("vb", 0, C), cu["unb"]))
+    ts(cu["kg"], io(0, 24, 8), col["x0"], O.add, col["hb96"], O.max)
+    ts(A("wt", 0, 8), A("wt", 8, 16), -1.0, O.mult)
+    ts(A("wt", 16, 24), io(1, 9), 256.0, O.mult)
+    tr(A("tt", 0, C), own_win(0, C * hi[0], C * hi[0] + C))
+    for k in range(3):
         ts(A("dz", 42 * k + 9, 42 * k + 41), io(0, 32), col["j32"], O.is_equal, -K, O.mult)
+    by_column()
+    quant(A("qu"), A("su"), A("ut"))
+    for k in range(3):
+        ms(A("s1", 384 * k + 80, 384 * k + 378, 9), 0.0)
     op("v", [A("qp")], [A("qu"), A("upk")], lambda: V.tensor_copy(T.qp[:, 0:144].bitcast(dt.uint32), T.qu[:, 0:128].bitcast(dt.uint32).indirect(T.upk[:, 0:9])))
     op("v", [A("sp")], [A("su"), A("upk")], lambda: V.tensor_copy(T.sp[:, 0:144], T.su[:, 0:128].indirect(T.upk[:, 0:9])))
     ms(A("yt", 4 * C, 1536), 0.0)
-    ts(A("uw", 288, 290), io(0, 2), col["e"], O.is_equal, BIG, O.mult)
-    tt(col["pw"], col["pq"], col["pe"], O.mult)
+    ts(A("me", 2, 4), io(0, 2), col["e"], O.is_equal, BIG, O.mult)
     ts(cu["q"], io(0, 16, 8), col["qh"], O.add, 10.0, O.min)
-    ts(A("me"), A("uw", 288, 290), -16.0, O.add)
-    ms(A("s1"), 0.0)
-    ms(A("ti"), 0.0)
-    aff(A("cb", 0, 22), io(0, C, 16), 1.0, col["q"])
-    aff(A("dz", 41, 126, 42), A("zz", 0, 3), 1.0, col["last"])
-    for k in range(3):
-        aff(A("wt", 32 * k, 32 * k + 8), A("w8", 0, 8), -1.0, 0.0)
-        aff(A("wt", 32 * k + 8, 32 * k + 16), A("w8", 0, 8), 1.0, 0.0)
-    by_column_2()
-    round_constants(0)
-    table()
-    for j in (8, 24):
-        aff(A("ti", j, J, 32), io(0, J, 32), 1.0, col["j32"])
-    tc(own_win(0, C - C * hi[0], J - C * hi[0]), ind(A("vb", C, J), cu["unb"]))
-    tc(A("ppf"), ind(own_win(0), A("la", 0, 22)))
-    share(0)
-    listed(A("ppf"), A("lb", 0, 22))
+    wait("s", ("sent", cnt["sent"], {}))
+    dma("s", [(cast(A("qw"), dt.uint8), ext(T.wc[:])), (A("sw"), ext(T.ws[:]))])
+    dma("s", [(A("vb", C * k, C * k + C, p0=r, ps=16), A("dv%d" % k)) for k in (2, 3) for r in range(16)] + [(A("vt"), ext(T.v[:]))])
+    ts(A("me", 0, 2), A("me", 2, 4), -16.0, O.add)
     unpack("psb", "lq0", "ls0")
-    for b in range(4):
-        halve("psb", C * (1 - hi[0]), b, "a" if b == 1 else "v")
-    for b in range(4):
-        first(0, b)
 
     for t in range(3):
-        o = 152 * t
-        down = (2, 1, 0)
-        for b in range(4):
-            tt(A("yt", b, 4 * C, 4), ind(A("fj", J * b, J * b + J), A("lb", 22 * t, 22 * t + 22)), A("ab", C * b, C * b + C), O.add)
-        pk = ind(A("pl"), cu["kg"])
-        tt(A("pw", 0, 48), pk, A("rc", o, o + 48), O.is_equal)
-        quant(A("qy"), A("sy"), A("yt"))
-        for k in down:
+        o, w = 168 * t, 24 * t
+        at = C * hi[t]
+
+        def gather(on, out, win, off):
+            (act if on == "a" else tc)(out, ind(win, off))
+
+        def swap(k, on="v"):
+            gather(on, own_win(t, at + CHUNK[k][0], at + CHUNK[k][1]), A("win", *WINDOW[t - 1]), lst("ix", 0, k))
+
+        def once(k):
+            run_max(0, own_win(t, at + CHUNK[k][0], at + CHUNK[k][1]), *CHUNK[k])
+
+        def once_list(k):
+            listed(lst("la", 22 * t, k), 0, *CHUNK[k])
+
+        def turn(k):
+            tr(A("tt", *CHUNK[k]), own_win(t, at + CHUNK[k][0], at + CHUNK[k][1]))
+
+        def twice(k, on="v"):
+            gather(on, A("ppf", *CHUNK[k]), own_win(t) if t else A("vb", 0, J), lst("la", 22 * t, k) if t else lst("ix", 0, k))
+
+        def twice_scan(k):
+            run_max(C, A("ppf", *CHUNK[k]), *CHUNK[k])
+
+        def twice_list(k):
+            listed(lst("lb", 22 * t, k), C, *CHUNK[k])
+
+        def first(k, bs=range(4)):
+            for b in bs:
+                act(A("ab", C * b + CHUNK[k][0], C * b + CHUNK[k][1]), ind(A("fj", J * b, J * b + J), lst("la", 22 * t, k)))
+
+        def blend(k, bs=range(4)):
+            for b in bs:
+                tt(A("yt", b + 4 * CHUNK[k][0], 4 * CHUNK[k][1], 4), ind(A("fj", J * b, J * b + J), lst("lb", 22 * t, k)),
+                   A("ab", C * b + CHUNK[k][0], C * b + CHUNK[k][1]), O.add)
+
+        def score(k):
+            quant(A("qy", 128 * k, 128 * k + 128), A("sy", 128 * k, 128 * k + 128), A("yt", 512 * k, 512 * k + 512))
             mm(A("psb", 512 * k, 512 * k + 144), A("qy", 128 * k, 128 * k + 128), A("sy", 128 * k, 128 * k + 128), A("qp"), A("sp"))
+
+        def right(k):
+            act(A("sr", 72 * k, 72 * k + 72), A("psb", 512 * k + 72, 512 * k + 144))
+
         bank = [3, 2, 1, 0]
 
         def layer(b):
@@ -399,64 +436,96 @@ def rank_program(g, core, T, topo):
                 tt(A("xn", b + 4 * c0, 4 * c1, 4), A("psa", 512 * b + c0, 512 * b + c1), A("rl", C * b + c0, C * b + c1), O.add)
             del left[:n]
 
-        layer(0)
+        pk = ind(A("pl"), cu["kg"])
+        z, s1, k32 = (lambda k, a, b: A("z", 42 * k + a, 42 * k + b)), (lambda k, a, b, st=1: A("s1", 384 * k + a, 384 * k + b, st)), (lambda n, k: A(n, 32 * k, 32 * k + 32))
+
+        def words(k):
+            aff(k32("rb", k), A("on"), A("so", 15 + 32 * k), A("rc", o + 96 + k))
+            aff(A("ow", k), z(k, 41, 42), 4096.0, A("so", 23 + 32 * k))
+            act(A("ow", 4 + k), z(k, 40, 41), AF.Relu, -BIG, TOP * BIG)
+            aff(A("ar2", 4 * k, 4 * k + 4), A("rc", o + 148, o + 152), 1.0, A("ow", k))
+            aff(A("ar2", 12 + 4 * k, 16 + 4 * k), A("rc", o + 152 + 4 * k, o + 156 + 4 * k), 1.0, A("ow", 4 + k))
+
+        steps = [
+            (lambda k: tt(A("fl", 72 * k, 72 * k + 72), A("psb", 512 * k, 512 * k + 72), A("sr", 72 * k, 72 * k + 72), O.is_ge),),
+            (lambda k: scan(s1(k, 0, 72), A("coef"), A("fl", 72 * k, 72 * k + 72), O.mult, O.add),),
+            (lambda k: tt(k32("f96", k), ind(s1(k, 0, 72), cu["F"]), A("c32"), O.is_ge),
+             lambda k: scan(z(k, 0, 42), A("dz", 42 * k, 42 * k + 42), s1(k, 8, 378, 9), O.add, O.max)),
+            (lambda k: tt(k32("fw", k), k32("f96", k), A("wt"), O.mult), lambda k: tr(k32("t96", k), z(k, 8, 40))),
+            (lambda k: scan(k32("so", k), A("rs"), k32("fw", k), O.mult, O.add),
+             words,
+             lambda k: ts(z(k, 8, 40), k32("t96", k), z(k, 40, 41), O.not_equal, BIG, O.mult)),
+            (lambda k: least(A("m3", k), z(k, 8, 42)),),
+            (lambda k: ts(A("lsc", 2 * k, 2 * k + 2), A("me", 0, 2), A("m3", k), O.min, col["r16"], O.add), lambda k: tr(k32("tbv", k), k32("rb", k))),
+            (lambda k: tc(ind(A("tb"), A("lsc", 2 * k, 2 * k + 2)), k32("tbv", k)),),
+        ]
+
+        def step(k, n):
+            if 0 <= n < len(steps):
+                for f in steps[n]:
+                    f(k)
+
+        if t:
+            swap(0, "a")
+            swap(2)
+            swap(1)
+            act(own_win(t, C - at, J - at), ind(A("win", *WINDOW[t - 1]), A("ix", 22, 44)))
+            once(2), turn(2), once(1), once(0), once_list(2), turn(1), once_list(1), once_list(0), turn(0)
+            first(2)
+            twice(0, "a")
+            twice(2)
+            by_column()
+            twice(1)
+            if t == 1:
+                share(1)
+            twice_scan(2), twice_scan(1), twice_list(2), twice_list(1)
+            first(1)
+            blend(2, [0])
+            twice_scan(0)
+            blend(2, [1])
+            twice_list(0)
+            blend(2, [2, 3])
+        else:
+            twice(2), twice(1), twice(0), twice_scan(2), twice_scan(1), twice_scan(0), twice_list(2), twice_list(1), twice_list(0)
+            halve("psb", C - at, 0)
+            halve("psb", C - at, 1, "v")
+            halve("psb", C - at, 2)
+            halve("psb", C - at, 3, "v")
+            first(2), first(1)
+            blend(2)
+        blend(1, [0])
+        score(2)
+        first(0)
+        right(2)
+        blend(1, [1, 2, 3])
+        blend(0, [0])
+        score(1)
+        right(1)
+        if t == 0:
+            table()
+            word_constants(0)
+        tt(A("pw", 0, 48), pk, A("rc", o, o + 48), O.is_equal)
+        blend(0, [1])
         tt(A("pw", 48, 96), A("pw", 0, 48), A("rc", o + 48, o + 96), O.mult)
-        for k in range(3):
-            aff(A("wt", 32 * k + 24, 32 * k + 32), A("pw", 16 * k, 16 * k + 8), BIG, A("rc", o + 100 + k))
+        blend(0, [2])
         tt(A("pw", 96, 144), pk, A("pw", 48, 96), O.add)
-        tt(A("pw", 144, 192), A("pw", 96, 144), A("zc"), O.add)
-        for k in down:
+        step(2, 0)
+        blend(0, [3])
+        for k in DOWN:
             tt(A("dz", 42 * k + 1, 42 * k + 9), A("pw", 96 + 16 * k, 104 + 16 * k), A("pw", 97 + 16 * k, 105 + 16 * k), O.subtract)
-        for k in down:
-            act(A("sr", 72 * k, 72 * k + 72), A("psb", 512 * k + 72, 512 * k + 144))
-            tt(A("fl", 72 * k, 72 * k + 72), A("psb", 512 * k, 512 * k + 72), A("sr", 72 * k, 72 * k + 72), O.is_ge)
-            if k < 2:
-                scan(A("s1", 378 * k + 378, 378 * k + 450), A("coef"), A("fl", 72 * k + 72, 72 * k + 144), O.mult, O.add)
-        for b in range(1, 4):
-            layer(b)
-        for k in range(3):
-            aff(A("wt", 32 * k + 16, 32 * k + 24), A("pw", 144 + 16 * k, 152 + 16 * k), 4096.0, 255.0 + 2.0 ** 22 * hi[t])
+        score(0)
+        right(0)
+        step(2, 1), step(1, 0)
+        layer(0), layer(1), layer(2)
         relu(0)
-
-        def asked(k):
-            scan(A("z", 42 * k, 42 * k + 42), A("dz", 42 * k, 42 * k + 42), A("s1", 378 * k + 8, 378 * k + 378, 9), O.add, O.max)
-
-        def turned(k):
-            tr(A("t96", 32 * k, 32 * k + 32), A("z", 42 * k + 8, 42 * k + 40))
-
-        def repeats(k):
-            ts(A("z", 42 * k + 8, 42 * k + 40), A("t96", 32 * k, 32 * k + 32), A("z", 42 * k + 40), O.not_equal, BIG, O.mult)
-
-        asked(2)
-        scan(A("s1", 0, 72), A("coef"), A("fl", 0, 72), O.mult, O.add)
-        asked(1)
-        turned(2)
-        tt(A("f96"), ind(A("s1"), cu["F"]), A("c96"), O.is_ge)
-        asked(0)
-        turned(1)
-        tt(A("fw"), A("f96"), A("wt"), O.mult)
-        repeats(2)
-        turned(0)
-        scan(A("so"), A("rs"), A("fw"), O.mult, O.add)
-        for k in down:
-            aff(A("rb", 32 * k, 32 * k + 32), A("on"), A("so", 15 + 32 * k), A("rc", o + 96 + k))
-        for k in range(3):
-            aff(A("ar2", 4 * k, 4 * k + 4), A("zo"), 1.0, A("so", 23 + 32 * k))
-            aff(A("ar2", 12 + 4 * k, 16 + 4 * k), A("zo"), 1.0, A("so", 31 + 32 * k))
+        for n in range(2, len(steps) + 4):
+            step(0, n - 4), step(2, n), step(1, n - 1)
+            if n == 4:
+                layer(3)
+            if n in (9, 10):
+                state()
         for b in range(1, 4):
             relu(b)
-        repeats(1)
-        repeats(0)
-        for k in down:
-            least(A("m3", k), A("z", 42 * k + 8, 42 * k + 42))
-        for k in down:
-            ts(A("lsc", 2 * k, 2 * k + 2), A("me"), A("m3", k), O.min, col["r16"], O.add)
-        for k in down:
-            tr(A("tbv", 32 * k, 32 * k + 32), A("rb", 32 * k, 32 * k + 32))
-        for k in down:
-            tc(ind(A("tb"), A("lsc", 2 * k, 2 * k + 2)), A("tbv", 32 * k, 32 * k + 32))
-            if k:
-                state()
         tt(A("b1", p1=64), A("ar2", p1=64), A("ar2", p0=64), O.min)
         tr(A("tt7"), A("tb", 32, 32 + J))
         for a in range(2):
@@ -465,7 +534,6 @@ def rank_program(g, core, T, topo):
         state()
         tt(A("a1", 0, 22, p1=64), A("ar", 0, 22, p1=64), A("ar", 0, 22, p0=64), O.min)
         state()
-        w = 24 * t
         for a in range(2):
             tt(A("wout", w, w + 22, p0=32 * a, p1=32 * a + 32), A("a1", 0, 22, p1=32), A("a1", 0, 22, p0=32, p1=64), O.min)
         state()
@@ -478,26 +546,29 @@ def rank_program(g, core, T, topo):
         tt(own, own, A("mg", 32, 43, p1=64), O.add)
         W = A("wout", w, w + 22)
         to = [STEP[t]] + ([STEP[t + 1], STEP[t] ^ STEP[t + 1]] if t < 2 else [])
-        lands = [A("wl", 24 * (3 * t + k), 24 * (3 * t + k) + 22) for k in range(len(to))]
-        deps("g", [], [W])
-        m = topo.mask(core, peer(to[0]))
-        for x in to:
-            m &= topo.mask(core, peer(x))
-        ids = [topo.addr(peer(x), core) for x in to]
-        g.remote_dma_fused([RemoteDMATransfer(dst_ids=[DstId(rid=r_, pnc=p_) for r_, p_ in ids], dma_engine_mask=m, remote_sem=T.sem["aw%d" % t],
-                                              srcs=[ap(W)], dsts=[ap(a) for a in lands])], local_sem=T.sem["sent"])
-        cnt["sent"] += bin(m).count("1")
-        arrive("aw%d" % t, bin(m).count("1") * len(to), lands)
+        spread(to, W, [A("wl", 24 * (3 * t + k), 24 * (3 * t + k) + 22) for k in range(len(to))], "aw%d" % t)
         state(8)
         qn, sn = "qx%d" % (t + 1), "sx%d" % (t + 1)
         quant(A(qn), A(sn), A("xn"))
+        if t == 0:
+            for a in range(4):
+                fill("cc", names.index("pq"), names.index("pq") + 1, 1, 2 ** (7 - 2 * a), 32 * a, 32 * a + 32)
+            aff(A("cb", 0, 22), io(0, C, 16), 1.0, col["q"])
+            for j in (8, 24):
+                aff(A("ti", j, J, 32), io(0, J, 32), 1.0, col["j32"])
+            tt(col["pw"], col["pq"], col["pe"], O.mult)
+        late_constants(t)
         if t < 2:
             send_x(t + 1)
+            if t == 0:
+                for k, to_ in enumerate((OWN[0] + C - at, NEXT[0] + at, NEXT[0] + C - at)):
+                    tc(A("win", to_, to_ + C), ind(A("vb", C * k + C, C * k + 2 * C), cu["unb"]))
             unpack("psa", qn, sn)
             table()
             for b in range(4):
                 halve("psa", C * hi[t + 1], b)
-            round_constants(t + 1)
+            early_constants(t + 1)
+            word_constants(t + 1)
         else:
             quant(A("qv"), A("sv"), A("vt"))
             mm(A("psa", 0, C), A("qv"), A("sv"), A(qn), A(sn))
@@ -506,9 +577,13 @@ def rank_program(g, core, T, topo):
             dma("a", [(ext(T.y[:]), A("yo"))])
         two = [("wout", w, "wl", 72 * t), ("wl", 72 * t + 24, "wl", 72 * t + 48) if t < 2 else ("wout", w, "wl", 72 * t)]
 
-        def lower(n, c0, c1, st, at, wide):
+        def lower(n, c0, c1, st, c, wide):
             for s, (n0, a0, n1, a1) in enumerate(two):
-                tt(A(n, c0, c1, st, 64 * s, 64 * s + 64), A(n0, a0 + at, a0 + at + wide, p1=64), A(n1, a1 + at, a1 + at + wide, p1=64), O.min)
+                tt(A(n, c0, c1, st, 64 * s, 64 * s + 64), A(n0, a0 + c, a0 + c + wide, p1=64), A(n1, a1 + c, a1 + c + wide, p1=64), O.min)
+
+        def split(n, win, l):
+            act(A(n, 192, C), ind(win, A(l, 12, 22)))
+            tc(A(n, 0, 192), ind(win, A(l, 0, 12)))
 
         lower("vi", 0, 11, 1, 11 * hi[t], 11)
         lower("ti", 0, J, 32, 0, 22)
@@ -517,12 +592,11 @@ def rank_program(g, core, T, topo):
         tr(A("wv", 0, C), A("ti", 0, C))
         tc(A("lq"), A("oi", 0, 22))
         tr(A("wv", C, J), A("ti", C, J))
-        split("gq", 0, A("wv"), "lq", 0)
-        at = C * hi[t + 1] if t < 2 else 0
+        split("gq", A("wv"), "lq")
         if t < 2:
             unpack("psb", "lq%d" % (t + 1), "ls%d" % (t + 1))
             for b in range(4):
-                halve("psb", C - at, b)
+                halve("psb", C - C * hi[t + 1], b)
         tr(A("tg"), A("gq"))
         d = 176 * t
         n = 44 if t < 2 else 22
@@ -544,21 +618,8 @@ def rank_program(g, core, T, topo):
         ts(A("dd", d + 1, d + 4 * n, 4), p[4], col["g1"], O.is_equal)
         scan(A("so2", 0, 4 * n), A("e0", d, d + 4 * n), A("dd", d, d + 4 * n), O.mult, O.add)
         tc(A("ix", 0, n), A("so2", 3, 4 * n, 4))
-        w0 = A("win", *WINDOW[t])
-        if t < 2:
-            split("win", OWN[t + 1] + at, w0, "ix", 0)
-            act(own_win(t + 1, C - at, J - at), ind(w0, A("ix", 22, 44)))
-            listed(own_win(t + 1, at, at + C), A("la", 22 * t + 22, 22 * t + 44))
-            split("ppf", 0, own_win(t + 1), "la", 22 * t + 22)
-            by_column_1(t + 1)
-            listed(A("ppf"), A("lb", 22 * t + 22, 22 * t + 44))
-            for b in range(4):
-                first(t + 1, b)
-            by_column_2()
-            if t == 0:
-                share(1)
-        else:
-            split("wov", 0, w0, "ix", 0)
-            dma("s", [(ext(T.ov[:]), A("wov", ps=16))])
+    act(A("wov", 192, C), ind(A("win", *WINDOW[2]), A("ix", 12, 22)))
+    tc(A("wov", 0, 192), ind(A("win", *WINDOW[2]), A("ix", 0, 12)))
+    dma("s", [(ext(T.ov[:]), A("wov", ps=16))])
     for s, n in cnt.items():
         g.wait_ge(T.sem[s], n)

@@ -17,14 +17,14 @@ SCRATCH = {
     "qv": sb(128, MX), "sv": sb(128, U8), "qw": sb(512, MX), "sw": sb(512, U8), "qe": sb(512, MX), "se": sb(512, U8),
     "psa": ("psum", [128, 2048], F32), "psb": ("psum", [128, 2048], F32),
     "pi": sb(16, I32), "cc": sb(48), "zz": sb(192), "upk": sb(10, U16), "uw": sb(432), "cu": sb(64, U16), "c16": sb(48), "ctrl": sb(C),
-    "coef": sb(72), "c32": sb(32), "wt": sb(32), "rs": sb(32), "on": sb(32), "zo": sb(8), "me": sb(4), "zc": sb(8),
+    "coef": sb(72), "c32": sb(32), "wt": sb(96), "rs": sb(32), "on": sb(32), "zo": sb(4), "me": sb(4), "zc": sb(24),
     "rc": sb(3 * 168), "cb": sb(72), "vgi": sb(22, I32), "vb": sb(2 * J, I32),
     "dv0": ("dram", [128, 22], I32), "dv": ("dram", [128, 22], I32), "dv2": ("dram", [128, 22], I32), "dv3": ("dram", [128, 22], I32),
     "win": sb(6 * J), "wov": sb(C),
     "la": sb(66, U16), "lb": sb(66, U16), "ppf": sb(C), "sc": sb(2 * C), "tt": sb(384), "pl": sb(104), "pw": sb(3 * 48),
     "sr": sb(216), "fl": sb(216), "s1": sb(3 * 384), "dz": sb(126), "z": sb(126), "f96": sb(96), "fw": sb(96), "so": sb(96), "t96": sb(96),
-    "m3": sb(4), "ow": sb(8), "lsc": sb(6, U16), "rb": sb(96), "tbv": sb(96),
-    "tb": sb(32 + J), "tt7": sb(J), "ar": sb(24), "a1": sb(24), "ar2": sb(24), "b1": sb(24), "b2": sb(24), "mg": sb(48), "wout": sb(3 * 24), "wl": sb(7 * 24),
+    "m3": sb(8), "lsc": sb(6, U16), "rb": sb(96), "tbv": sb(96),
+    "tb": sb(32 + J), "tt7": sb(96 * 23), "ar": sb(132), "a1": sb(24), "r6": sb(132), "wout": sb(3 * 24), "wl": sb(7 * 24),
     "vi": sb(16, I32), "ti": sb(J), "wv": sb(J), "oi": sb(32, I32), "lq": sb(22, U16), "gq": sb(C), "tg": sb(C),
     "dd": sb(3 * 176), "e0": sb(3 * 176), "so2": sb(176), "p7": sb(44 * 5, I32), "ix": sb(44, U16),
     "dsrc1": ("dram", [128, 44], F32), "dland1": ("dram", [128, 44], F32),
@@ -39,9 +39,11 @@ SEMAPHORES = ["sv", "sa", "sp", "sg", "sent", "av", "ad0", "ad1", "ad2", "aw0", 
 BIG = 2.0 ** 25
 K = 2048.0
 TOP = 7 * 4096 + 1.0
+LEVEL = 2.0 ** 21
 OWN, NEXT, NUM = [J, 3 * J, 5 * J], [0, 4 * J], 2 * J
 WINDOW = [(0, 3 * J), (2 * J, 5 * J), (2 * J, 6 * J)]
-CHUNK = [(0, 128), (128, 256), (256, C)]
+CHUNK = [(0, 128), (128, C)]
+UP = 1
 DOWN = (2, 1, 0)
 
 
@@ -171,7 +173,7 @@ def rank_program(g, core, T, topo):
         op("v", [o], [], lambda: V.memset(ap(o), v))
 
     def scan(o, a, b, f1, f2, init=0.0):
-        op("v", [o], [a, b], lambda: V.tensor_tensor_scan(ap(o), ap(a), ap(b), init, f1, f2))
+        op("v", [o], [a, b, init], lambda: V.tensor_tensor_scan(ap(o), ap(a), ap(b), ap(init), f1, f2))
 
     def least(o, i):
         op("v", [o], [i], lambda: V.tensor_reduce(ap(o), ap(i), AX.X, O.min))
@@ -230,8 +232,8 @@ def rank_program(g, core, T, topo):
         for b in range(4):
             mm(A(ps, 512 * b, 512 * b + C), A("qe", 128 * b, 128 * b + 128), A("se", 128 * b, 128 * b + 128), A(q), A(s))
 
-    def halve(ps, at, b, on="a"):
-        o, i = A("fj", J * b + at, J * b + at + C), A(ps, 512 * b, 512 * b + C)
+    def halve(ps, at, b, on="a", c0=0, c1=C):
+        o, i = A("fj", J * b + at + c0, J * b + at + c1), A(ps, 512 * b + c0, 512 * b + c1)
         if on == "a":
             act(o, i, scale=0.5)
         else:
@@ -251,21 +253,16 @@ def rank_program(g, core, T, topo):
     def early_constants(t):
         o = 168 * t
         aff(A("rc", o, o + 48), A("cb", 24, 72), 1.0, float(C * hi[t]))
+        aff(A("rc", o + 96, o + 99), A("cb", 24, 72, 16), 2048.0, 2048.0 * C * hi[t] + 255.0)
         fill("rc", o + 32, o + 48, 1, -1, 96, 128)
+        aff(A("rc", o + 100, o + 103), A("cb", 24, 72, 16), -2048.0, LEVEL - 2048.0 * C * hi[t])
+        aff(A("rc", o + 148, o + 151), A("cb", 24, 72, 16), 1.0, TOP + C * hi[t])
         aff(A("rc", o + 48, o + 96), A("rc", o, o + 48), -1.0, col["self"])
-
-    def word_constants(t):
-        o, pr = 168 * t, 2.0 ** 22 * hi[t]
-        aff(A("rc", o + 148, o + 152), A("zo", 4, 8), 1.0, 255.0 + pr)
-        aff(A("rc", o + 96, o + 99), A("rc", o, o + 48, 16), 4096.0, 255.0 + pr)
-        aff(A("rc", o + 100, o + 103), A("rc", o, o + 48, 16), 4096.0, pr)
-        for k in range(3):
-            aff(A("rc", o + 152 + 4 * k, o + 156 + 4 * k), A("zo", 0, 4), 1.0, A("rc", o + 100 + k))
 
     def late_constants(t):
         o, j0 = 168 * t, float(C * hi[t])
         fill("e0", 176 * t, 176 * t + 176, 1, 0)
-        aff(A("rc", o + 104, o + 148, 2), A("cb", 0, 22), 4096.0, 4096 * j0)
+        aff(A("rc", o + 104, o + 148, 2), A("cb", 0, 22), 2048.0, 2048 * j0)
         aff(A("rc", o + 105, o + 148, 2), A("cb", 0, 22), 1.0, j0)
         for s, base in enumerate([OWN[t]] + NEXT[t:t + 1]):
             at = 176 * t + 88 * s
@@ -273,7 +270,8 @@ def rank_program(g, core, T, topo):
             fill("e0", at + 2, at + 88, 4, NUM - base)
 
     def table():
-        aff(A("tb", 32, 32 + J), io(0, J), 4096.0, 2.0 ** 23)
+        aff(A("tb", 32, 32 + J), io(0, J), 2048.0, 3 * LEVEL)
+        fill("tt7", 16, 96 * 23, 96, BIG)
 
     def by_column():
         tc(A("pl", 0, 24), A("tt", 0, 384, 16))
@@ -297,15 +295,16 @@ def rank_program(g, core, T, topo):
     for k, (s_, m_) in enumerate([(0, 15), (0, 31), (4, 1), (4, 7), (3, 1), (0, 7), (5, 3), (1, 7), (0, 1), (1, 3)]):
         ts(A("pi", k + 1), A("pi", 0), s_, sh, m_, an)
     tc(A("cc", 0, 11), A("pi", 0, 11))
-    for n_, c0, c1, v in (("coef", 0, 72, 1), ("rs", 0, 32, 1), ("on", 0, 32, 1), ("zc", 0, 8, 2), ("c32", 0, 8, 4 * 4096), ("c32", 8, 32, 7 * 4096),
-                          ("tt", C, 384, -1), ("pl", 96, 104, -K), ("tb", 0, 32, 0), ("dz", 0, 126, 0), ("wout", 0, 72, 0), ("wt", 24, 32, 0)):
+    for n_, c0, c1, v in (("coef", 0, 72, 1), ("rs", 0, 32, 1), ("on", 0, 32, 2 * LEVEL), ("zc", 0, 8, 2), ("c32", 0, 8, 4 * 4096), ("c32", 8, 32, 7 * 4096),
+                          ("tt", C, 384, -1), ("pl", 96, 104, -K), ("tb", 0, 32, 0), ("dz", 0, 126, 0), ("wout", 0, 72, 0), ("r6", 0, 132, 0)):
         fill(n_, c0, c1, 1, v)
-    for n_, i_, s_, b_ in (("q22", "q", 22, 0), ("q1", "q", 1, 1), ("fb", "i8", 9, 8), ("pe", "e", -0.5, 1), ("g1", "g", 1, 1), ("r16", "q", 1, 16),
-                           ("self", "q", 1, -16), ("last", "q", -1, 16 - TOP), ("hb96", "hb", 96, 0), ("x3", "q", 4096, -16 * 4096)):
+    for n_, i_, s_, b_ in (("q22", "q", 22, 0), ("q1", "q", 1, 1), ("fb", "i8", 9, 8), ("pe", "e", -0.5, 1), ("g1", "g", 1, 8192), ("r16", "q", 1, 16),
+                           ("self", "q", 1, -16), ("last", "q", -1, 16 - TOP), ("hb96", "hb", 96, 0)):
         aff(col[n_], col[i_], float(s_), float(b_))
     for b in range(4):
         ts(A("et", 512 * b + b, 512 * b + 512, 4), io(0, 128), col["P"], O.is_equal)
-    for n_, c0, c1, st, v in (("coef", 0, 72, 9, 0), ("coef", 8, 72, 9, 4096), ("coef", 16, 57, 8, -1), ("rs", 0, 1, 1, 0), ("dz", 0, 126, 42, -BIG), ("coef", 8, 9, 1, -4096)):
+    for n_, c0, c1, st, v in (("coef", 0, 72, 9, 0), ("coef", 8, 72, 9, 4096), ("coef", 16, 57, 8, -1), ("dz", 0, 126, 42, -BIG), ("r6", 0, 132, 6, BIG),
+                              ("tt7", 32, 96 * 22, 96, BIG), ("tt7", 64, 96 * 22, 96, BIG), ("tt7", 80, 96 * 22, 96, BIG), ("coef", 8, 9, 1, -4096)):
         fill(n_, c0, c1, st, v)
     aff(A("coef", 1, 72, 9), io(0, 8), 1.0, -7.0)
     aff(A("dz", 41, 126, 42), A("zz", 0, 3), 1.0, col["last"])
@@ -338,7 +337,6 @@ def rank_program(g, core, T, topo):
     tt(A("uw", 72, 144), A("uw", 144, 216), A("uw", 360, 432), O.max)
     for k in range(3):
         ts(A("cb", 24 + 16 * k, 40 + 16 * k), A("zz", 0, 16), col["P"], O.add, 128.0 * k, O.add)
-    ts(A("zo", 4, 8), A("zo", 0, 4), col["x3"], O.add)
     ts(A("pi", 13), A("pi", 12), 3, an)
     ts(col["x2"], col["a"], 2.0, O.mult, col["b0"], O.add)
     run_max(0, A("uw", 0, 144), 0, 144)
@@ -351,13 +349,15 @@ def rank_program(g, core, T, topo):
     for c in (128, 256, 512):
         aff(io(c, min(2 * c, J)), io(0, min(c, J - c)), 1.0, float(c))
     ts(col["x0"], A("pi", 13), 24.0, O.mult, col["x2"], O.add)
-    scan(A("wt", 8, 16), A("zc"), A("zz", 0, 8), O.mult, O.add, 0.5)
+    scan(A("zc", 8, 16), A("zc", 0, 8), A("zz", 0, 8), O.mult, O.add, 0.5)
+    ts(A("zc", 16, 24), io(0, 8), 256.0, O.mult)
     ts(cu["F"], A("zz", 0, 2), col["fb"], O.add)
     listed(A("upk", 0, 9), 0, 0, 144)
     tc(own_win(0, C * hi[0], C * hi[0] + C), ind(A("vb", 0, C), cu["unb"]))
     ts(cu["kg"], io(0, 24, 8), col["x0"], O.add, col["hb96"], O.max)
-    ts(A("wt", 0, 8), A("wt", 8, 16), -1.0, O.mult)
-    ts(A("wt", 16, 24), io(1, 9), 256.0, O.mult)
+    for k in range(3):
+        ts(A("wt", 32 * k, 32 * k + 8), A("zc", 8, 16), -1.0, O.mult)
+        tt(A("wt", 32 * k + 8, 32 * k + 16), A("zc", 8, 16), A("zc", 16, 24), O.add)
     tr(A("tt", 0, C), own_win(0, C * hi[0], C * hi[0] + C))
     for k in range(3):
         ts(A("dz", 42 * k + 9, 42 * k + 41), io(0, 32), col["j32"], O.is_equal, -K, O.mult)
@@ -414,11 +414,11 @@ def rank_program(g, core, T, topo):
                    A("ab", C * b + CHUNK[k][0], C * b + CHUNK[k][1]), O.add)
 
         def score(k):
-            quant(A("qy", 128 * k, 128 * k + 128), A("sy", 128 * k, 128 * k + 128), A("yt", 512 * k, 512 * k + 512))
-            mm(A("psb", 512 * k, 512 * k + 144), A("qy", 128 * k, 128 * k + 128), A("sy", 128 * k, 128 * k + 128), A("qp"), A("sp"))
-
-        def right(k):
-            act(A("sr", 72 * k, 72 * k + 72), A("psb", 512 * k + 72, 512 * k + 144))
+            c0, c1 = (0, 128) if k == 0 else (128, 384)
+            quant(A("qy", c0, c1), A("sy", c0, c1), A("yt", 4 * c0, 4 * c1))
+            for j in range(c1 // 128 - 1, c0 // 128 - 1, -1):
+                mm(A("psb", 512 * j, 512 * j + 144), A("qy", 128 * j, 128 * j + 128), A("sy", 128 * j, 128 * j + 128), A("qp"), A("sp"))
+                act(A("sr", 72 * j, 72 * j + 72), A("psb", 512 * j + 72, 512 * j + 144))
 
         bank = [3, 2, 1, 0]
 
@@ -440,19 +440,18 @@ def rank_program(g, core, T, topo):
         z, s1, k32 = (lambda k, a, b: A("z", 42 * k + a, 42 * k + b)), (lambda k, a, b, st=1: A("s1", 384 * k + a, 384 * k + b, st)), (lambda n, k: A(n, 32 * k, 32 * k + 32))
 
         def words(k):
-            aff(k32("rb", k), A("on"), A("so", 15 + 32 * k), A("rc", o + 96 + k))
-            aff(A("ow", k), z(k, 41, 42), 4096.0, A("so", 23 + 32 * k))
-            act(A("ow", 4 + k), z(k, 40, 41), AF.Relu, -BIG, TOP * BIG)
-            aff(A("ar2", 4 * k, 4 * k + 4), A("rc", o + 148, o + 152), 1.0, A("ow", k))
-            aff(A("ar2", 12 + 4 * k, 16 + 4 * k), A("rc", o + 152 + 4 * k, o + 156 + 4 * k), 1.0, A("ow", 4 + k))
+            aff(k32("rb", k), A("on"), A("m3", 4 + k), A("so", 15 + 32 * k))
+            c = 96 * (11 * hi[t] + 4 * k) + 16
+            aff(A("tt7", c, c + 289, 96), A("zo"), 1.0, A("so", 31 + 32 * k))
 
         steps = [
             (lambda k: tt(A("fl", 72 * k, 72 * k + 72), A("psb", 512 * k, 512 * k + 72), A("sr", 72 * k, 72 * k + 72), O.is_ge),),
             (lambda k: scan(s1(k, 0, 72), A("coef"), A("fl", 72 * k, 72 * k + 72), O.mult, O.add),),
             (lambda k: tt(k32("f96", k), ind(s1(k, 0, 72), cu["F"]), A("c32"), O.is_ge),
              lambda k: scan(z(k, 0, 42), A("dz", 42 * k, 42 * k + 42), s1(k, 8, 378, 9), O.add, O.max)),
-            (lambda k: tt(k32("fw", k), k32("f96", k), A("wt"), O.mult), lambda k: tr(k32("t96", k), z(k, 8, 40))),
-            (lambda k: scan(k32("so", k), A("rs"), k32("fw", k), O.mult, O.add),
+            (lambda k: tt(k32("fw", k), k32("f96", k), k32("wt", k), O.mult), lambda k: tr(k32("t96", k), z(k, 8, 40)),
+             lambda k: ts(A("m3", 4 + k), z(k, 40, 41), A("rc", o + 148 + k), O.is_lt)),
+            (lambda k: scan(k32("so", k), A("rs"), k32("fw", k), O.mult, O.add, A("rc", o + 96 + k)),
              words,
              lambda k: ts(z(k, 8, 40), k32("t96", k), z(k, 40, 41), O.not_equal, BIG, O.mult)),
             (lambda k: least(A("m3", k), z(k, 8, 42)),),
@@ -467,83 +466,59 @@ def rank_program(g, core, T, topo):
 
         if t:
             swap(0, "a")
-            swap(2)
-            swap(1)
+            swap(UP)
             act(own_win(t, C - at, J - at), ind(A("win", *WINDOW[t - 1]), A("ix", 22, 44)))
-            once(2), turn(2), once(1), once(0), once_list(2), turn(1), once_list(1), once_list(0), turn(0)
-            first(2)
+            once(0), once(UP), turn(0), once_list(0), once_list(UP), turn(UP)
             twice(0, "a")
-            twice(2)
+            twice(UP)
             by_column()
-            twice(1)
             if t == 1:
                 share(1)
-            twice_scan(2), twice_scan(1), twice_list(2), twice_list(1)
-            first(1)
-            blend(2, [0])
-            twice_scan(0)
-            blend(2, [1])
-            twice_list(0)
-            blend(2, [2, 3])
+            twice_scan(0), twice_scan(UP), twice_list(0), twice_list(UP)
         else:
-            twice(2), twice(1), twice(0), twice_scan(2), twice_scan(1), twice_scan(0), twice_list(2), twice_list(1), twice_list(0)
+            twice(0), twice(UP), twice_scan(0), twice_scan(UP), twice_list(0), twice_list(UP)
             halve("psb", C - at, 0)
             halve("psb", C - at, 1, "v")
             halve("psb", C - at, 2)
             halve("psb", C - at, 3, "v")
-            first(2), first(1)
-            blend(2)
-        blend(1, [0])
-        score(2)
-        first(0)
-        right(2)
-        blend(1, [1, 2, 3])
-        blend(0, [0])
-        score(1)
-        right(1)
+        first(0, [0]), first(UP), first(0, [1, 2, 3])
         if t == 0:
             table()
-            word_constants(0)
+        blend(0, [0]), blend(UP), blend(0, [1])
+        score(UP)
         tt(A("pw", 0, 48), pk, A("rc", o, o + 48), O.is_equal)
-        blend(0, [1])
-        tt(A("pw", 48, 96), A("pw", 0, 48), A("rc", o + 48, o + 96), O.mult)
-        blend(0, [2])
-        tt(A("pw", 96, 144), pk, A("pw", 48, 96), O.add)
-        step(2, 0)
-        blend(0, [3])
         for k in DOWN:
-            tt(A("dz", 42 * k + 1, 42 * k + 9), A("pw", 96 + 16 * k, 104 + 16 * k), A("pw", 97 + 16 * k, 105 + 16 * k), O.subtract)
+            aff(A("wt", 32 * k + 24, 32 * k + 32), A("pw", 16 * k, 16 * k + 8), BIG, 0.0)
+        blend(0, [2])
+        tt(A("pw", 48, 96), A("pw", 0, 48), A("rc", o + 48, o + 96), O.mult)
+        blend(0, [3])
+        tt(A("pw", 96, 144), pk, A("pw", 48, 96), O.add)
+        for k in DOWN:
+            aff(A("wt", 32 * k + 16, 32 * k + 24), A("pw", 96 + 16 * k, 104 + 16 * k), 2048.0, A("rc", o + 100 + k))
         score(0)
-        right(0)
-        step(2, 1), step(1, 0)
-        layer(0), layer(1), layer(2)
-        relu(0)
-        for n in range(2, len(steps) + 4):
-            step(0, n - 4), step(2, n), step(1, n - 1)
-            if n == 4:
+        layer(0)
+        for n in range(len(steps) + 3):
+            step(0, n - 3), step(2, n), step(1, n if n < 7 else n - 1 if n == 8 else -1)
+            if n == 0:
+                for k in DOWN:
+                    tt(A("dz", 42 * k + 1, 42 * k + 9), A("pw", 96 + 16 * k, 104 + 16 * k), A("pw", 97 + 16 * k, 105 + 16 * k), O.subtract)
+                layer(1), layer(2)
+                relu(0)
+            if n == 3:
                 layer(3)
-            if n in (9, 10):
+            if n == 9:
                 state()
         for b in range(1, 4):
             relu(b)
-        tt(A("b1", p1=64), A("ar2", p1=64), A("ar2", p0=64), O.min)
-        tr(A("tt7"), A("tb", 32, 32 + J))
-        for a in range(2):
-            tt(A("b2", p0=32 * a, p1=32 * a + 32), A("b1", p1=32), A("b1", p0=32, p1=64), O.min)
-        tt(A("ar", 0, 22), A("tt7", 0, J, 32), A("tt7", 16, J, 32), O.min)
         state()
-        tt(A("a1", 0, 22, p1=64), A("ar", 0, 22, p1=64), A("ar", 0, 22, p0=64), O.min)
+        tr(A("tt7", 0, 3 * J, 3), A("tb", 32, 32 + J))
+        state()
+        scan(A("ar"), A("r6"), A("tt7", 0, 3 * J, 16), O.add, O.min)
+        state()
+        tt(A("a1", 0, 22, p1=64), A("ar", 5, 132, 6, p1=64), A("ar", 5, 132, 6, p0=64), O.min)
         state()
         for a in range(2):
             tt(A("wout", w, w + 22, p0=32 * a, p1=32 * a + 32), A("a1", 0, 22, p1=32), A("a1", 0, 22, p0=32, p1=64), O.min)
-        state()
-        own = A("wout", w + 11 * hi[t], w + 11 * hi[t] + 11, p1=64)
-        tt(A("mg", 0, 11, p1=64), A("b2", 12, 23, p1=64), own, O.is_lt)
-        tt(A("mg", 16, 27, p1=64), A("b2", 0, 11, p1=64), own, O.subtract)
-        state()
-        tt(A("mg", 32, 43, p1=64), A("mg", 0, 11, p1=64), A("mg", 16, 27, p1=64), O.mult)
-        state()
-        tt(own, own, A("mg", 32, 43, p1=64), O.add)
         W = A("wout", w, w + 22)
         to = [STEP[t]] + ([STEP[t + 1], STEP[t] ^ STEP[t + 1]] if t < 2 else [])
         spread(to, W, [A("wl", 24 * (3 * t + k), 24 * (3 * t + k) + 22) for k in range(len(to))], "aw%d" % t)
@@ -568,7 +543,6 @@ def rank_program(g, core, T, topo):
             for b in range(4):
                 halve("psa", C * hi[t + 1], b)
             early_constants(t + 1)
-            word_constants(t + 1)
         else:
             quant(A("qv"), A("sv"), A("vt"))
             mm(A("psa", 0, C), A("qv"), A("sv"), A(qn), A(sn))
@@ -588,15 +562,20 @@ def rank_program(g, core, T, topo):
         lower("vi", 0, 11, 1, 11 * hi[t], 11)
         lower("ti", 0, J, 32, 0, 22)
         lower("ti", 16, J, 32, 0, 22)
-        ts(A("oi"), ind(A("vi", 0, 11), cu["q"]), 12, sh, 1023, an)
+        ts(A("oi"), ind(A("vi", 0, 11), cu["q"]), 11, sh, 1023, an)
         tr(A("wv", 0, C), A("ti", 0, C))
         tc(A("lq"), A("oi", 0, 22))
         tr(A("wv", C, J), A("ti", C, J))
         split("gq", A("wv"), "lq")
         if t < 2:
             unpack("psb", "lq%d" % (t + 1), "ls%d" % (t + 1))
-            for b in range(4):
+            for b in range(3):
                 halve("psb", C - C * hi[t + 1], b)
+
+        def piece(h):
+            if t < 2:
+                halve("psb", C - C * hi[t + 1], 3, "v", C // 2 * h, C // 2 * h + C // 2)
+
         tr(A("tg"), A("gq"))
         d = 176 * t
         n = 44 if t < 2 else 22
@@ -612,12 +591,14 @@ def rank_program(g, core, T, topo):
         ts(p[0], D, col["pw"], O.mult)
         tc(p[1], D)
         ts(p[2], p[0], 7, sh, 1, an)
-        ts(p[3], p[1], 12, sh, 1023, an)
+        ts(p[3], p[1], 11, sh, 1023, an)
         ts(p[4], p[1], 8, sh, 16383, an)
         tt(A("e0", d + 3, d + 4 * n, 4), p[2], p[3], O.is_gt)
         ts(A("dd", d + 1, d + 4 * n, 4), p[4], col["g1"], O.is_equal)
         scan(A("so2", 0, 4 * n), A("e0", d, d + 4 * n), A("dd", d, d + 4 * n), O.mult, O.add)
+        piece(0)
         tc(A("ix", 0, n), A("so2", 3, 4 * n, 4))
+        piece(1)
     act(A("wov", 192, C), ind(A("win", *WINDOW[2]), A("ix", 12, 22)))
     tc(A("wov", 0, 192), ind(A("win", *WINDOW[2]), A("ix", 0, 12)))
     dma("s", [(ext(T.ov[:]), A("wov", ps=16))])

@@ -12,22 +12,23 @@ def sb(n, t=F32):
 
 SCRATCH = {
     "xt": sb(4 * C, BF), "xn": sb(4 * C, BF), "yt": sb(1536, BF), "fj": sb(4 * J, BF), "ab": sb(4 * C, BF), "rl": sb(4 * C),
-    "ut": sb(512, BF), "vt": sb(512, BF), "et": sb(2048, BF), "yo": sb(C),
+    "ut": sb(512, BF), "vt": sb(512, BF), "et": sb(1032, BF), "yo": sb(C),
     "qy": sb(384, MX), "sy": sb(384, U8), "qu": sb(128, MX), "su": sb(128, U8), "qp": sb(144, MX), "sp": sb(144, U8),
     "qv": sb(128, MX), "sv": sb(128, U8), "qw": sb(512, MX), "sw": sb(512, U8), "qe": sb(512, MX), "se": sb(512, U8),
     "psa": ("psum", [128, 2048], F32), "psb": ("psum", [128, 2048], F32),
-    "pi": sb(16, I32), "cc": sb(48), "zz": sb(192), "upk": sb(10, U16), "uw": sb(432), "cu": sb(64, U16), "c16": sb(48), "ctrl": sb(C),
+    "pi": sb(16, I32), "cc": sb(24), "zz": sb(192), "upk": sb(10, U16), "uw": sb(432), "cu": sb(64, U16), "c16": sb(48), "ctrl": sb(C),
     "coef": sb(72), "c32": sb(32), "wt": sb(96), "rs": sb(32), "on": sb(32), "zo": sb(4), "me": sb(4), "zc": sb(24),
-    "rc": sb(3 * 168), "cb": sb(72), "vgi": sb(22, I32), "vb": sb(2 * J, I32),
-    "dv0": ("dram", [128, 22], I32), "dv": ("dram", [128, 22], I32), "dv2": ("dram", [128, 22], I32), "dv3": ("dram", [128, 22], I32),
+    "rc": sb(3 * 152), "cb": sb(56), "kr": sb(128), "vgi": sb(22, I32), "vgf": sb(22), "vb": sb(J, I32), "vc": sb(J),
+    "dv0": ("dram", [128, 22], I32), "dv": ("dram", [128, 22], I32),
+    "dv1": ("dram", [128, 22], F32), "dv2": ("dram", [128, 22], F32), "dv3": ("dram", [128, 22], F32),
     "win": sb(6 * J), "wov": sb(C),
-    "la": sb(66, U16), "lb": sb(66, U16), "ppf": sb(C), "sc": sb(2 * C), "tt": sb(384), "pl": sb(104), "pw": sb(3 * 48),
+    "la": sb(66, U16), "lb": sb(66, U16), "ppf": sb(C), "sc": sb(2 * C), "tt": sb(384), "pl": sb(104), "pw": sb(96),
     "sr": sb(216), "fl": sb(216), "s1": sb(3 * 384), "dz": sb(126), "z": sb(126), "f96": sb(96), "fw": sb(96), "so": sb(96), "t96": sb(96),
     "m3": sb(8), "lsc": sb(6, U16), "rb": sb(96), "tbv": sb(96),
     "tb": sb(32 + J), "tt7": sb(96 * 23), "ar": sb(132), "a1": sb(24), "r6": sb(132), "wout": sb(3 * 24), "wl": sb(7 * 24),
     "vi": sb(16, I32), "ti": sb(J), "wv": sb(J), "oi": sb(32, I32), "lq": sb(22, U16), "gq": sb(C), "tg": sb(C),
-    "dd": sb(3 * 176), "e0": sb(3 * 176), "so2": sb(176), "p7": sb(44 * 5, I32), "ix": sb(44, U16),
-    "dsrc1": ("dram", [128, 44], F32), "dland1": ("dram", [128, 44], F32),
+    "dd": sb(3 * 440, I32), "e0": sb(3 * 220, I32), "so2": sb(220), "p7": sb(44 * 5, I32), "ix": sb(44, U16),
+    "dsrc": ("dram", [128, 44], F32), "dland": ("dram", [128, 44], F32),
 }
 for _t in range(4):
     SCRATCH["qx%d" % _t] = sb(C, MX)
@@ -35,8 +36,9 @@ for _t in range(4):
 for _t in range(3):
     SCRATCH["lq%d" % _t] = sb(C, MX)
     SCRATCH["ls%d" % _t] = sb(C, U8)
-SEMAPHORES = ["sv", "sa", "sp", "sg", "sent", "av", "ad0", "ad1", "ad2", "aw0", "aw1", "aw2", "af0", "af1"] + ["d%d" % _t for _t in range(24)]
+SEMAPHORES = ["sv", "sa", "sp", "sg", "sent", "gone", "av", "au", "ad0", "ad1", "ad2", "aw0", "aw1", "aw2", "ax0", "ax1", "af"] + ["d%d" % _t for _t in range(24)]
 BIG = 2.0 ** 25
+FAR = 2 ** 24 - 1
 K = 2048.0
 TOP = 7 * 4096 + 1.0
 LEVEL = 2.0 ** 21
@@ -144,15 +146,15 @@ def rank_program(g, core, T, topo):
         cnt["sent"] = cnt.get("sent", 0) + bin(m).count("1")
         return bin(m).count("1")
 
-    def spread(to, i, lands, sem):
+    def spread(to, i, lands, sem, left="sent"):
         deps("g", [], [i])
         m = topo.mask(core, peer(to[0]))
         for x in to:
             m &= topo.mask(core, peer(x))
         ids = [topo.addr(peer(x), core) for x in to]
         g.remote_dma_fused([RemoteDMATransfer(dst_ids=[DstId(rid=r_, pnc=p_) for r_, p_ in ids], dma_engine_mask=m, remote_sem=T.sem[sem],
-                                              srcs=[ap(i)], dsts=[ap(a) for a in lands])], local_sem=T.sem["sent"])
-        cnt["sent"] = cnt.get("sent", 0) + bin(m).count("1")
+                                              srcs=[ap(i)], dsts=[ap(a) for a in lands])], local_sem=T.sem[left])
+        cnt[left] = cnt.get(left, 0) + bin(m).count("1")
         arrive(sem, bin(m).count("1") * len(to), lands)
 
     V = g.vector
@@ -208,10 +210,9 @@ def rank_program(g, core, T, topo):
             op("g", [o], [], lambda: g.iota(ap(o), pat, base, cm))
 
     hi = [1 if rank & s else 0 for s in STEP]
-    names = ["P", "q", "j32", "e", "g", "hb", "i8", "a", "qh", "b0", "a2", "g1", "q1", "corr", "pw", "fb", "pq", "pe", "q22",
-             "r16", "self", "last", "hb96", "x0", "x1", "x2", "x3"]
+    names = ["P", "q", "j32", "e", "g", "i8", "a", "qh", "g1", "q1", "corr", "pw", "fb", "pq", "pe", "q22", "r16", "self", "last"]
     col = {n: A("cc", k) for k, n in enumerate(names)}
-    cu = {"unb": A("cu", 0, 22), "m16": A("cu", 22, 44), "F": A("cu", 44, 46), "kg": A("cu", 50, 53), "q": A("cu", 54, 56)}
+    cu = {"unb": A("cu", 0, 22), "m16": A("cu", 22, 44), "F": A("cu", 44, 46), "kg": A("cu", 50, 52), "q": A("cu", 54, 56)}
     sh, an = O.arith_shift_right, O.bitwise_and
 
     def io(a, b, st=1):
@@ -245,29 +246,32 @@ def rank_program(g, core, T, topo):
     def listed(dst, at, c0, c1):
         ts(dst, A("sc", at + c0 + 15, at + c1, 16), col["corr"], O.subtract)
 
-    def share(t):
-        dma("s", [(A("dsrc%d" % t), own_win(t, ps=16))])
-        arrive("af%d" % t, send(STEP[t + 1], A("dland%d" % t), A("dsrc%d" % t), "af%d" % t), [A("dland%d" % t)])
-        dma("s", [(A("win", NEXT[t], NEXT[t] + J, p0=r, ps=16), A("dland%d" % t)) for r in range(16)])
+    def share():
+        dma("s", [(A("dsrc"), own_win(1, ps=16))])
+        arrive("af", send(STEP[2], A("dland"), A("dsrc"), "af"), [A("dland")])
+        dma("s", [(A("win", NEXT[1], NEXT[1] + J, p0=r, ps=16), A("dland")) for r in range(16)])
 
     def early_constants(t):
-        o = 168 * t
-        aff(A("rc", o, o + 48), A("cb", 24, 72), 1.0, float(C * hi[t]))
-        aff(A("rc", o + 96, o + 99), A("cb", 24, 72, 16), 2048.0, 2048.0 * C * hi[t] + 255.0)
-        fill("rc", o + 32, o + 48, 1, -1, 96, 128)
-        aff(A("rc", o + 100, o + 103), A("cb", 24, 72, 16), -2048.0, LEVEL - 2048.0 * C * hi[t])
-        aff(A("rc", o + 148, o + 151), A("cb", 24, 72, 16), 1.0, TOP + C * hi[t])
-        aff(A("rc", o + 48, o + 96), A("rc", o, o + 48), -1.0, col["self"])
+        o, j0 = 152 * t, float(C * hi[t])
+        aff(A("rc", o, o + 32), A("cb", 24, 56), 1.0, j0)
+        aff(A("rc", o + 96, o + 99), A("cb", 24, 27), 2048.0, 2048.0 * j0 + 255.0 + LEVEL)
+        fill("rc", o + 2, o + 24, 3, -1, 96, 128)
+        aff(A("rc", o + 100, o + 103), A("cb", 24, 27), -2048.0, -2048.0 * j0)
+        aff(A("rc", o + 148, o + 151), A("cb", 24, 27), 1.0, TOP + j0)
+        aff(A("rc", o + 48, o + 80), A("rc", o, o + 32), -1.0, col["self"])
 
     def late_constants(t):
-        o, j0 = 168 * t, float(C * hi[t])
-        fill("e0", 176 * t, 176 * t + 176, 1, 0)
+        o, j0 = 152 * t, float(C * hi[t])
         aff(A("rc", o + 104, o + 148, 2), A("cb", 0, 22), 2048.0, 2048 * j0)
         aff(A("rc", o + 105, o + 148, 2), A("cb", 0, 22), 1.0, j0)
         for s, base in enumerate([OWN[t]] + NEXT[t:t + 1]):
-            at = 176 * t + 88 * s
-            aff(A("dd", at + 3, at + 88, 4), A("cb", 0, 22), 1.0, j0 + base - WINDOW[t][0])
-            fill("e0", at + 2, at + 88, 4, NUM - base)
+            ts(A("dd", 440 * t + 220 * s + 9, 440 * t + 220 * s + 220, 10), A("cb", 0, 22), j0 + base - WINDOW[t][0], O.add)
+
+    def scan_constants(t):
+        iota(A("e0", 220 * t, 220 * t + 220), [[0, 220]], 0, 0, False)
+        iota(A("dd", 440 * t + 1, 440 * t + 440, 2), [[0, 220]], 0, 0, False)
+        for s, base in enumerate([OWN[t]] + NEXT[t:t + 1]):
+            iota(A("e0", 220 * t + 110 * s + 2, 220 * t + 110 * s + 110, 5), [[0, 22]], NUM - base, 0, False)
 
     def table():
         aff(A("tb", 32, 32 + J), io(0, J), 2048.0, 3 * LEVEL)
@@ -287,58 +291,64 @@ def rank_program(g, core, T, topo):
     iota(io(0, 128), [[1, 128]], 0, 0)
     iota(A("uw", 144, 216), [[16, 8], [0, 9]], 0, 0)
     iota(A("uw", 216, 288), [[16, 8], [16, 9]], 0, 0)
-    spread([STEP[0], STEP[1], STEP[0] ^ STEP[1]], A("dv0"), [A("dv"), A("dv2"), A("dv3")], "av")
+    spread([STEP[0]], A("dv0"), [A("dv")], "av")
     dma("s", [(A("vb", C, J, p0=r, ps=16), A("dv")) for r in range(8)])
 
     ms(A("zz"), 0.0)
     ms(A("et"), 0.0)
-    for k, (s_, m_) in enumerate([(0, 15), (0, 31), (4, 1), (4, 7), (3, 1), (0, 7), (5, 3), (1, 7), (0, 1), (1, 3)]):
+    for k, (s_, m_) in enumerate([(0, 15), (0, 31), (4, 1), (4, 7), (0, 7), (5, 3), (1, 7)]):
         ts(A("pi", k + 1), A("pi", 0), s_, sh, m_, an)
-    tc(A("cc", 0, 11), A("pi", 0, 11))
-    for n_, c0, c1, v in (("coef", 0, 72, 1), ("rs", 0, 32, 1), ("on", 0, 32, 2 * LEVEL), ("zc", 0, 8, 2), ("c32", 0, 8, 4 * 4096), ("c32", 8, 32, 7 * 4096),
-                          ("tt", C, 384, -1), ("pl", 96, 104, -K), ("tb", 0, 32, 0), ("dz", 0, 126, 0), ("wout", 0, 72, 0), ("r6", 0, 132, 0)):
+    tc(A("cc", 0, 8), A("pi", 0, 8))
+    for n_, c0, c1, v in (("coef", 0, 72, 1), ("rs", 0, 32, 1), ("on", 0, 32, LEVEL), ("zc", 0, 8, 2), ("c32", 0, 8, 4 * 4096), ("c32", 8, 32, 7 * 4096),
+                          ("tt", C, 384, -1), ("pl", 96, 104, -K), ("dz", 0, 3, -BIG), ("kr", 120, 128, 96)):
         fill(n_, c0, c1, 1, v)
+    for c0, c1, st, v in ((0, 72, 9, 0), (8, 72, 9, 4096), (16, 57, 8, -1)):
+        fill("coef", c0, c1, st, v)
     for n_, i_, s_, b_ in (("q22", "q", 22, 0), ("q1", "q", 1, 1), ("fb", "i8", 9, 8), ("pe", "e", -0.5, 1), ("g1", "g", 1, 8192), ("r16", "q", 1, 16),
-                           ("self", "q", 1, -16), ("last", "q", -1, 16 - TOP), ("hb96", "hb", 96, 0)):
+                           ("self", "q", 1, -16), ("last", "q", -1, 16 - TOP)):
         aff(col[n_], col[i_], float(s_), float(b_))
-    for b in range(4):
-        ts(A("et", 512 * b + b, 512 * b + 512, 4), io(0, 128), col["P"], O.is_equal)
-    for n_, c0, c1, st, v in (("coef", 0, 72, 9, 0), ("coef", 8, 72, 9, 4096), ("coef", 16, 57, 8, -1), ("dz", 0, 126, 42, -BIG), ("r6", 0, 132, 6, BIG),
-                              ("tt7", 32, 96 * 22, 96, BIG), ("tt7", 64, 96 * 22, 96, BIG), ("tt7", 80, 96 * 22, 96, BIG), ("coef", 8, 9, 1, -4096)):
-        fill(n_, c0, c1, st, v)
+    fill("coef", 8, 9, 1, -4096)
     aff(A("coef", 1, 72, 9), io(0, 8), 1.0, -7.0)
-    aff(A("dz", 41, 126, 42), A("zz", 0, 3), 1.0, col["last"])
-    pv = [A("p7", 44 * k + c, 44 * k + c + 22) for k in range(3) for c in (0, 22)]
+    for k in range(3):
+        aff(A("cb", 24 + k, 56, 3), A("on", 0, len(range(k, 32, 3))), 128.0 * k / LEVEL, col["P"])
+    aff(A("dz", 123, 126), A("zz", 0, 3), 1.0, col["last"])
+    for e in range(2):
+        ts(A("et", 516 * e + 2 + e, 516 * e + 514, 4), io(0, 128), col["P"], O.is_equal)
     tc(A("la", 0, 22), A("vgi"))
-    ts(pv[0], A("vgi"), 15, an)
-    ts(pv[1], A("vgi"), 4, sh)
-    ts(pv[2], A("vgi"), float(C), O.is_ge, -374.0 if hi[0] else 330.0, O.mult)
-    quant(A("qe"), A("se"), A("et"))
-    ts(pv[3], pv[0], 22.0, O.mult, float(C * hi[0]), O.add)
-    tt(pv[4], pv[1], pv[2], O.add)
-    ts(A("uw", 288, 360), A("uw", 216, 288), 128.0, O.is_ge, 128.0, O.mult)
-    ts(col["corr"], col["q"], 15.0, O.is_lt, 4096.0, O.mult)
-    tt(pv[5], pv[3], pv[4], O.add)
     ts(A("c16", 0, 16), io(0, 16), col["q"], O.is_equal, -2.0 ** 20, O.mult)
     ts(A("c16", 16, 32), io(0, 16), col["q1"], O.is_equal, 4096.0, O.mult)
+    for b in range(4):
+        c = 516 * (b % 2) + 2 - b // 2 * 2
+        quant(A("qe", 128 * b, 128 * b + 128), A("se", 128 * b, 128 * b + 128), A("et", c, c + 512))
     ts(cu["m16"], A("zz", 0, 22), col["q"], O.add)
-    tc(A("ix", 0, 22), pv[5])
     tt(A("c16", 32, 48), A("c16", 0, 16), A("c16", 16, 32), O.add)
     quant(A("qx0"), A("sx0"), A("xt"))
     send_x(0)
-    iota(A("ti"), [[0, J]], 0, 0)
+    left_x = cnt["sent"]
+    iota(A("kr", 0, 24), [[1, 4], [0, 6]], 4, 0)
+    iota(A("kr", 32, 56), [[0, 4], [1, 2], [8, 3]], 0, 0)
+    iota(io(128, J), [[1, J - 128]], 128, 0)
+    iota(A("yt", 4 * C, 1536), [[0, 128]], 0, 0)
+    for k in range(3):
+        iota(A("s1", 384 * k + 80, 384 * k + 378, 9), [[0, 34]], 0, 0)
     unpack("psa", "qx0", "sx0")
     act(A("ctrl"), ind(A("c16", 32, 48), cu["m16"]))
-    tt(A("uw", 360, 432), A("uw", 216, 288), A("uw", 288, 360), O.subtract)
+    pv = [A("p7", 44 * k + c, 44 * k + c + 22) for k in range(3) for c in (0, 22)]
+    ts(pv[0], A("vgi"), 15, an)
+    ts(pv[1], A("vgi"), 4, sh)
+    ts(pv[2], A("vgi"), float(C), O.is_ge, -374.0 if hi[0] else 330.0, O.mult)
+    ts(A("uw", 288, 360), A("uw", 216, 288), 128.0, O.is_ge, 128.0, O.mult)
     ts(cu["unb"], io(0, 22), col["q22"], O.add)
-    ts(A("zo", 0, 4), io(0, 4), col["a"], O.not_equal, BIG, O.mult)
-    ts(A("pi", 12), col["a2"], col["a"], O.subtract, 4.0, O.add)
+    ts(pv[3], pv[0], 22.0, O.mult, float(C * hi[0]), O.add)
+    tt(pv[4], pv[1], pv[2], O.add)
+    tt(A("uw", 360, 432), A("uw", 216, 288), A("uw", 288, 360), O.subtract)
+    ts(col["corr"], col["q"], 15.0, O.is_lt, 4096.0, O.mult)
+    tc(A("vgf"), A("vgi"))
+    tt(pv[5], pv[3], pv[4], O.add)
     tt(A("uw", 0, 72), A("uw", 144, 216), A("uw", 360, 432), O.min)
     tt(A("uw", 72, 144), A("uw", 144, 216), A("uw", 360, 432), O.max)
-    for k in range(3):
-        ts(A("cb", 24 + 16 * k, 40 + 16 * k), A("zz", 0, 16), col["P"], O.add, 128.0 * k, O.add)
-    ts(A("pi", 13), A("pi", 12), 3, an)
-    ts(col["x2"], col["a"], 2.0, O.mult, col["b0"], O.add)
+    tc(A("ix", 0, 22), pv[5])
+    tc(own_win(0, C * hi[0], C * hi[0] + C), ind(A("vb", 0, C), cu["unb"]))
     run_max(0, A("uw", 0, 144), 0, 144)
     halve("psa", C * hi[0], 0)
     halve("psa", C * hi[0], 1)
@@ -346,38 +356,46 @@ def rank_program(g, core, T, topo):
     halve("psa", C * hi[0], 2)
     halve("psa", C * hi[0], 3)
     early_constants(0)
-    for c in (128, 256, 512):
-        aff(io(c, min(2 * c, J)), io(0, min(c, J - c)), 1.0, float(c))
-    ts(col["x0"], A("pi", 13), 24.0, O.mult, col["x2"], O.add)
     scan(A("zc", 8, 16), A("zc", 0, 8), A("zz", 0, 8), O.mult, O.add, 0.5)
     ts(A("zc", 16, 24), io(0, 8), 256.0, O.mult)
-    ts(cu["F"], A("zz", 0, 2), col["fb"], O.add)
-    listed(A("upk", 0, 9), 0, 0, 144)
-    tc(own_win(0, C * hi[0], C * hi[0] + C), ind(A("vb", 0, C), cu["unb"]))
-    ts(cu["kg"], io(0, 24, 8), col["x0"], O.add, col["hb96"], O.max)
-    for k in range(3):
-        ts(A("wt", 32 * k, 32 * k + 8), A("zc", 8, 16), -1.0, O.mult)
-        tt(A("wt", 32 * k + 8, 32 * k + 16), A("zc", 8, 16), A("zc", 16, 24), O.add)
     tr(A("tt", 0, C), own_win(0, C * hi[0], C * hi[0] + C))
-    for k in range(3):
-        ts(A("dz", 42 * k + 9, 42 * k + 41), io(0, 32), col["j32"], O.is_equal, -K, O.mult)
+    listed(A("upk", 0, 9), 0, 0, 144)
+    ts(A("oi", 0, 24), A("kr", 0, 24), col["a"], O.subtract)
+    ts(A("kr", 64, 88), A("kr", 32, 56), col["a"], O.add, col["a"], O.add)
     by_column()
+    dma("s", [(A("dv1"), A("vgf"))])
+    spread([STEP[1], STEP[0] ^ STEP[1]], A("dv1"), [A("dv2"), A("dv3")], "au", "gone")
     quant(A("qu"), A("su"), A("ut"))
-    for k in range(3):
-        ms(A("s1", 384 * k + 80, 384 * k + 378, 9), 0.0)
+    ts(A("p7", 176, 200), A("oi", 0, 24), 3, an)
+    tt(A("wt", 8, 16), A("zc", 8, 16), A("zc", 16, 24), O.add)
+    ts(A("dz", 27, 123, 3), io(0, 32), col["j32"], O.is_equal, -K, O.mult)
+    ts(cu["F"], A("zz", 0, 2), col["fb"], O.add)
+    ts(A("kr", 0, 24), A("p7", 176, 200), 24.0, O.mult)
     op("v", [A("qp")], [A("qu"), A("upk")], lambda: V.tensor_copy(T.qp[:, 0:144].bitcast(dt.uint32), T.qu[:, 0:128].bitcast(dt.uint32).indirect(T.upk[:, 0:9])))
-    op("v", [A("sp")], [A("su"), A("upk")], lambda: V.tensor_copy(T.sp[:, 0:144], T.su[:, 0:128].indirect(T.upk[:, 0:9])))
-    ms(A("yt", 4 * C, 1536), 0.0)
+    op("a", [A("sp")], [A("su"), A("upk")], lambda: g.scalar.activation(T.sp[:, 0:144], T.su[:, 0:128].indirect(T.upk[:, 0:9]), AF.Copy))
+    tt(A("kr", 96, 120), A("kr", 0, 24), A("kr", 64, 88), O.add)
     ts(A("me", 2, 4), io(0, 2), col["e"], O.is_equal, BIG, O.mult)
+    ts(A("zo", 0, 4), io(0, 4), col["a"], O.not_equal, BIG, O.mult)
     ts(cu["q"], io(0, 16, 8), col["qh"], O.add, 10.0, O.min)
-    wait("s", ("sent", cnt["sent"], {}))
-    dma("s", [(cast(A("qw"), dt.uint8), ext(T.wc[:])), (A("sw"), ext(T.ws[:]))])
-    dma("s", [(A("vb", C * k, C * k + C, p0=r, ps=16), A("dv%d" % k)) for k in (2, 3) for r in range(16)] + [(A("vt"), ext(T.v[:]))])
+    run_max(0, A("kr", 96, 128), 0, 32)
     ts(A("me", 0, 2), A("me", 2, 4), -16.0, O.add)
+    wait("s", ("sent", left_x, {}))
+    dma("s", [(cast(A("qw"), dt.uint8), ext(T.wc[:])), (A("sw"), ext(T.ws[:]))])
+    dma("s", [(A("vc", C * k, C * k + C, p0=r, ps=16), A("dv%d" % (k + 2))) for k in (0, 1) for r in range(16)] + [(A("vt"), ext(T.v[:]))])
+    listed(cu["kg"], 0, 0, 32)
+    for n_, c0, c1, st, v in (("tb", 0, 32, 1, 0), ("r6", 0, 132, 1, 0), ("r6", 0, 132, 6, FAR), ("tt7", 32, 96 * 22, 96, FAR), ("tt7", 64, 96 * 22, 96, FAR),
+                              ("tt7", 80, 96 * 22, 96, FAR), ("wout", 0, 72, 1, 0), ("ti", 0, J, 1, 0)):
+        iota(A(n_, c0, c1, st), [[0, len(range(c0, c1, st))]], v, 0)
+    scan_constants(0)
+    for k in range(3):
+        aff(A("wt", 32 * k, 32 * k + 8), A("zc", 8, 16), -1.0, 0.0)
+    for k in (1, 2):
+        act(A("dz", 27 + k, 123, 3), A("dz", 27, 123, 3))
+        act(A("wt", 32 * k + 8, 32 * k + 16), A("wt", 8, 16))
     unpack("psb", "lq0", "ls0")
 
     for t in range(3):
-        o, w = 168 * t, 24 * t
+        o, w = 152 * t, 24 * t
         at = C * hi[t]
 
         def gather(on, out, win, off):
@@ -396,7 +414,7 @@ def rank_program(g, core, T, topo):
             tr(A("tt", *CHUNK[k]), own_win(t, at + CHUNK[k][0], at + CHUNK[k][1]))
 
         def twice(k, on="v"):
-            gather(on, A("ppf", *CHUNK[k]), own_win(t) if t else A("vb", 0, J), lst("la", 22 * t, k) if t else lst("ix", 0, k))
+            gather(on, A("ppf", *CHUNK[k]), own_win(t) if t else A("vb"), lst("la", 22 * t, k) if t else lst("ix", 0, k))
 
         def twice_scan(k):
             run_max(C, A("ppf", *CHUNK[k]), *CHUNK[k])
@@ -414,9 +432,9 @@ def rank_program(g, core, T, topo):
                    A("ab", C * b + CHUNK[k][0], C * b + CHUNK[k][1]), O.add)
 
         def score(k):
-            c0, c1 = (0, 128) if k == 0 else (128, 384)
+            c0, c1 = (0, 128) if k == 0 else (128, C if t else 384)
             quant(A("qy", c0, c1), A("sy", c0, c1), A("yt", 4 * c0, 4 * c1))
-            for j in range(c1 // 128 - 1, c0 // 128 - 1, -1):
+            for j in (2, 1) if k else (0,):
                 mm(A("psb", 512 * j, 512 * j + 144), A("qy", 128 * j, 128 * j + 128), A("sy", 128 * j, 128 * j + 128), A("qp"), A("sp"))
                 act(A("sr", 72 * j, 72 * j + 72), A("psb", 512 * j + 72, 512 * j + 144))
 
@@ -428,13 +446,15 @@ def rank_program(g, core, T, topo):
         def relu(b):
             act(A("rl", C * b, C * b + C), A("psb", 512 * bank[b], 512 * bank[b] + C), AF.Relu, scale=0.03125)
 
-        left = [(b, h) for b in range(4) for h in range(2)]
+        done = [0]
 
-        def state(n=1):
-            for b, h in left[:n]:
-                c0, c1 = C // 2 * h, C // 2 * h + C // 2
+        def state(n=C // 4):
+            end = min(done[0] + n, 4 * C)
+            while done[0] < end:
+                b, c0 = divmod(done[0], C)
+                c1 = min(C, c0 + end - done[0])
                 tt(A("xn", b + 4 * c0, 4 * c1, 4), A("psa", 512 * b + c0, 512 * b + c1), A("rl", C * b + c0, C * b + c1), O.add)
-            del left[:n]
+                done[0] += c1 - c0
 
         pk = ind(A("pl"), cu["kg"])
         z, s1, k32 = (lambda k, a, b: A("z", 42 * k + a, 42 * k + b)), (lambda k, a, b, st=1: A("s1", 384 * k + a, 384 * k + b, st)), (lambda n, k: A(n, 32 * k, 32 * k + 32))
@@ -448,11 +468,10 @@ def rank_program(g, core, T, topo):
             (lambda k: tt(A("fl", 72 * k, 72 * k + 72), A("psb", 512 * k, 512 * k + 72), A("sr", 72 * k, 72 * k + 72), O.is_ge),),
             (lambda k: scan(s1(k, 0, 72), A("coef"), A("fl", 72 * k, 72 * k + 72), O.mult, O.add),),
             (lambda k: tt(k32("f96", k), ind(s1(k, 0, 72), cu["F"]), A("c32"), O.is_ge),
-             lambda k: scan(z(k, 0, 42), A("dz", 42 * k, 42 * k + 42), s1(k, 8, 378, 9), O.add, O.max)),
+             lambda k: scan(z(k, 0, 42), A("dz", k, 126, 3), s1(k, 8, 378, 9), O.add, O.max)),
             (lambda k: tt(k32("fw", k), k32("f96", k), k32("wt", k), O.mult), lambda k: tr(k32("t96", k), z(k, 8, 40)),
-             lambda k: ts(A("m3", 4 + k), z(k, 40, 41), A("rc", o + 148 + k), O.is_lt)),
-            (lambda k: scan(k32("so", k), A("rs"), k32("fw", k), O.mult, O.add, A("rc", o + 96 + k)),
-             words,
+             lambda k: act(A("m3", 4 + k), z(k, 40, 41), AF.Sign, -1.0, A("rc", o + 148 + k))),
+            (lambda k: scan(k32("so", k), A("rs"), k32("fw", k), O.mult, O.add, A("rc", o + 96 + k)), words,
              lambda k: ts(z(k, 8, 40), k32("t96", k), z(k, 40, 41), O.not_equal, BIG, O.mult)),
             (lambda k: least(A("m3", k), z(k, 8, 42)),),
             (lambda k: ts(A("lsc", 2 * k, 2 * k + 2), A("me", 0, 2), A("m3", k), O.min, col["r16"], O.add), lambda k: tr(k32("tbv", k), k32("rb", k))),
@@ -473,7 +492,7 @@ def rank_program(g, core, T, topo):
             twice(UP)
             by_column()
             if t == 1:
-                share(1)
+                share()
             twice_scan(0), twice_scan(UP), twice_list(0), twice_list(UP)
         else:
             twice(0), twice(UP), twice_scan(0), twice_scan(UP), twice_list(0), twice_list(UP)
@@ -486,22 +505,21 @@ def rank_program(g, core, T, topo):
             table()
         blend(0, [0]), blend(UP), blend(0, [1])
         score(UP)
-        tt(A("pw", 0, 48), pk, A("rc", o, o + 48), O.is_equal)
+        tt(A("pw", 0, 32), pk, A("rc", o, o + 32), O.is_equal)
         for k in DOWN:
-            aff(A("wt", 32 * k + 24, 32 * k + 32), A("pw", 16 * k, 16 * k + 8), BIG, 0.0)
+            aff(A("wt", 32 * k + 24, 32 * k + 32), A("pw", k, 24, 3), BIG, 0.0)
         blend(0, [2])
-        tt(A("pw", 48, 96), A("pw", 0, 48), A("rc", o + 48, o + 96), O.mult)
+        tt(A("pw", 32, 64), A("pw", 0, 32), A("rc", o + 48, o + 80), O.mult)
         blend(0, [3])
-        tt(A("pw", 96, 144), pk, A("pw", 48, 96), O.add)
+        tt(A("pw", 64, 96), pk, A("pw", 32, 64), O.add)
         for k in DOWN:
-            aff(A("wt", 32 * k + 16, 32 * k + 24), A("pw", 96 + 16 * k, 104 + 16 * k), 2048.0, A("rc", o + 100 + k))
+            aff(A("wt", 32 * k + 16, 32 * k + 24), A("pw", 64 + k, 88, 3), 2048.0, A("rc", o + 100 + k))
         score(0)
         layer(0)
         for n in range(len(steps) + 3):
             step(0, n - 3), step(2, n), step(1, n if n < 7 else n - 1 if n == 8 else -1)
             if n == 0:
-                for k in DOWN:
-                    tt(A("dz", 42 * k + 1, 42 * k + 9), A("pw", 96 + 16 * k, 104 + 16 * k), A("pw", 97 + 16 * k, 105 + 16 * k), O.subtract)
+                tt(A("dz", 3, 27), A("pw", 64, 88), A("pw", 67, 91), O.subtract)
                 layer(1), layer(2)
                 relu(0)
             if n == 3:
@@ -520,9 +538,10 @@ def rank_program(g, core, T, topo):
         for a in range(2):
             tt(A("wout", w, w + 22, p0=32 * a, p1=32 * a + 32), A("a1", 0, 22, p1=32), A("a1", 0, 22, p0=32, p1=64), O.min)
         W = A("wout", w, w + 22)
-        to = [STEP[t]] + ([STEP[t + 1], STEP[t] ^ STEP[t + 1]] if t < 2 else [])
-        spread(to, W, [A("wl", 24 * (3 * t + k), 24 * (3 * t + k) + 22) for k in range(len(to))], "aw%d" % t)
-        state(8)
+        spread([STEP[t]], W, [A("wl", 72 * t, 72 * t + 22)], "aw%d" % t)
+        if t < 2:
+            spread([STEP[t + 1], STEP[t] ^ STEP[t + 1]], W, [A("wl", 72 * t + 24 * k, 72 * t + 24 * k + 22) for k in (1, 2)], "ax%d" % t)
+        state(4 * C)
         qn, sn = "qx%d" % (t + 1), "sx%d" % (t + 1)
         quant(A(qn), A(sn), A("xn"))
         if t == 0:
@@ -535,9 +554,11 @@ def rank_program(g, core, T, topo):
         late_constants(t)
         if t < 2:
             send_x(t + 1)
+            scan_constants(t + 1)
             if t == 0:
-                for k, to_ in enumerate((OWN[0] + C - at, NEXT[0] + at, NEXT[0] + C - at)):
-                    tc(A("win", to_, to_ + C), ind(A("vb", C * k + C, C * k + 2 * C), cu["unb"]))
+                tc(own_win(0, C - at, J - at), ind(A("vb", C, J), cu["unb"]))
+                tc(A("win", NEXT[0] + at, NEXT[0] + at + C), ind(A("vc", 0, C), cu["unb"]))
+                act(A("win", NEXT[0] + C - at, NEXT[0] + J - at), ind(A("vc", C, J), cu["unb"]))
             unpack("psa", qn, sn)
             table()
             for b in range(4):
@@ -549,24 +570,16 @@ def rank_program(g, core, T, topo):
             dma("s", [(ext(T.oc[:]), cast(A(qn), dt.uint8))] + [(ext(T.osc[4 * k:4 * k + 4, :]), A(sn, p0=32 * k, p1=32 * k + 4)) for k in range(4)])
             act(A("yo"), A("psa", 0, C))
             dma("a", [(ext(T.y[:]), A("yo"))])
-        two = [("wout", w, "wl", 72 * t), ("wl", 72 * t + 24, "wl", 72 * t + 48) if t < 2 else ("wout", w, "wl", 72 * t)]
-
-        def lower(n, c0, c1, st, c, wide):
-            for s, (n0, a0, n1, a1) in enumerate(two):
-                tt(A(n, c0, c1, st, 64 * s, 64 * s + 64), A(n0, a0 + c, a0 + c + wide, p1=64), A(n1, a1 + c, a1 + c + wide, p1=64), O.min)
-
-        def split(n, win, l):
-            act(A(n, 192, C), ind(win, A(l, 12, 22)))
-            tc(A(n, 0, 192), ind(win, A(l, 0, 12)))
-
-        lower("vi", 0, 11, 1, 11 * hi[t], 11)
-        lower("ti", 0, J, 32, 0, 22)
-        lower("ti", 16, J, 32, 0, 22)
+        two = [("wout", w, 72 * t), ("wl", 72 * t + 24, 72 * t + 48) if t < 2 else ("wout", w, 72 * t)]
+        for s, (n0, a0, a1) in enumerate(two):
+            for n_, c0, c1, st, c, wide in (("vi", 0, 11, 1, 11 * hi[t], 11), ("ti", 0, J, 32, 0, 22), ("ti", 16, J, 32, 0, 22)):
+                tt(A(n_, c0, c1, st, 64 * s, 64 * s + 64), A(n0, a0 + c, a0 + c + wide, p1=64), A("wl", a1 + c, a1 + c + wide, p1=64), O.min)
         ts(A("oi"), ind(A("vi", 0, 11), cu["q"]), 11, sh, 1023, an)
         tr(A("wv", 0, C), A("ti", 0, C))
         tc(A("lq"), A("oi", 0, 22))
         tr(A("wv", C, J), A("ti", C, J))
-        split("gq", A("wv"), "lq")
+        gather("a", A("gq", 192, C), A("wv"), A("lq", 12, 22))
+        gather("v", A("gq", 0, 192), A("wv"), A("lq", 0, 12))
         if t < 2:
             unpack("psb", "lq%d" % (t + 1), "ls%d" % (t + 1))
             for b in range(3):
@@ -577,27 +590,26 @@ def rank_program(g, core, T, topo):
                 halve("psb", C - C * hi[t + 1], 3, "v", C // 2 * h, C // 2 * h + C // 2)
 
         tr(A("tg"), A("gq"))
-        d = 176 * t
+        d, e = 440 * t, 220 * t
         n = 44 if t < 2 else 22
         cn = [o + 104, o + 148, 1]
         if t < 2:
             for s in range(2):
                 for h in range(2):
-                    tt(A("dd", d + 88 * s, d + 88 * s + 88, 2, 64 * h, 64 * h + 64), A("tg", 0, C, 8, 64 * s, 64 * s + 64), A("rc", *cn, 64 * s, 64 * s + 64), O.subtract)
+                    tt(A("dd", d + 220 * s, d + 220 * s + 220, 5, 64 * h, 64 * h + 64), A("tg", 0, C, 8, 64 * s, 64 * s + 64), A("rc", *cn, 64 * s, 64 * s + 64), O.subtract)
         else:
-            tt(A("dd", d, d + 88, 2), A("tg", 0, C, 8), A("rc", *cn), O.subtract)
-        D = A("dd", d, d + 4 * n, 4)
-        p = [A("p7", 44 * k, 44 * k + n) for k in range(5)]
+            tt(A("dd", d, d + 220, 5), A("tg", 0, C, 8), A("rc", *cn), O.subtract)
+        D = A("dd", d, d + 10 * n, 10)
+        p = [A("p7", 44 * k, 44 * k + n) for k in range(3)]
         ts(p[0], D, col["pw"], O.mult)
-        tc(p[1], D)
-        ts(p[2], p[0], 7, sh, 1, an)
-        ts(p[3], p[1], 11, sh, 1023, an)
-        ts(p[4], p[1], 8, sh, 16383, an)
-        tt(A("e0", d + 3, d + 4 * n, 4), p[2], p[3], O.is_gt)
-        ts(A("dd", d + 1, d + 4 * n, 4), p[4], col["g1"], O.is_equal)
-        scan(A("so2", 0, 4 * n), A("e0", d, d + 4 * n), A("dd", d, d + 4 * n), O.mult, O.add)
+        ts(p[1], D, 11, sh, 1023, an)
+        ts(p[2], D, 8, sh, 16383, an)
+        ts(A("e0", e + 3, e + 5 * n, 5), p[0], 7, sh, 1, an)
+        ts(A("e0", e + 4, e + 5 * n, 5), p[1], 0.0, O.is_equal)
+        ts(A("dd", d + 3, d + 10 * n, 10), p[2], col["g1"], O.is_equal)
+        scan(A("so2", 0, 5 * n), A("e0", e, e + 5 * n), A("dd", d + 1, d + 10 * n, 2), O.mult, O.add)
         piece(0)
-        tc(A("ix", 0, n), A("so2", 3, 4 * n, 4))
+        tc(A("ix", 0, n), A("so2", 4, 5 * n, 5))
         piece(1)
     act(A("wov", 192, C), ind(A("win", *WINDOW[2]), A("ix", 12, 22)))
     tc(A("wov", 0, 192), ind(A("win", *WINDOW[2]), A("ix", 0, 12)))

from concourse.bass import DstId, RemoteDMATransfer
from concourse.mybir import dt, AluOpType as O, ActivationFunctionType as AF, AxisListType as AX

C, J = 352, 704
STEP = [4, 2, 1]
F32, BF, I32, U16, MX, U8 = "float32", "bfloat16", "int32", "uint16", "float8_e4m3fn_x4", "uint8"


def sb(n, t=F32):
    return ("sbuf", [128, n], t)


SCRATCH = {
    "xt": sb(4 * C, BF), "xn": sb(4 * C, BF), "yt": sb(1536, BF), "fj": sb(4 * J, BF), "ab": sb(4 * C, BF), "rl": sb(4 * C),
    "ut": sb(512, BF), "vt": sb(512, BF), "et": sb(1032, BF), "yo": sb(C),
    "qy": sb(384, MX), "sy": sb(384, U8), "qu": sb(128, MX), "su": sb(128, U8), "qp": sb(144, MX), "sp": sb(144, U8),
    "qv": sb(128, MX), "sv": sb(128, U8), "qw": sb(512, MX), "sw": sb(512, U8), "qe": sb(512, MX), "se": sb(512, U8),
    "psa": ("psum", [128, 2048], F32), "psb": ("psum", [128, 2048], F32),
    "pi": sb(16, I32), "cc": sb(24), "zz": sb(192), "upk": sb(10, U16), "uw": sb(432), "cu": sb(64, U16), "c16": sb(48), "ctrl": sb(C),
    "coef": sb(72), "c32": sb(32), "wt": sb(96), "rs": sb(32), "on": sb(32), "zo": sb(4), "me": sb(4), "zc": sb(24),
    "rc": sb(3 * 152), "cb": sb(56), "kr": sb(128), "vgi": sb(22, I32), "vgf": sb(22), "vb": sb(J, I32), "vc": sb(J),
    "dv0": ("dram", [128, 22], I32), "dv": ("dram", [128, 22], I32),
    "dv1": ("dram", [128, 22], F32), "dv2": ("dram", [128, 22], F32), "dv3": ("dram", [128, 22], F32),
    "win": sb(6 * J), "wov": sb(C),
    "la": sb(66, U16), "lb": sb(66, U16), "ppf": sb(C), "sc": sb(2 * C), "tt": sb(384), "pl": sb(104), "pw": sb(96),
    "sr": sb(216), "fl": sb(216), "s1": sb(3 * 384), "dz": sb(126), "z": sb(126), "f96": sb(96), "fw": sb(96), "so": sb(96), "t96": sb(96),
    "m3": sb(8), "lsc": sb(6, U16), "rb": sb(96), "tbv": sb(96),
    "tb": sb(32 + J), "tt7": sb(96 * 23), "ar": sb(132), "a1": sb(24), "r6": sb(132), "wout": sb(3 * 24), "wl": sb(7 * 24),
    "vi": sb(16, I32), "ti": sb(J), "wv": sb(J), "oi": sb(32, I32), "lq": sb(22, U16), "gq": sb(C), "tg": sb(C),
    "dd": sb(3 * 440, I32), "e0": sb(3 * 220, I32), "so2": sb(220), "p7": sb(44 * 5, I32), "ix": sb(44, U16),
    "dsrc": ("dram", [128, 44], F32), "dland": ("dram", [128, 44], F32),
}
for _t in range(4):
    SCRATCH["qx%d" % _t] = sb(C, MX)
    SCRATCH["sx%d" % _t] = sb(C, U8)
for _t in range(3):
    SCRATCH["lq%d" % _t] = sb(C, MX)
    SCRATCH["ls%d" % _t] = sb(C, U8)
SEMAPHORES = ["sv", "sa", "sp", "sg", "sent", "gone", "av", "au", "ad0", "ad1", "ad2", "aw0", "aw1", "aw2", "ax0", "ax1", "af"] + ["d%d" % _t for _t in range(24)]
BIG = 2.0 ** 25
FAR = 2 ** 24 - 1
K = 2048.0
TOP = 7 * 4096 + 1.0
LEVEL = 2.0 ** 21
OWN, NEXT, NUM = [J, 3 * J, 5 * J], [0, 4 * J], 2 * J
WINDOW = [(0, 3 * J), (2 * J, 5 * J), (2 * J, 6 * J)]
CHUNK = [(0, 128), (128, C)]
UP = 1
DOWN = (2, 1, 0)


def rank_program(g, core, T, topo):
    rank = T.rank_of(core)
    if rank is None:
        return
    eng = {"v": g.vector, "a": g.scalar, "p": g.tensor, "g": g, "s": g.sync}
    qsem = {"v": "sv", "a": "sa", "p": "sp", "g": "sg"}
    cnt = {}
    know = {k: {} for k in eng}
    log = {}
    nd = [0]

    def A(n, c0=None, c1=None, st=1, p0=0, p1=128, ps=1):
        w = SCRATCH[n][1][1]
        c0, c1 = (0, w) if c0 is None else (c0, c0 + 1 if c1 is None else c1)
        ap = T[n][slice(p0, p1, ps) if ps > 1 else slice(p0, p1), slice(c0, c1, st) if st > 1 else slice(c0, c1)]
        if SCRATCH[n][0] == "psum":
            return {"ap": ap, "r": [(n, 0, 128, c0 // 512 * 512, c0 // 512 * 512 + 512, 1, 1)], "x": True}
        return {"ap": ap, "r": [(n, p0, p1, c0, c1, st, ps)]}

    def ind(w, o):
        return {"ap": w["ap"].indirect(o["ap"]), "r": w["r"] + o["r"], "w": w["r"], "o": o["r"]}

    def cast(a, d):
        return {"ap": a["ap"].bitcast(d), "r": a["r"]}

    def ext(ap):
        return {"ap": ap, "r": []}

    def meet(a, b):
        if a[1] >= b[2] or b[1] >= a[2] or a[3] >= b[4] or b[3] >= a[4]:
            return False
        return not any(a[s] == b[s] and a[s] > 1 and (a[c] - b[c]) % a[s] for s, c in ((5, 3), (6, 1)))

    def wait(q, ev):
        if know[q].get(ev[0], 0) < ev[1]:
            eng[q].wait_ge(T.sem[ev[0]], ev[1])
            for k, v in list(ev[2].items()) + [(ev[0], ev[1])]:
                know[q][k] = max(know[q].get(k, 0), v)

    def deps(q, outs, ins):
        touch = []
        for a in outs:
            touch += [(r, "w") for r in a.get("w", a["r"])] + [(r, "r") for r in a.get("o", [])]
        for a in ins:
            if isinstance(a, dict):
                touch += [(r, "x" if a.get("x") else "r") for r in a["r"]]
        need = {}
        for r, k in touch:
            for (r2, k2, ev) in log.get(r[0], []):
                clash = k == "w" or k2 == "w" or (k == "x" and ev[0] != qsem.get(q))
                if clash and meet(r, r2) and need.get(ev[0], (0, 0))[1] < ev[1]:
                    need[ev[0]] = ev
        for ev in sorted(need.values(), key=lambda e: -len(e[2])):
            wait(q, ev)
        return touch

    def note(touch, ev):
        for r, k in touch:
            log.setdefault(r[0], []).append((r, k, ev))

    def ap(a):
        return a["ap"] if isinstance(a, dict) else a

    def op(q, outs, ins, f):
        touch = deps(q, outs, ins)
        s = qsem[q]
        if q == "g":
            wait(q, (s, cnt.get(s, 0), {}))
        cnt[s] = cnt.get(s, 0) + 1
        f().then_inc(T.sem[s], 1)
        note(touch, (s, cnt[s], dict(know[q])))

    def dma(q, pairs):
        s = "d%d" % nd[0]
        nd[0] += 1
        touch = [deps(q, [o], [i]) for o, i in pairs]
        for o, i in pairs:
            eng[q].dma_start(ap(o), ap(i)).then_inc(T.sem[s], 16)
        cnt[s] = 16 * len(pairs)
        for x in touch:
            note(x, (s, cnt[s], dict(know[q])))

    def arrive(sem, n, lands):
        cnt[sem] = n
        note([(r, "w") for a in lands for r in a["r"]], (sem, n, {}))

    def peer(x):
        return T.cores[rank ^ x]

    def send(x, o, i, sem):
        deps("g", [], [i])
        m = topo.mask(core, peer(x))
        rid, pid = topo.addr(peer(x), core)
        g.remote_dma(ap(o), ap(i), T.sem[sem], T.sem["sent"], pid, rid, m)
        cnt["sent"] = cnt.get("sent", 0) + bin(m).count("1")
        return bin(m).count("1")

    def spread(to, i, lands, sem, left="sent"):
        deps("g", [], [i])
        m = topo.mask(core, peer(to[0]))
        for x in to:
            m &= topo.mask(core, peer(x))
        ids = [topo.addr(peer(x), core) for x in to]
        g.remote_dma_fused([RemoteDMATransfer(dst_ids=[DstId(rid=r_, pnc=p_) for r_, p_ in ids], dma_engine_mask=m, remote_sem=T.sem[sem],
                                              srcs=[ap(i)], dsts=[ap(a) for a in lands])], local_sem=T.sem[left])
        cnt[left] = cnt.get(left, 0) + bin(m).count("1")
        arrive(sem, bin(m).count("1") * len(to), lands)

    V = g.vector

    def tc(o, i):
        op("v", [o], [i], lambda: V.tensor_copy(ap(o), ap(i)))

    def tt(o, a, b, f):
        op("v", [o], [a, b], lambda: V.tensor_tensor(ap(o), ap(a), ap(b), f))

    def ts(o, a, s1, f1, s2=None, f2=None):
        if f2 is None:
            op("v", [o], [a, s1], lambda: V.tensor_scalar(ap(o), ap(a), ap(s1), None, f1))
        else:
            op("v", [o], [a, s1, s2], lambda: V.tensor_scalar(ap(o), ap(a), ap(s1), ap(s2), f1, f2))

    def ms(o, v):
        op("v", [o], [], lambda: V.memset(ap(o), v))

    def scan(o, a, b, f1, f2, init=0.0):
        op("v", [o], [a, b, init], lambda: V.tensor_tensor_scan(ap(o), ap(a), ap(b), ap(init), f1, f2))

    def least(o, i):
        op("v", [o], [i], lambda: V.tensor_reduce(ap(o), ap(i), AX.X, O.min))

    def tr(o, i):
        op("v", [o], [i], lambda: V.transpose(ap(o), ap(i)))

    def act(o, i, f=AF.Copy, scale=None, bias=None):
        kw = {}
        if scale is not None:
            kw["scale"] = ap(scale)
        if bias is not None:
            kw["bias"] = ap(bias)
        op("a", [o], [i, scale, bias], lambda: g.scalar.activation(ap(o), ap(i), f, **kw))

    def aff(o, i, scale, bias):
        act(o, i, AF.Identity, scale, bias)

    def fill(n, c0, c1, st, v, p0=0, p1=128):
        aff(A(n, c0, c1, st, p0, p1), A("zz", 0, len(range(c0, c1, st)), 1, p0, p1), 1.0, float(v))

    def quant(q, s, i):
        op("v", [q, s], [i], lambda: V.quantize_mx(ap(q), ap(s), ap(i)))

    def mm(o, l, ls, r, rs):
        op("p", [o], [l, ls, r, rs], lambda: g.tensor.matmul_mx(ap(o), ap(l), ap(ls), ap(r), ap(rs), True, True))

    def iota(o, pat, base, cm, fl=True):
        if fl:
            op("g", [o], [], lambda: g.iota(ap(o), pat, base, cm, allow_small_or_imprecise_dtypes=True))
        else:
            op("g", [o], [], lambda: g.iota(ap(o), pat, base, cm))

    hi = [1 if rank & s else 0 for s in STEP]
    names = ["P", "q", "j32", "e", "g", "i8", "a", "qh", "g1", "q1", "corr", "pw", "fb", "pq", "pe", "q22", "r16", "self", "last"]
    col = {n: A("cc", k) for k, n in enumerate(names)}
    cu = {"unb": A("cu", 0, 22), "m16": A("cu", 22, 44), "F": A("cu", 44, 46), "kg": A("cu", 50, 52), "q": A("cu", 54, 56)}
    sh, an = O.arith_shift_right, O.bitwise_and

    def io(a, b, st=1):
        return A("win", NUM + a, NUM + b, st)

    def own_win(t, c0=0, c1=J, **k):
        return A("win", OWN[t] + c0, OWN[t] + c1, **k)

    def lst(n, at, k):
        return A(n, at + CHUNK[k][0] // 16, at + CHUNK[k][1] // 16)

    def send_x(t):
        n = send(STEP[t], cast(A("lq%d" % t), dt.uint8), cast(A("qx%d" % t), dt.uint8), "ad%d" % t)
        n += send(STEP[t], A("ls%d" % t), A("sx%d" % t), "ad%d" % t)
        arrive("ad%d" % t, n, [A("lq%d" % t), A("ls%d" % t)])

    def unpack(ps, q, s):
        for b in range(4):
            mm(A(ps, 512 * b, 512 * b + C), A("qe", 128 * b, 128 * b + 128), A("se", 128 * b, 128 * b + 128), A(q), A(s))

    def halve(ps, at, b, on="a", c0=0, c1=C):
        o, i = A("fj", J * b + at + c0, J * b + at + c1), A(ps, 512 * b + c0, 512 * b + c1)
        if on == "a":
            act(o, i, scale=0.5)
        else:
            ts(o, i, 0.5, O.mult)

    def run_max(at, src, c0, c1):
        scan(A("sc", at + c0, at + c1), A("ctrl", c0, c1), src, O.add, O.max)

    def listed(dst, at, c0, c1):
        ts(dst, A("sc", at + c0 + 15, at + c1, 16), col["corr"], O.subtract)

    def share():
        dma("s", [(A("dsrc"), own_win(1, ps=16))])
        arrive("af", send(STEP[2], A("dland"), A("dsrc"), "af"), [A("dland")])
        dma("s", [(A("win", NEXT[1], NEXT[1] + J, p0=r, ps=16), A("dland")) for r in range(16)])

    def early_constants(t):
        o, j0 = 152 * t, float(C * hi[t])
        aff(A("rc", o, o + 32), A("cb", 24, 56), 1.0, j0)
        aff(A("rc", o + 96, o + 99), A("cb", 24, 27), 2048.0, 2048.0 * j0 + 255.0 + LEVEL)
        fill("rc", o + 2, o + 24, 3, -1, 96, 128)
        aff(A("rc", o + 100, o + 103), A("cb", 24, 27), -2048.0, -2048.0 * j0)
        aff(A("rc", o + 148, o + 151), A("cb", 24, 27), 1.0, TOP + j0)
        aff(A("rc", o + 48, o + 80), A("rc", o, o + 32), -1.0, col["self"])

    def late_constants(t):
        o, j0 = 152 * t, float(C * hi[t])
        aff(A("rc", o + 104, o + 148, 2), A("cb", 0, 22), 2048.0, 2048 * j0)
        aff(A("rc", o + 105, o + 148, 2), A("cb", 0, 22), 1.0, j0)
        for s, base in enumerate([OWN[t]] + NEXT[t:t + 1]):
            ts(A("dd", 440 * t + 220 * s + 9, 440 * t + 220 * s + 220, 10), A("cb", 0, 22), j0 + base - WINDOW[t][0], O.add)

    def scan_constants(t):
        iota(A("e0", 220 * t, 220 * t + 220), [[0, 220]], 0, 0, False)
        iota(A("dd", 440 * t + 1, 440 * t + 440, 2), [[0, 220]], 0, 0, False)
        for s, base in enumerate([OWN[t]] + NEXT[t:t + 1]):
            iota(A("e0", 220 * t + 110 * s + 2, 220 * t + 110 * s + 110, 5), [[0, 22]], NUM - base, 0, False)

    def table():
        aff(A("tb", 32, 32 + J), io(0, J), 2048.0, 3 * LEVEL)
        fill("tt7", 16, 96 * 23, 96, BIG)

    def by_column():
        tc(A("pl", 0, 24), A("tt", 0, 384, 16))
        dma("s", [(A("pl", 24 * m, 24 * m + 24, p0=p0, p1=p1), A("pl", 0, 24, p0=(p0 + 32 * m) % 128, p1=(p0 + 32 * m) % 128 + p1 - p0))
                  for m in range(1, 4) for p0, p1 in ((0, 128 - 32 * m), (128 - 32 * m, 128))])

    dma("a", [(A("dv0"), ext(T.vg[:]))])
    dma("s", [(A("vgi"), ext(T.vg[:]))])
    dma("s", [(A("xt"), ext(T.x[:]))])
    dma("s", [(A("vb", 0, C, p0=r, ps=16), ext(T.vg[:])) for r in range(16)])
    dma("s", [(A("ut"), ext(T.u[:]))])
    iota(A("pi", 0), [[0, 1]], 0, 1, False)
    iota(io(0, 128), [[1, 128]], 0, 0)
    iota(A("uw", 144, 216), [[16, 8], [0, 9]], 0, 0)
    iota(A("uw", 216, 288), [[16, 8], [16, 9]], 0, 0)
    spread([STEP[0]], A("dv0"), [A("dv")], "av")
    dma("s", [(A("vb", C, J, p0=r, ps=16), A("dv")) for r in range(8)])

    ms(A("zz"), 0.0)
    ms(A("et"), 0.0)
    for k, (s_, m_) in enumerate([(0, 15), (0, 31), (4, 1), (4, 7), (0, 7), (5, 3), (1, 7)]):
        ts(A("pi", k + 1), A("pi", 0), s_, sh, m_, an)
    tc(A("cc", 0, 8), A("pi", 0, 8))
    for n_, c0, c1, v in (("coef", 0, 72, 1), ("rs", 0, 32, 1), ("on", 0, 32, LEVEL), ("zc", 0, 8, 2), ("c32", 0, 8, 4 * 4096), ("c32", 8, 32, 7 * 4096),
                          ("tt", C, 384, -1), ("pl", 96, 104, -K), ("dz", 0, 3, -BIG), ("kr", 120, 128, 96)):
        fill(n_, c0, c1, 1, v)
    for c0, c1, st, v in ((0, 72, 9, 0), (8, 72, 9, 4096), (16, 57, 8, -1)):
        fill("coef", c0, c1, st, v)
    for n_, i_, s_, b_ in (("q22", "q", 22, 0), ("q1", "q", 1, 1), ("fb", "i8", 9, 8), ("pe", "e", -0.5, 1), ("g1", "g", 1, 8192), ("r16", "q", 1, 16),
                           ("self", "q", 1, -16), ("last", "q", -1, 16 - TOP)):
        aff(col[n_], col[i_], float(s_), float(b_))
    fill("coef", 8, 9, 1, -4096)
    aff(A("coef", 1, 72, 9), io(0, 8), 1.0, -7.0)
    for k in range(3):
        aff(A("cb", 24 + k, 56, 3), A("on", 0, len(range(k, 32, 3))), 128.0 * k / LEVEL, col["P"])
    aff(A("dz", 123, 126), A("zz", 0, 3), 1.0, col["last"])
    for e in range(2):
        ts(A("et", 516 * e + 2 + e, 516 * e + 514, 4), io(0, 128), col["P"], O.is_equal)
    tc(A("la", 0, 22), A("vgi"))
    ts(A("c16", 0, 16), io(0, 16), col["q"], O.is_equal, -2.0 ** 20, O.mult)
    ts(A("c16", 16, 32), io(0, 16), col["q1"], O.is_equal, 4096.0, O.mult)
    for b in range(4):
        c = 516 * (b % 2) + 2 - b // 2 * 2
        quant(A("qe", 128 * b, 128 * b + 128), A("se", 128 * b, 128 * b + 128), A("et", c, c + 512))
    ts(cu["m16"], A("zz", 0, 22), col["q"], O.add)
    tt(A("c16", 32, 48), A("c16", 0, 16), A("c16", 16, 32), O.add)
    quant(A("qx0"), A("sx0"), A("xt"))
    send_x(0)
    left_x = cnt["sent"]
    iota(A("kr", 0, 24), [[1, 4], [0, 6]], 4, 0)
    iota(A("kr", 32, 56), [[0, 4], [1, 2], [8, 3]], 0, 0)
    iota(io(128, J), [[1, J - 128]], 128, 0)
    iota(A("yt", 4 * C, 1536), [[0, 128]], 0, 0)
    for k in range(3):
        iota(A("s1", 384 * k + 80, 384 * k + 378, 9), [[0, 34]], 0, 0)
    unpack("psa", "qx0", "sx0")
    act(A("ctrl"), ind(A("c16", 32, 48), cu["m16"]))
    pv = [A("p7", 44 * k + c, 44 * k + c + 22) for k in range(3) for c in (0, 22)]
    ts(pv[0], A("vgi"), 15, an)
    ts(pv[1], A("vgi"), 4, sh)
    ts(pv[2], A("vgi"), float(C), O.is_ge, -374.0 if hi[0] else 330.0, O.mult)
    ts(A("uw", 288, 360), A("uw", 216, 288), 128.0, O.is_ge, 128.0, O.mult)
    ts(cu["unb"], io(0, 22), col["q22"], O.add)
    ts(pv[3], pv[0], 22.0, O.mult, float(C * hi[0]), O.add)
    tt(pv[4], pv[1], pv[2], O.add)
    tt(A("uw", 360, 432), A("uw", 216, 288), A("uw", 288, 360), O.subtract)
    ts(col["corr"], col["q"], 15.0, O.is_lt, 4096.0, O.mult)
    tc(A("vgf"), A("vgi"))
    tt(pv[5], pv[3], pv[4], O.add)
    tt(A("uw", 0, 72), A("uw", 144, 216), A("uw", 360, 432), O.min)
    tt(A("uw", 72, 144), A("uw", 144, 216), A("uw", 360, 432), O.max)
    tc(A("ix", 0, 22), pv[5])
    tc(own_win(0, C * hi[0], C * hi[0] + C), ind(A("vb", 0, C), cu["unb"]))
    run_max(0, A("uw", 0, 144), 0, 144)
    halve("psa", C * hi[0], 0)
    halve("psa", C * hi[0], 1)
    dma("a", [(A("vb", C, J, p0=r, ps=16), A("dv")) for r in range(8, 16)])
    halve("psa", C * hi[0], 2)
    halve("psa", C * hi[0], 3)
    early_constants(0)
    scan(A("zc", 8, 16), A("zc", 0, 8), A("zz", 0, 8), O.mult, O.add, 0.5)
    ts(A("zc", 16, 24), io(0, 8), 256.0, O.mult)
    tr(A("tt", 0, C), own_win(0, C * hi[0], C * hi[0] + C))
    listed(A("upk", 0, 9), 0, 0, 144)
    ts(A("oi", 0, 24), A("kr", 0, 24), col["a"], O.subtract)
    ts(A("kr", 64, 88), A("kr", 32, 56), col["a"], O.add, col["a"], O.add)
    by_column()
    dma("s", [(A("dv1"), A("vgf"))])
    spread([STEP[1], STEP[0] ^ STEP[1]], A("dv1"), [A("dv2"), A("dv3")], "au", "gone")
    quant(A("qu"), A("su"), A("ut"))
    ts(A("p7", 176, 200), A("oi", 0, 24), 3, an)
    tt(A("wt", 8, 16), A("zc", 8, 16), A("zc", 16, 24), O.add)
    ts(A("dz", 27, 123, 3), io(0, 32), col["j32"], O.is_equal, -K, O.mult)
    ts(cu["F"], A("zz", 0, 2), col["fb"], O.add)
    ts(A("kr", 0, 24), A("p7", 176, 200), 24.0, O.mult)
    op("v", [A("qp")], [A("qu"), A("upk")], lambda: V.tensor_copy(T.qp[:, 0:144].bitcast(dt.uint32), T.qu[:, 0:128].bitcast(dt.uint32).indirect(T.upk[:, 0:9])))
    op("a", [A("sp")], [A("su"), A("upk")], lambda: g.scalar.activation(T.sp[:, 0:144], T.su[:, 0:128].indirect(T.upk[:, 0:9]), AF.Copy))
    tt(A("kr", 96, 120), A("kr", 0, 24), A("kr", 64, 88), O.add)
    ts(A("me", 2, 4), io(0, 2), col["e"], O.is_equal, BIG, O.mult)
    ts(A("zo", 0, 4), io(0, 4), col["a"], O.not_equal, BIG, O.mult)
    ts(cu["q"], io(0, 16, 8), col["qh"], O.add, 10.0, O.min)
    run_max(0, A("kr", 96, 128), 0, 32)
    ts(A("me", 0, 2), A("me", 2, 4), -16.0, O.add)
    wait("s", ("sent", left_x, {}))
    dma("s", [(cast(A("qw"), dt.uint8), ext(T.wc[:])), (A("sw"), ext(T.ws[:]))])
    dma("s", [(A("vc", C * k, C * k + C, p0=r, ps=16), A("dv%d" % (k + 2))) for k in (0, 1) for r in range(16)] + [(A("vt"), ext(T.v[:]))])
    listed(cu["kg"], 0, 0, 32)
    for n_, c0, c1, st, v in (("tb", 0, 32, 1, 0), ("r6", 0, 132, 1, 0), ("r6", 0, 132, 6, FAR), ("tt7", 32, 96 * 22, 96, FAR), ("tt7", 64, 96 * 22, 96, FAR),
                              ("tt7", 80, 96 * 22, 96, FAR), ("wout", 0, 72, 1, 0), ("ti", 0, J, 1, 0)):
        iota(A(n_, c0, c1, st), [[0, len(range(c0, c1, st))]], v, 0)
    scan_constants(0)
    for k in range(3):
        aff(A("wt", 32 * k, 32 * k + 8), A("zc", 8, 16), -1.0, 0.0)
    for k in (1, 2):
        act(A("dz", 27 + k, 123, 3), A("dz", 27, 123, 3))
        act(A("wt", 32 * k + 8, 32 * k + 16), A("wt", 8, 16))
    unpack("psb", "lq0", "ls0")

    for t in range(3):
        o, w = 152 * t, 24 * t
        at = C * hi[t]

        def gather(on, out, win, off):
            (act if on == "a" else tc)(out, ind(win, off))

        def swap(k, on="v"):
            gather(on, own_win(t, at + CHUNK[k][0], at + CHUNK[k][1]), A("win", *WINDOW[t - 1]), lst("ix", 0, k))

        def once(k):
            run_max(0, own_win(t, at + CHUNK[k][0], at + CHUNK[k][1]), *CHUNK[k])

        def once_list(k):
            listed(lst("la", 22 * t, k), 0, *CHUNK[k])

        def turn(k):
            tr(A("tt", *CHUNK[k]), own_win(t, at + CHUNK[k][0], at + CHUNK[k][1]))

        def twice(k, on="v"):
            gather(on, A("ppf", *CHUNK[k]), own_win(t) if t else A("vb"), lst("la", 22 * t, k) if t else lst("ix", 0, k))

        def twice_scan(k):
            run_max(C, A("ppf", *CHUNK[k]), *CHUNK[k])

        def twice_list(k):
            listed(lst("lb", 22 * t, k), C, *CHUNK[k])

        def first(k, bs=range(4)):
            for b in bs:
                act(A("ab", C * b + CHUNK[k][0], C * b + CHUNK[k][1]), ind(A("fj", J * b, J * b + J), lst("la", 22 * t, k)))

        def blend(k, bs=range(4)):
            for b in bs:
                tt(A("yt", b + 4 * CHUNK[k][0], 4 * CHUNK[k][1], 4), ind(A("fj", J * b, J * b + J), lst("lb", 22 * t, k)),
                   A("ab", C * b + CHUNK[k][0], C * b + CHUNK[k][1]), O.add)

        def score(k):
            c0, c1 = (0, 128) if k == 0 else (128, C if t else 384)
            quant(A("qy", c0, c1), A("sy", c0, c1), A("yt", 4 * c0, 4 * c1))
            for j in (2, 1) if k else (0,):
                mm(A("psb", 512 * j, 512 * j + 144), A("qy", 128 * j, 128 * j + 128), A("sy", 128 * j, 128 * j + 128), A("qp"), A("sp"))
                act(A("sr", 72 * j, 72 * j + 72), A("psb", 512 * j + 72, 512 * j + 144))

        bank = [3, 2, 1, 0]

        def layer(b):
            mm(A("psb", 512 * bank[b], 512 * bank[b] + C), A("qw", 128 * b, 128 * b + 128), A("sw", 128 * b, 128 * b + 128), A("qy", 0, C), A("sy", 0, C))

        def relu(b):
            act(A("rl", C * b, C * b + C), A("psb", 512 * bank[b], 512 * bank[b] + C), AF.Relu, scale=0.03125)

        done = [0]

        def state(n=C // 4):
            end = min(done[0] + n, 4 * C)
            while done[0] < end:
                b, c0 = divmod(done[0], C)
                c1 = min(C, c0 + end - done[0])
                tt(A("xn", b + 4 * c0, 4 * c1, 4), A("psa", 512 * b + c0, 512 * b + c1), A("rl", C * b + c0, C * b + c1), O.add)
                done[0] += c1 - c0

        pk = ind(A("pl"), cu["kg"])
        z, s1, k32 = (lambda k, a, b: A("z", 42 * k + a, 42 * k + b)), (lambda k, a, b, st=1: A("s1", 384 * k + a, 384 * k + b, st)), (lambda n, k: A(n, 32 * k, 32 * k + 32))

        def words(k):
            aff(k32("rb", k), A("on"), A("m3", 4 + k), A("so", 15 + 32 * k))
            c = 96 * (11 * hi[t] + 4 * k) + 16
            aff(A("tt7", c, c + 289, 96), A("zo"), 1.0, A("so", 31 + 32 * k))

        steps = [
            (lambda k: tt(A("fl", 72 * k, 72 * k + 72), A("psb", 512 * k, 512 * k + 72), A("sr", 72 * k, 72 * k + 72), O.is_ge),),
            (lambda k: scan(s1(k, 0, 72), A("coef"), A("fl", 72 * k, 72 * k + 72), O.mult, O.add),),
            (lambda k: tt(k32("f96", k), ind(s1(k, 0, 72), cu["F"]), A("c32"), O.is_ge),
             lambda k: scan(z(k, 0, 42), A("dz", k, 126, 3), s1(k, 8, 378, 9), O.add, O.max)),
            (lambda k: tt(k32("fw", k), k32("f96", k), k32("wt", k), O.mult), lambda k: tr(k32("t96", k), z(k, 8, 40)),
             lambda k: act(A("m3", 4 + k), z(k, 40, 41), AF.Sign, -1.0, A("rc", o + 148 + k))),
            (lambda k: scan(k32("so", k), A("rs"), k32("fw", k), O.mult, O.add, A("rc", o + 96 + k)), words,
             lambda k: ts(z(k, 8, 40), k32("t96", k), z(k, 40, 41), O.not_equal, BIG, O.mult)),
            (lambda k: least(A("m3", k), z(k, 8, 42)),),
            (lambda k: ts(A("lsc", 2 * k, 2 * k + 2), A("me", 0, 2), A("m3", k), O.min, col["r16"], O.add), lambda k: tr(k32("tbv", k), k32("rb", k))),
            (lambda k: tc(ind(A("tb"), A("lsc", 2 * k, 2 * k + 2)), k32("tbv", k)),),
        ]

        def step(k, n):
            if 0 <= n < len(steps):
                for f in steps[n]:
                    f(k)

        if t:
            swap(0, "a")
            swap(UP)
            act(own_win(t, C - at, J - at), ind(A("win", *WINDOW[t - 1]), A("ix", 22, 44)))
            once(0), once(UP), turn(0), once_list(0), once_list(UP), turn(UP)
            twice(0, "a")
            twice(UP)
            by_column()
            if t == 1:
                share()
            twice_scan(0), twice_scan(UP), twice_list(0), twice_list(UP)
        else:
            twice(0), twice(UP), twice_scan(0), twice_scan(UP), twice_list(0), twice_list(UP)
            halve("psb", C - at, 0)
            halve("psb", C - at, 1, "v")
            halve("psb", C - at, 2)
            halve("psb", C - at, 3, "v")
        first(0, [0]), first(UP), first(0, [1, 2, 3])
        if t == 0:
            table()
        blend(0, [0]), blend(UP), blend(0, [1])
        score(UP)
        tt(A("pw", 0, 32), pk, A("rc", o, o + 32), O.is_equal)
        for k in DOWN:
            aff(A("wt", 32 * k + 24, 32 * k + 32), A("pw", k, 24, 3), BIG, 0.0)
        blend(0, [2])
        tt(A("pw", 32, 64), A("pw", 0, 32), A("rc", o + 48, o + 80), O.mult)
        blend(0, [3])
        tt(A("pw", 64, 96), pk, A("pw", 32, 64), O.add)
        for k in DOWN:
            aff(A("wt", 32 * k + 16, 32 * k + 24), A("pw", 64 + k, 88, 3), 2048.0, A("rc", o + 100 + k))
        score(0)
        layer(0)
        for n in range(len(steps) + 3):
            step(0, n - 3), step(2, n), step(1, n if n < 7 else n - 1 if n == 8 else -1)
            if n == 0:
                tt(A("dz", 3, 27), A("pw", 64, 88), A("pw", 67, 91), O.subtract)
                layer(1), layer(2)
                relu(0)
            if n == 3:
                layer(3)
            if n == 9:
                state()
        for b in range(1, 4):
            relu(b)
        state()
        tr(A("tt7", 0, 3 * J, 3), A("tb", 32, 32 + J))
        state()
        scan(A("ar"), A("r6"), A("tt7", 0, 3 * J, 16), O.add, O.min)
        state()
        tt(A("a1", 0, 22, p1=64), A("ar", 5, 132, 6, p1=64), A("ar", 5, 132, 6, p0=64), O.min)
        state()
        for a in range(2):
            tt(A("wout", w, w + 22, p0=32 * a, p1=32 * a + 32), A("a1", 0, 22, p1=32), A("a1", 0, 22, p0=32, p1=64), O.min)
        W = A("wout", w, w + 22)
        spread([STEP[t]], W, [A("wl", 72 * t, 72 * t + 22)], "aw%d" % t)
        if t < 2:
            spread([STEP[t + 1], STEP[t] ^ STEP[t + 1]], W, [A("wl", 72 * t + 24 * k, 72 * t + 24 * k + 22) for k in (1, 2)], "ax%d" % t)
        state(4 * C)
        qn, sn = "qx%d" % (t + 1), "sx%d" % (t + 1)
        quant(A(qn), A(sn), A("xn"))
        if t == 0:
            for a in range(4):
                fill("cc", names.index("pq"), names.index("pq") + 1, 1, 2 ** (7 - 2 * a), 32 * a, 32 * a + 32)
            aff(A("cb", 0, 22), io(0, C, 16), 1.0, col["q"])
            for j in (8, 24):
                aff(A("ti", j, J, 32), io(0, J, 32), 1.0, col["j32"])
            tt(col["pw"], col["pq"], col["pe"], O.mult)
        late_constants(t)
        if t < 2:
            send_x(t + 1)
            scan_constants(t + 1)
            if t == 0:
                tc(own_win(0, C - at, J - at), ind(A("vb", C, J), cu["unb"]))
                tc(A("win", NEXT[0] + at, NEXT[0] + at + C), ind(A("vc", 0, C), cu["unb"]))
                act(A("win", NEXT[0] + C - at, NEXT[0] + J - at), ind(A("vc", C, J), cu["unb"]))
            unpack("psa", qn, sn)
            table()
            for b in range(4):
                halve("psa", C * hi[t + 1], b)
            early_constants(t + 1)
        else:
            quant(A("qv"), A("sv"), A("vt"))
            mm(A("psa", 0, C), A("qv"), A("sv"), A(qn), A(sn))
            dma("s", [(ext(T.oc[:]), cast(A(qn), dt.uint8))] + [(ext(T.osc[4 * k:4 * k + 4, :]), A(sn, p0=32 * k, p1=32 * k + 4)) for k in range(4)])
            act(A("yo"), A("psa", 0, C))
            dma("a", [(ext(T.y[:]), A("yo"))])
        two = [("wout", w, 72 * t), ("wl", 72 * t + 24, 72 * t + 48) if t < 2 else ("wout", w, 72 * t)]
        for s, (n0, a0, a1) in enumerate(two):
            for n_, c0, c1, st, c, wide in (("vi", 0, 11, 1, 11 * hi[t], 11), ("ti", 0, J, 32, 0, 22), ("ti", 16, J, 32, 0, 22)):
                tt(A(n_, c0, c1, st, 64 * s, 64 * s + 64), A(n0, a0 + c, a0 + c + wide, p1=64), A("wl", a1 + c, a1 + c + wide, p1=64), O.min)
        ts(A("oi"), ind(A("vi", 0, 11), cu["q"]), 11, sh, 1023, an)
        tr(A("wv", 0, C), A("ti", 0, C))
        tc(A("lq"), A("oi", 0, 22))
        tr(A("wv", C, J), A("ti", C, J))
        gather("a", A("gq", 192, C), A("wv"), A("lq", 12, 22))
        gather("v", A("gq", 0, 192), A("wv"), A("lq", 0, 12))
        if t < 2:
            unpack("psb", "lq%d" % (t + 1), "ls%d" % (t + 1))
            for b in range(3):
                halve("psb", C - C * hi[t + 1], b)

        def piece(h):
            if t < 2:
                halve("psb", C - C * hi[t + 1], 3, "v", C // 2 * h, C // 2 * h + C // 2)

        tr(A("tg"), A("gq"))
        d, e = 440 * t, 220 * t
        n = 44 if t < 2 else 22
        cn = [o + 104, o + 148, 1]
        if t < 2:
            for s in range(2):
                for h in range(2):
                    tt(A("dd", d + 220 * s, d + 220 * s + 220, 5, 64 * h, 64 * h + 64), A("tg", 0, C, 8, 64 * s, 64 * s + 64), A("rc", *cn, 64 * s, 64 * s + 64), O.subtract)
        else:
            tt(A("dd", d, d + 220, 5), A("tg", 0, C, 8), A("rc", *cn), O.subtract)
        D = A("dd", d, d + 10 * n, 10)
        p = [A("p7", 44 * k, 44 * k + n) for k in range(3)]
        ts(p[0], D, col["pw"], O.mult)
        ts(p[1], D, 11, sh, 1023, an)
        ts(p[2], D, 8, sh, 16383, an)
        ts(A("e0", e + 3, e + 5 * n, 5), p[0], 7, sh, 1, an)
        ts(A("e0", e + 4, e + 5 * n, 5), p[1], 0.0, O.is_equal)
        ts(A("dd", d + 3, d + 10 * n, 10), p[2], col["g1"], O.is_equal)
        scan(A("so2", 0, 5 * n), A("e0", e, e + 5 * n), A("dd", d + 1, d + 10 * n, 2), O.mult, O.add)
        piece(0)
        tc(A("ix", 0, n), A("so2", 4, 5 * n, 5))
        piece(1)
    act(A("wov", 192, C), ind(A("win", *WINDOW[2]), A("ix", 12, 22)))
    tc(A("wov", 0, 192), ind(A("win", *WINDOW[2]), A("ix", 0, 12)))
    dma("s", [(ext(T.ov[:]), A("wov", ps=16))])
    for s, n in cnt.items():
        g.wait_ge(T.sem[s], n)
